import numpy as np
import ml_dtypes


def mxq(x, axis, fmt="e4m3"):
    dtype, down = {"e4m3": (ml_dtypes.float8_e4m3fn, 7), "e5m2": (ml_dtypes.float8_e5m2, 14)}[fmt]
    v = np.moveaxis(np.asarray(x, np.float32).astype(ml_dtypes.bfloat16).astype(np.float64), axis, -1)
    blocks = v.reshape(v.shape[:-1] + (-1, 32))
    amax = np.abs(blocks).max(-1, keepdims=True)
    byte = np.maximum(np.where(amax > 0, np.frexp(amax)[1] - 1 + 127, 0) - down, 1)
    scale = np.exp2(byte - 127.0)
    codes = (blocks / scale).astype(np.float32).astype(dtype).astype(np.float64)
    return np.moveaxis((codes * scale).reshape(v.shape), -1, axis)


WIDE = False


def mx_kscale(k):
    if not WIDE:
        return np.ones(k)
    levels = np.array([10, -10, 5, -5, 0])
    if k % 512:
        return np.exp2(np.random.permutation(np.resize(levels, k // 32))).repeat(32)
    a = np.empty((k // 512, 16))
    for p in range(k // 512):
        a[p, :8] = np.random.permutation(np.resize(levels, 8))
        for g in range(8):
            far = levels[np.abs(levels - a[p, g]) >= 10]
            a[p, g + 8] = far[np.random.randint(len(far))]
    return np.exp2(a.ravel()).repeat(32)


def f64(x):
    return np.asarray(x).astype(np.float64)


def striped(idx):
    return np.tile(idx.reshape(-1, 16).T, (8, 1)).astype(np.uint16)


def unstriped(offs):
    return offs[:16].T.reshape(-1).astype(np.int64)


E2M1 = np.array([0.0, 0.5, 1.0, 1.5, 2.0, 3.0, 4.0, 6.0, -0.0, -0.5, -1.0, -1.5, -2.0, -3.0, -4.0, -6.0])


def pack_weight(w, fmt):
    k, n = w.shape
    w = f64(np.asarray(w, np.float32).astype(ml_dtypes.bfloat16)).reshape(k // 32, 32, n)
    amax = np.abs(w).max(1)
    if fmt == "e4m3":
        byte = np.frexp(amax)[1] - 1 + 127 - 7
    else:
        mant, ex = np.frexp(amax / 6.0)
        byte = np.where(mant > 0.5, ex, ex - 1) + 127
    byte = np.clip(np.where(amax > 0, byte, 1), 1, 254)
    scaled = (w * np.exp2(127.0 - byte)[:, None, :]).reshape(k, n).astype(np.float32)
    by_word = np.ascontiguousarray(scaled.reshape(k // 512, 128, 4, n).transpose(0, 1, 3, 2))
    if fmt == "e4m3":
        words = by_word.astype(ml_dtypes.float8_e4m3fn).view(np.uint8)
    else:
        c = by_word.astype(ml_dtypes.float4_e2m1fn).view(np.uint8) & 0xF
        words = (c[..., 0::2] | (c[..., 1::2] << 4)).reshape(k // 512, 128, 2 * n)
    return np.ascontiguousarray(words), np.ascontiguousarray(byte.astype(np.uint8).reshape(k // 512, 16, n))


def unpack_weight(words, scales, fmt):
    g, _, n = scales.shape
    words = np.ascontiguousarray(words).reshape(g, 128, n, -1)
    if fmt == "e4m3":
        vals = words.view(ml_dtypes.float8_e4m3fn).astype(np.float64)
    else:
        nib = np.empty((g, 128, n, 4), np.uint8)
        nib[..., 0::2] = words & 0xF
        nib[..., 1::2] = words >> 4
        vals = E2M1[nib]
    vals = vals * np.repeat(np.exp2(scales.astype(np.float64) - 127.0), 8, axis=1)[..., None]
    return vals.transpose(0, 1, 3, 2).reshape(g * 512, n)


def gelu(v):
    return 0.5 * v * (1.0 + np.tanh(np.sqrt(2.0 / np.pi) * (v + 0.044715 * v**3)))


T, S, P, K, H, N = 4096, 1024, 512, 1536, 1024, 256

def setup_inputs():
    n = np.random.standard_normal
    s = mx_kscale(K)[:, None]
    u = mx_kscale(H)[:, None]
    tab_words, tab_scales = pack_weight(n((K, T)) * s, "e4m3")
    w1_words, w1_scales = pack_weight(n((K, H)) / np.sqrt(K) / s, "e2m1")
    return {
        "tab_words": tab_words, "tab_scales": tab_scales,
        "offs": striped(np.random.permutation(T)[:S]),
        "w1_words": w1_words, "w1_scales": w1_scales,
        "pos1": striped(np.random.permutation(S)[:P]),
        "pos2": striped(np.random.permutation(S)[:P]),
        "gain": (2.0 * np.exp(0.3 * n(H)) * u[:, 0]).astype(np.float32),
        "w2": (n((H, N)) / np.sqrt(H) / u).astype(np.float32),
        "b2": (0.3 * n(N)).astype(np.float32),
    }

def reference(tab_words, tab_scales, offs, w1_words, w1_scales, pos1, pos2, gain, w2, b2):
    v = unpack_weight(tab_words, tab_scales, "e4m3")[:, unstriped(offs)]
    w1 = unpack_weight(w1_words, w1_scales, "e2m1")
    h = np.tanh(w1.T @ v)
    a = h[:, unstriped(pos1)]
    b = h[:, unstriped(pos2)]
    z = f64(gain)[:, None] * (a * b)
    y = mxq(f64(w2), 0, "e4m3").T @ mxq(z, 0, "e4m3")
    return y + f64(b2)[:, None]

@@ -1,0 +1,262 @@
+from contextlib import ExitStack
+
+import concourse.mybir as mybir
+from concourse.masks import make_identity
+
+T, S, PAIRS, K, H, N = 4096, 1024, 512, 1536, 1024, 256
+FLOPS = 2 * K * H * S + 2 * H * N * PAIRS
+
+F32 = mybir.dt.float32
+BF16 = mybir.dt.bfloat16
+I32 = mybir.dt.int32
+U32 = mybir.dt.uint32
+U16 = mybir.dt.uint16
+U8 = mybir.dt.uint8
+FP8X4 = mybir.dt.float8_e4m3fn_x4
+FP4X4 = mybir.dt.float4_e2m1fn_x4
+ACT = mybir.ActivationFunctionType
+ALU = mybir.AluOpType
+
+P = 128
+BANK = 512
+K_PASSES = K // 512
+R_PASSES = H // 512
+PIECES = ((0, 256), (256, 256))
+
+
+def tile_list_pair_bond_logits_kernel(
+    tc, tab_words, tab_scales, offs, w1_words, w1_scales, pos1, pos2, gain, w2, b2, out
+):
+    nc = tc.nc
+    with ExitStack() as ctx:
+        held = ctx.enter_context(tc.tile_pool(name="held", bufs=1))
+        turn = ctx.enter_context(tc.tile_pool(name="turn", bufs=1))
+        psum = ctx.enter_context(tc.psum_pool(name="psum", bufs=8))
+
+        def bank(name):
+            return psum.tile([P, BANK], F32, name=name, tag="bank")
+
+        offs_t = held.tile([P, S // 16], U16, name="offs_t")
+        pos1_t = held.tile([P, PAIRS // 16], U16, name="pos1_t")
+        pos2_t = held.tile([P, PAIRS // 16], U16, name="pos2_t")
+        tab_w = [turn.tile([P, T], I32, name=f"tab_w{a}", offset=(a % 2) * 4 * T) for a in range(K_PASSES)]
+        tab_s = held.tile([P, T], U8, name="tab_s", align_bytes=64)
+        picked_s = held.tile([P, S], U8, name="picked_s", align_bytes=64)
+        w1_raw = [
+            held.tile([P, K_PASSES * 1024], U8, name="w1_raw0", align_bytes=64),
+            turn.tile([P, K_PASSES * 1024], U8, name="w1_raw1", offset=4 * T),
+        ]
+        w1s_raw = held.tile([P, H], U8, name="w1s_raw", align_bytes=64)
+        staged = held.tile([P, S + H], U8, name="staged", align_bytes=64)
+        w1_w = [held.tile([P, K_PASSES * 1024], U8, name=f"w1_w{b}", align_bytes=64) for b in range(R_PASSES)]
+        v_w = [held.tile([P, S], I32, name=f"v_w{a}", align_bytes=64) for a in range(K_PASSES)]
+        planes = held.tile([P, K_PASSES, S + H], U8, name="planes", align_bytes=64)
+        gain_rows = held.tile([R_PASSES, 512], F32, name="gain_rows")
+        gain_perm = held.tile([P, 512], F32, name="gain_perm")
+        gain_cols = held.tile([P, 4, 4], F32, name="gain_cols")
+        ident = held.tile([P, P], F32, name="ident")
+        ones = held.tile([P, PAIRS], F32, name="ones")
+        warm = held.tile([P, 1], F32, name="warm")
+        w2_raw = turn.tile([P, R_PASSES, 4, N], F32, name="w2_raw", offset=6 * T)
+        w2_bf = held.tile([P, R_PASSES, N, 4], BF16, name="w2_bf", align_bytes=64)
+        w2_w = held.tile([P, R_PASSES * N], U32, name="w2_w", align_bytes=64)
+        w2_s = held.tile([P, R_PASSES * N], U8, name="w2_s", align_bytes=64)
+
+        nc.gpsimd.dma_start(out=gain_rows[:], in_=gain.rearrange("(b c) -> b c", b=R_PASSES))
+        nc.vector.memset(gain_perm[:], 0.0)
+        nc.gpsimd.dma_start(out=gain_perm[2:4, 0:P], in_=b2.rearrange("(c p) -> c p", p=P))
+        make_identity(nc, ident[:])
+        nc.vector.memset(tab_s[32:64, :].bitcast(I32), 0)
+        nc.vector.memset(tab_s[96:128, :].bitcast(I32), 0)
+        nc.vector.memset(ones[:], 1.0)
+        nc.vector.memset(planes[:].rearrange("p a c -> p (a c)").bitcast(I32), 0)
+        nc.scalar.activation(out=warm[:], in_=ones[:, 0:1], func=ACT.Tanh)
+
+        w1_src = w1_words.bitcast(I32).rearrange("a p (b c) -> b p a c", b=R_PASSES)
+
+        def load_w1(b):
+            nc.sync.dma_start(
+                out=w1_raw[b][:].bitcast(I32).rearrange("p (a c) -> p a c", a=K_PASSES), in_=w1_src[b]
+            )
+
+        def load_scale_rows(dst, src):
+            rows = src.bitcast(I32).rearrange("a q c -> (a q) c")
+            nc.sync.dma_start(out=dst[0:32, :].bitcast(I32), in_=rows[0:32])
+            nc.sync.dma_start(out=dst[64:96, :].bitcast(I32), in_=rows[16:48])
+
+        def load_table(a):
+            nc.sync.dma_start(out=tab_w[a][:], in_=tab_words[a].rearrange("p t i -> p (t i)").bitcast(I32))
+
+        nc.sync.dma_start(offs_t[:], offs)
+        load_scale_rows(tab_s, tab_scales)
+        load_scale_rows(w1s_raw, w1_scales)
+        nc.sync.dma_start(pos1_t[:], pos1)
+        nc.sync.dma_start(pos2_t[:], pos2)
+        load_table(0)
+        load_w1(0)
+        load_table(1)
+
+        for lo in (0, 64):
+            nc.vector.tensor_copy(
+                out=staged[lo : lo + 32, S:].bitcast(I32).rearrange("p (b t m) -> p b t m", b=R_PASSES, t=4),
+                in_=w1s_raw[lo : lo + 32, :].bitcast(I32).rearrange("p (b m t) -> p b t m", b=R_PASSES, t=4),
+            )
+        nc.vector.tensor_copy(out=picked_s[:], in_=tab_s[:].indirect(offs_t[:]))
+        nc.vector.tensor_copy(out=staged[:, 0:S].bitcast(I32), in_=picked_s[:].bitcast(I32))
+        for a, base in enumerate((0, 16, 80)):
+            for r in range(4):
+                nc.scalar.dma_start(
+                    out=planes[r:P:32, a, :].bitcast(I32), in_=staged[base + r : base + 16 : 4, :].bitcast(I32)
+                )
+
+        nc.vector.tensor_copy(
+            out=gain_perm[0:R_PASSES, :].rearrange("b (t m e) -> b t m e", t=4, e=4),
+            in_=gain_rows[:].rearrange("b (m t e) -> b t m e", t=4, e=4),
+        )
+        gain_ps = bank("gain_ps")
+        for t in range(4):
+            nc.tensor.transpose(gain_ps[:, t * P : (t + 1) * P], gain_perm[:, t * P : (t + 1) * P], ident[:])
+        nc.vector.tensor_copy(out=gain_cols[:], in_=gain_ps[:].rearrange("p (t c) -> p t c", t=4)[:, :, 0:4])
+
+        def order_w1_words(b):
+            for a in range(K_PASSES):
+                cols = slice(a * 1024, (a + 1) * 1024)
+                nc.vector.tensor_copy(
+                    out=w1_w[b][:, cols].bitcast(I32).rearrange("p (t m w) -> p t m w", t=4, w=2),
+                    in_=w1_raw[b][:, cols].bitcast(I32).rearrange("p (m t w) -> p t m w", t=4, w=2),
+                )
+
+        def gather_words(a, lo, n):
+            nc.vector.tensor_copy(
+                out=v_w[a][:, lo : lo + n].bitcast(U32),
+                in_=tab_w[a][:].bitcast(U32).indirect(offs_t[:, lo // 16 : (lo + n) // 16]),
+            )
+
+        gather_words(0, 0, S)
+        load_table(2)
+        order_w1_words(0)
+        gain_wide = []
+        for s in range(8):
+            b, t = divmod(s, 4)
+            g = held.tile([P, PAIRS], F32, name=f"gain_wide{s}")
+            nc.vector.tensor_scalar(g[:], ones[:], gain_cols[:, t, b : b + 1], None, ALU.mult)
+            gain_wide.append(g)
+        gather_words(1, 0, S)
+        load_w1(1)
+        w2_src = w2.rearrange("(b m t e) n -> e b m t n", b=R_PASSES, t=4, e=4)
+        for b in range(R_PASSES):
+            for e in range(4):
+                nc.sync.dma_start(out=w2_raw[e:P:4, b, :, :], in_=w2_src[e, b])
+        gather_words(2, 0, BANK)
+        gather_words(2, BANK, BANK)
+        order_w1_words(1)
+
+        h = [held.tile([P, S], F32, name=f"h{s}") for s in range(8)]
+        acc = {}
+
+        def h_pass(s, half, a):
+            b, t = divmod(s, 4)
+            if a == 0:
+                acc[s, half] = bank(f"acc{s}_{half}")
+            cols = slice(half * BANK, (half + 1) * BANK)
+            nc.tensor.matmul_mx(
+                out=acc[s, half][:],
+                lhsT=w1_w[b][:, a * 1024 + t * 256 : a * 1024 + (t + 1) * 256].bitcast(FP4X4),
+                lhsT_scale=planes[:, a, S + s * P : S + (s + 1) * P],
+                rhs=v_w[a][:, cols].bitcast(FP8X4),
+                rhs_scale=planes[:, a, cols],
+                start=(a == 0),
+                stop=(a == K_PASSES - 1),
+            )
+
+        def h_tanh(s, half):
+            nc.scalar.activation(out=h[s][:, half * BANK : (half + 1) * BANK], in_=acc[s, half][:], func=ACT.Tanh)
+
+        for a in range(K_PASSES - 1):
+            for s in range(4):
+                for half in range(2):
+                    h_pass(s, half, a)
+        for s, half in ((0, 0), (1, 0), (0, 1), (1, 1), (2, 0), (2, 1), (3, 0), (3, 1)):
+            h_pass(s, half, K_PASSES - 1)
+            h_tanh(s, half)
+
+        def h_whole(s):
+            for half in range(2):
+                for a in range(K_PASSES):
+                    h_pass(s, half, a)
+                h_tanh(s, half)
+
+        def interleave_w2(b):
+            nc.scalar.activation(out=w2_bf[:, b], in_=w2_raw[:, b].rearrange("p t n -> p n t"), func=ACT.Copy)
+
+        first = [held.tile([P, PAIRS], F32, name=f"first{s}") for s in range(8)]
+        z0 = held.tile([P, 4, PAIRS], F32, name="z0")
+        z1 = [held.tile([P, 4, n], F32, name=f"z1_{lo}") for lo, n in PIECES]
+        z0_bf = held.tile([P, PAIRS, 4], BF16, name="z0_bf", align_bytes=64)
+        z1_bf = [held.tile([P, n, 4], BF16, name=f"z1_bf{lo}", align_bytes=64) for lo, n in PIECES]
+        z0_w = held.tile([P, PAIRS], U32, name="z0_w", align_bytes=64)
+        z0_s = held.tile([P, PAIRS], U8, name="z0_s", align_bytes=64)
+        z1_w = [held.tile([P, n], U32, name=f"z1_w{lo}", align_bytes=64) for lo, n in PIECES]
+        z1_s = [held.tile([P, n], U8, name=f"z1_s{lo}", align_bytes=64) for lo, n in PIECES]
+
+        def gather_first(s):
+            nc.vector.tensor_tensor(first[s][:], h[s][:].indirect(pos1_t[:]), gain_wide[s][:], ALU.mult)
+
+        def gather_second(s, dst, lo, n):
+            nc.vector.tensor_tensor(
+                dst, h[s][:].indirect(pos2_t[:, lo // 16 : (lo + n) // 16]), first[s][:, lo : lo + n], ALU.mult
+            )
+
+        def quantize(codes, scales, src):
+            nc.vector.quantize_mx(out=codes[:].bitcast(FP8X4), scales=scales[:], in_=src)
+
+        def logits(i, evac_engines):
+            lo, n = PIECES[i]
+            for c in range(N // P):
+                o = bank(f"o{i}_{c}")
+                operands = ((z0_w[:, lo : lo + n], z0_s[:, lo : lo + n]), (z1_w[i][:], z1_s[i][:]))
+                for b, (zw, zs) in enumerate(operands):
+                    cols = slice(b * N + c * P, b * N + (c + 1) * P)
+                    nc.tensor.matmul_mx(
+                        out=o[:, 0:n],
+                        lhsT=w2_w[:, cols].bitcast(FP8X4),
+                        lhsT_scale=w2_s[:, cols],
+                        rhs=zw.bitcast(FP8X4),
+                        rhs_scale=zs,
+                        start=(b == 0),
+                        stop=(b == R_PASSES - 1),
+                    )
+                res = held.tile([P, n], F32, name=f"res{i}_{c}")
+                if evac_engines[c] == "scalar":
+                    nc.scalar.activation(out=res[:], in_=o[:, 0:n], func=ACT.Identity, bias=gain_cols[:, 0, 2 + c : 3 + c])
+                else:
+                    nc.vector.tensor_scalar(res[:], o[:, 0:n], gain_cols[:, 0, 2 + c : 3 + c], None, ALU.add)
+                nc.sync.dma_start(out=out[c * P : (c + 1) * P, lo : lo + n], in_=res[:])
+
+        lo_a, n_a = PIECES[0]
+        lo_b, n_b = PIECES[1]
+        gather_first(0)
+        for s in range(1, 8):
+            if s >= 4:
+                h_whole(s)
+            if s in (5, 6):
+                interleave_w2(s - 5)
+            gather_first(s)
+            if s - 1 < 4:
+                gather_second(s - 1, z0[:, s - 1, :], 0, PAIRS)
+            else:
+                gather_second(s - 1, z1[0][:, s - 5, :], lo_a, n_a)
+        nc.scalar.activation(out=z0_bf[:], in_=z0[:].rearrange("p t j -> p j t"), func=ACT.Copy)
+        quantize(w2_w, w2_s, w2_bf[:].rearrange("p b n t -> p (b n t)"))
+        gather_second(7, z1[0][:, 3, :], lo_a, n_a)
+        nc.scalar.activation(out=z1_bf[0][:], in_=z1[0][:].rearrange("p t j -> p j t"), func=ACT.Copy)
+        gather_second(4, z1[1][:, 0, :], lo_b, n_b)
+        gather_second(5, z1[1][:, 1, :], lo_b, n_b)
+        quantize(z0_w, z0_s, z0_bf[:].rearrange("p j t -> p (j t)"))
+        gather_second(6, z1[1][:, 2, :], lo_b, n_b)
+        gather_second(7, z1[1][:, 3, :], lo_b, n_b)
+        quantize(z1_w[0], z1_s[0], z1_bf[0][:].rearrange("p j t -> p (j t)"))
+        nc.vector.tensor_copy(out=z1_bf[1][:], in_=z1[1][:].rearrange("p t j -> p j t"))
+        logits(0, ("scalar", "scalar"))
+        quantize(z1_w[1], z1_s[1], z1_bf[1][:].rearrange("p j t -> p (j t)"))
+        logits(1, ("scalar", "vector"))

@@ -21,7 +21,7 @@ P = 128
 BANK = 512
 K_PASSES = K // 512
 R_PASSES = H // 512
-PIECES = ((0, 256), (256, 256))
+PIECES = ((0, 256), (256, 128), (384, 128))
 
 
 def tile_list_pair_bond_logits_kernel(
@@ -39,13 +39,10 @@ def tile_list_pair_bond_logits_kernel(
         offs_t = held.tile([P, S // 16], U16, name="offs_t")
         pos1_t = held.tile([P, PAIRS // 16], U16, name="pos1_t")
         pos2_t = held.tile([P, PAIRS // 16], U16, name="pos2_t")
-        tab_w = [turn.tile([P, T], I32, name=f"tab_w{a}", offset=(a % 2) * 4 * T) for a in range(K_PASSES)]
+        tab_w = [held.tile([P, T], I32, name=f"tab_w{a}", align_bytes=64) for a in range(K_PASSES)]
         tab_s = held.tile([P, T], U8, name="tab_s", align_bytes=64)
         picked_s = held.tile([P, S], U8, name="picked_s", align_bytes=64)
-        w1_raw = [
-            held.tile([P, K_PASSES * 1024], U8, name="w1_raw0", align_bytes=64),
-            turn.tile([P, K_PASSES * 1024], U8, name="w1_raw1", offset=4 * T),
-        ]
+        w1_raw = [held.tile([P, K_PASSES * 1024], U8, name=f"w1_raw{b}", align_bytes=64) for b in range(R_PASSES)]
         w1s_raw = held.tile([P, H], U8, name="w1s_raw", align_bytes=64)
         staged = held.tile([P, S + H], U8, name="staged", align_bytes=64)
         w1_w = [held.tile([P, K_PASSES * 1024], U8, name=f"w1_w{b}", align_bytes=64) for b in range(R_PASSES)]
@@ -55,27 +52,25 @@ def tile_list_pair_bond_logits_kernel(
         gain_perm = held.tile([P, 512], F32, name="gain_perm")
         gain_cols = held.tile([P, 4, 4], F32, name="gain_cols")
         ident = held.tile([P, P], F32, name="ident")
-        ones = held.tile([P, PAIRS], F32, name="ones")
         warm = held.tile([P, 1], F32, name="warm")
-        w2_raw = turn.tile([P, R_PASSES, 4, N], F32, name="w2_raw", offset=6 * T)
-        w2_bf = held.tile([P, R_PASSES, N, 4], BF16, name="w2_bf", align_bytes=64)
+        w2_raw = held.tile([P, R_PASSES, 4, N], F32, name="w2_raw")
+        w2_bf = turn.tile([P, R_PASSES, N, 4], BF16, name="w2_bf", offset=2 * 4 * PAIRS, align_bytes=64)
         w2_w = held.tile([P, R_PASSES * N], U32, name="w2_w", align_bytes=64)
         w2_s = held.tile([P, R_PASSES * N], U8, name="w2_s", align_bytes=64)
 
-        nc.gpsimd.dma_start(out=gain_rows[:], in_=gain.rearrange("(b c) -> b c", b=R_PASSES))
-        nc.vector.memset(gain_perm[:], 0.0)
-        nc.gpsimd.dma_start(out=gain_perm[2:4, 0:P], in_=b2.rearrange("(c p) -> c p", p=P))
+        for a in range(K_PASSES):
+            nc.gpsimd.dma_start(out=tab_w[a][:], in_=tab_words[a].rearrange("p t i -> p (t i)").bitcast(I32))
         make_identity(nc, ident[:])
         nc.vector.memset(tab_s[32:64, :].bitcast(I32), 0)
         nc.vector.memset(tab_s[96:128, :].bitcast(I32), 0)
-        nc.vector.memset(ones[:], 1.0)
+        nc.vector.memset(gain_perm[:], 0.0)
         nc.vector.memset(planes[:].rearrange("p a c -> p (a c)").bitcast(I32), 0)
-        nc.scalar.activation(out=warm[:], in_=ones[:, 0:1], func=ACT.Tanh)
+        nc.scalar.activation(out=warm[:], in_=gain_perm[:, 511:512], func=ACT.Tanh)
 
         w1_src = w1_words.bitcast(I32).rearrange("a p (b c) -> b p a c", b=R_PASSES)
 
-        def load_w1(b):
-            nc.sync.dma_start(
+        def load_w1(b, queue):
+            queue.dma_start(
                 out=w1_raw[b][:].bitcast(I32).rearrange("p (a c) -> p a c", a=K_PASSES), in_=w1_src[b]
             )
 
@@ -84,39 +79,41 @@ def tile_list_pair_bond_logits_kernel(
             nc.sync.dma_start(out=dst[0:32, :].bitcast(I32), in_=rows[0:32])
             nc.sync.dma_start(out=dst[64:96, :].bitcast(I32), in_=rows[16:48])
 
-        def load_table(a):
-            nc.sync.dma_start(out=tab_w[a][:], in_=tab_words[a].rearrange("p t i -> p (t i)").bitcast(I32))
-
         nc.sync.dma_start(offs_t[:], offs)
         load_scale_rows(tab_s, tab_scales)
         load_scale_rows(w1s_raw, w1_scales)
+        load_w1(0, nc.sync)
+        nc.sync.dma_start(out=gain_rows[:], in_=gain.rearrange("(b c) -> b c", b=R_PASSES))
+        nc.sync.dma_start(out=gain_perm[2:4, 0:P], in_=b2.rearrange("(c p) -> c p", p=P))
         nc.sync.dma_start(pos1_t[:], pos1)
         nc.sync.dma_start(pos2_t[:], pos2)
-        load_table(0)
-        load_w1(0)
-        load_table(1)
+        load_w1(1, nc.gpsimd)
+        w2_src = w2.rearrange("(b m t e) n -> e b m t n", b=R_PASSES, t=4, e=4)
+        for b in range(R_PASSES):
+            for e in range(4):
+                nc.gpsimd.dma_start(out=w2_raw[e:P:4, b, :, :], in_=w2_src[e, b])
 
-        for lo in (0, 64):
+        for lo, hi in ((0, 32), (64, 96)):
             nc.vector.tensor_copy(
-                out=staged[lo : lo + 32, S:].bitcast(I32).rearrange("p (b t m) -> p b t m", b=R_PASSES, t=4),
-                in_=w1s_raw[lo : lo + 32, :].bitcast(I32).rearrange("p (b m t) -> p b t m", b=R_PASSES, t=4),
+                out=staged[lo:hi, S:].bitcast(I32).rearrange("p (b t m) -> p b t m", b=R_PASSES, t=4),
+                in_=w1s_raw[lo:hi, :].bitcast(I32).rearrange("p (b m t) -> p b t m", b=R_PASSES, t=4),
             )
         nc.vector.tensor_copy(out=picked_s[:], in_=tab_s[:].indirect(offs_t[:]))
         nc.vector.tensor_copy(out=staged[:, 0:S].bitcast(I32), in_=picked_s[:].bitcast(I32))
         for a, base in enumerate((0, 16, 80)):
             for r in range(4):
-                nc.scalar.dma_start(
+                nc.sync.dma_start(
                     out=planes[r:P:32, a, :].bitcast(I32), in_=staged[base + r : base + 16 : 4, :].bitcast(I32)
                 )
 
-        nc.vector.tensor_copy(
+        nc.scalar.copy(
             out=gain_perm[0:R_PASSES, :].rearrange("b (t m e) -> b t m e", t=4, e=4),
             in_=gain_rows[:].rearrange("b (m t e) -> b t m e", t=4, e=4),
         )
         gain_ps = bank("gain_ps")
         for t in range(4):
             nc.tensor.transpose(gain_ps[:, t * P : (t + 1) * P], gain_perm[:, t * P : (t + 1) * P], ident[:])
-        nc.vector.tensor_copy(out=gain_cols[:], in_=gain_ps[:].rearrange("p (t c) -> p t c", t=4)[:, :, 0:4])
+        nc.scalar.copy(out=gain_cols[:], in_=gain_ps[:].rearrange("p (t c) -> p t c", t=4)[:, :, 0:4])
 
         def order_w1_words(b):
             for a in range(K_PASSES):
@@ -133,20 +130,14 @@ def tile_list_pair_bond_logits_kernel(
             )
 
         gather_words(0, 0, S)
-        load_table(2)
         order_w1_words(0)
         gain_wide = []
         for s in range(8):
             b, t = divmod(s, 4)
-            g = held.tile([P, PAIRS], F32, name=f"gain_wide{s}")
-            nc.vector.tensor_scalar(g[:], ones[:], gain_cols[:, t, b : b + 1], None, ALU.mult)
+            g = turn.tile([P, PAIRS], F32, name=f"gain_wide{s}", offset=s * 4 * PAIRS)
+            nc.scalar.activation(out=g[:], in_=gain_cols[:, t, b : b + 1].to_broadcast([P, PAIRS]), func=ACT.Copy)
             gain_wide.append(g)
         gather_words(1, 0, S)
-        load_w1(1)
-        w2_src = w2.rearrange("(b m t e) n -> e b m t n", b=R_PASSES, t=4, e=4)
-        for b in range(R_PASSES):
-            for e in range(4):
-                nc.sync.dma_start(out=w2_raw[e:P:4, b, :, :], in_=w2_src[e, b])
         gather_words(2, 0, BANK)
         gather_words(2, BANK, BANK)
         order_w1_words(1)
@@ -210,31 +201,47 @@ def tile_list_pair_bond_logits_kernel(
         def quantize(codes, scales, src):
             nc.vector.quantize_mx(out=codes[:].bitcast(FP8X4), scales=scales[:], in_=src)
 
+        logit_banks = {}
+
+        def logit_pass(i, c, b):
+            lo, n = PIECES[i]
+            if b == 0:
+                logit_banks[i, c] = bank(f"o{i}_{c}")
+            zw, zs = (z0_w[:, lo : lo + n], z0_s[:, lo : lo + n]) if b == 0 else (z1_w[i][:], z1_s[i][:])
+            cols = slice(b * N + c * P, b * N + (c + 1) * P)
+            nc.tensor.matmul_mx(
+                out=logit_banks[i, c][:, 0:n],
+                lhsT=w2_w[:, cols].bitcast(FP8X4),
+                lhsT_scale=w2_s[:, cols],
+                rhs=zw.bitcast(FP8X4),
+                rhs_scale=zs,
+                start=(b == 0),
+                stop=(b == R_PASSES - 1),
+            )
+
         def logits(i, evac_engines):
             lo, n = PIECES[i]
             for c in range(N // P):
-                o = bank(f"o{i}_{c}")
-                operands = ((z0_w[:, lo : lo + n], z0_s[:, lo : lo + n]), (z1_w[i][:], z1_s[i][:]))
-                for b, (zw, zs) in enumerate(operands):
-                    cols = slice(b * N + c * P, b * N + (c + 1) * P)
-                    nc.tensor.matmul_mx(
-                        out=o[:, 0:n],
-                        lhsT=w2_w[:, cols].bitcast(FP8X4),
-                        lhsT_scale=w2_s[:, cols],
-                        rhs=zw.bitcast(FP8X4),
-                        rhs_scale=zs,
-                        start=(b == 0),
-                        stop=(b == R_PASSES - 1),
-                    )
+                logit_pass(i, c, 1)
+                o = logit_banks[i, c]
+                bias = gain_cols[:, 0, 2 + c : 3 + c]
                 res = held.tile([P, n], F32, name=f"res{i}_{c}")
                 if evac_engines[c] == "scalar":
-                    nc.scalar.activation(out=res[:], in_=o[:, 0:n], func=ACT.Identity, bias=gain_cols[:, 0, 2 + c : 3 + c])
+                    nc.scalar.activation(out=res[:], in_=o[:, 0:n], func=ACT.Identity, bias=bias)
                 else:
-                    nc.vector.tensor_scalar(res[:], o[:, 0:n], gain_cols[:, 0, 2 + c : 3 + c], None, ALU.add)
+                    nc.vector.tensor_scalar(res[:], o[:, 0:n], bias, None, ALU.add)
                 nc.sync.dma_start(out=out[c * P : (c + 1) * P, lo : lo + n], in_=res[:])
 
-        lo_a, n_a = PIECES[0]
-        lo_b, n_b = PIECES[1]
+        def gather_piece(i, t):
+            lo, n = PIECES[i]
+            gather_second(4 + t, z1[i][:, t, :], lo, n)
+
+        def quantize_piece(i):
+            quantize(z1_w[i], z1_s[i], z1_bf[i][:].rearrange("p j t -> p (j t)"))
+
+        def interleave_on_scalar(dst, src):
+            nc.scalar.activation(out=dst[:], in_=src[:].rearrange("p t j -> p j t"), func=ACT.Copy)
+
         gather_first(0)
         for s in range(1, 8):
             if s >= 4:
@@ -245,18 +252,28 @@ def tile_list_pair_bond_logits_kernel(
             if s - 1 < 4:
                 gather_second(s - 1, z0[:, s - 1, :], 0, PAIRS)
             else:
-                gather_second(s - 1, z1[0][:, s - 5, :], lo_a, n_a)
-        nc.scalar.activation(out=z0_bf[:], in_=z0[:].rearrange("p t j -> p j t"), func=ACT.Copy)
+                gather_piece(0, s - 5)
+        interleave_on_scalar(z0_bf, z0)
         quantize(w2_w, w2_s, w2_bf[:].rearrange("p b n t -> p (b n t)"))
-        gather_second(7, z1[0][:, 3, :], lo_a, n_a)
-        nc.scalar.activation(out=z1_bf[0][:], in_=z1[0][:].rearrange("p t j -> p j t"), func=ACT.Copy)
-        gather_second(4, z1[1][:, 0, :], lo_b, n_b)
-        gather_second(5, z1[1][:, 1, :], lo_b, n_b)
+        gather_piece(0, 3)
+        interleave_on_scalar(z1_bf[0], z1[0])
+        gather_piece(1, 0)
+        gather_piece(1, 1)
         quantize(z0_w, z0_s, z0_bf[:].rearrange("p j t -> p (j t)"))
-        gather_second(6, z1[1][:, 2, :], lo_b, n_b)
-        gather_second(7, z1[1][:, 3, :], lo_b, n_b)
-        quantize(z1_w[0], z1_s[0], z1_bf[0][:].rearrange("p j t -> p (j t)"))
-        nc.vector.tensor_copy(out=z1_bf[1][:], in_=z1[1][:].rearrange("p t j -> p j t"))
+        for i in range(len(PIECES)):
+            for c in range(N // P):
+                logit_pass(i, c, 0)
+        gather_piece(1, 2)
+        gather_piece(1, 3)
+        interleave_on_scalar(z1_bf[1], z1[1])
+        gather_piece(2, 0)
+        gather_piece(2, 1)
+        quantize_piece(0)
         logits(0, ("scalar", "scalar"))
-        quantize(z1_w[1], z1_s[1], z1_bf[1][:].rearrange("p j t -> p (j t)"))
-        logits(1, ("scalar", "vector"))
+        gather_piece(2, 2)
+        gather_piece(2, 3)
+        quantize_piece(1)
+        logits(1, ("scalar", "scalar"))
+        nc.vector.tensor_copy(out=z1_bf[2][:], in_=z1[2][:].rearrange("p t j -> p j t"))
+        quantize_piece(2)
+        logits(2, ("scalar", "vector"))

@@ -39,35 +39,38 @@ def tile_list_pair_bond_logits_kernel(
         offs_t = held.tile([P, S // 16], U16, name="offs_t")
         pos1_t = held.tile([P, PAIRS // 16], U16, name="pos1_t")
         pos2_t = held.tile([P, PAIRS // 16], U16, name="pos2_t")
-        tab_w = [held.tile([P, T], I32, name=f"tab_w{a}", align_bytes=64) for a in range(K_PASSES)]
-        tab_s = held.tile([P, T], U8, name="tab_s", align_bytes=64)
-        picked_s = held.tile([P, S], U8, name="picked_s", align_bytes=64)
-        w1_raw = [held.tile([P, K_PASSES * 1024], U8, name=f"w1_raw{b}", align_bytes=64) for b in range(R_PASSES)]
+        tab_w = [turn.tile([P, T], I32, name=f"tab_w{a}", offset=o * 1024) for a, o in enumerate((3, 20, 36))]
+        tab_s = turn.tile([P, T], U8, name="tab_s", offset=56 * 1024)
+        picked_s = turn.tile([P, S], U8, name="picked_s", offset=36 * 1024 - 512)
+        w1_raw = [turn.tile([P, K_PASSES * 1024], U8, name=f"w1_raw{b}", offset=o * 1024) for b, o in enumerate((0, 24))]
         w1s_raw = held.tile([P, H], U8, name="w1s_raw", align_bytes=64)
         staged = held.tile([P, S + H], U8, name="staged", align_bytes=64)
-        w1_w = [held.tile([P, K_PASSES * 1024], U8, name=f"w1_w{b}", align_bytes=64) for b in range(R_PASSES)]
-        v_w = [held.tile([P, S], I32, name=f"v_w{a}", align_bytes=64) for a in range(K_PASSES)]
+        w1_w = [
+            turn.tile([P, K_PASSES * 1024], U8, name=f"w1_w{b}", offset=o * 1024, align_bytes=64)
+            for b, o in enumerate((57, 40))
+        ]
+        v_w = [
+            turn.tile([P, S], I32, name=f"v_w{a}", offset=o * 1024, align_bytes=64) for a, o in enumerate((53, 0, 20))
+        ]
         planes = held.tile([P, K_PASSES, S + H], U8, name="planes", align_bytes=64)
         gain_rows = held.tile([R_PASSES, 512], F32, name="gain_rows")
         gain_perm = held.tile([P, 512], F32, name="gain_perm")
         gain_cols = held.tile([P, 4, 4], F32, name="gain_cols")
         ident = held.tile([P, P], F32, name="ident")
         warm = held.tile([P, 1], F32, name="warm")
-        w2_raw = held.tile([P, R_PASSES, 4, N], F32, name="w2_raw")
-        w2_bf = turn.tile([P, R_PASSES, N, 4], BF16, name="w2_bf", offset=2 * 4 * PAIRS, align_bytes=64)
+        w2_raw = turn.tile([P, R_PASSES, 4, N], F32, name="w2_raw", offset=27 * 1024)
+        w2_bf = turn.tile([P, R_PASSES, N, 4], BF16, name="w2_bf", offset=64 * 1024, align_bytes=64)
         w2_w = held.tile([P, R_PASSES * N], U32, name="w2_w", align_bytes=64)
         w2_s = held.tile([P, R_PASSES * N], U8, name="w2_s", align_bytes=64)
 
-        for a in range(K_PASSES):
-            nc.gpsimd.dma_start(out=tab_w[a][:], in_=tab_words[a].rearrange("p t i -> p (t i)").bitcast(I32))
-        make_identity(nc, ident[:])
         nc.vector.memset(tab_s[32:64, :].bitcast(I32), 0)
         nc.vector.memset(tab_s[96:128, :].bitcast(I32), 0)
-        nc.vector.memset(gain_perm[:], 0.0)
         nc.vector.memset(planes[:].rearrange("p a c -> p (a c)").bitcast(I32), 0)
-        nc.scalar.activation(out=warm[:], in_=gain_perm[:, 511:512], func=ACT.Tanh)
 
         w1_src = w1_words.bitcast(I32).rearrange("a p (b c) -> b p a c", b=R_PASSES)
+
+        def load_table(a):
+            nc.sync.dma_start(out=tab_w[a][:], in_=tab_words[a].rearrange("p t i -> p (t i)").bitcast(I32))
 
         def load_w1(b, queue):
             queue.dma_start(
@@ -82,16 +85,15 @@ def tile_list_pair_bond_logits_kernel(
         nc.sync.dma_start(offs_t[:], offs)
         load_scale_rows(tab_s, tab_scales)
         load_scale_rows(w1s_raw, w1_scales)
-        load_w1(0, nc.sync)
-        nc.sync.dma_start(out=gain_rows[:], in_=gain.rearrange("(b c) -> b c", b=R_PASSES))
-        nc.sync.dma_start(out=gain_perm[2:4, 0:P], in_=b2.rearrange("(c p) -> c p", p=P))
         nc.sync.dma_start(pos1_t[:], pos1)
         nc.sync.dma_start(pos2_t[:], pos2)
-        load_w1(1, nc.gpsimd)
-        w2_src = w2.rearrange("(b m t e) n -> e b m t n", b=R_PASSES, t=4, e=4)
-        for b in range(R_PASSES):
-            for e in range(4):
-                nc.gpsimd.dma_start(out=w2_raw[e:P:4, b, :, :], in_=w2_src[e, b])
+        load_table(0)
+        load_w1(0, nc.gpsimd)
+        nc.gpsimd.dma_start(out=gain_rows[:], in_=gain.rearrange("(b c) -> b c", b=R_PASSES))
+        nc.gpsimd.memset(gain_perm[:], 0.0)
+        nc.gpsimd.dma_start(out=gain_perm[2:4, 0:P], in_=b2.rearrange("(c p) -> c p", p=P))
+        make_identity(nc, ident[:])
+        nc.scalar.activation(out=warm[:], in_=gain_perm[:, 511:512], func=ACT.Tanh)
 
         for lo, hi in ((0, 32), (64, 96)):
             nc.vector.tensor_copy(
@@ -100,11 +102,13 @@ def tile_list_pair_bond_logits_kernel(
             )
         nc.vector.tensor_copy(out=picked_s[:], in_=tab_s[:].indirect(offs_t[:]))
         nc.vector.tensor_copy(out=staged[:, 0:S].bitcast(I32), in_=picked_s[:].bitcast(I32))
-        for a, base in enumerate((0, 16, 80)):
-            for r in range(4):
+        moves = [(a, base, r) for a, base in enumerate((0, 16, 80)) for r in range(4)]
+        for a_next, run in ((1, moves[:6]), (2, moves[6:])):
+            for a, base, r in run:
                 nc.sync.dma_start(
                     out=planes[r:P:32, a, :].bitcast(I32), in_=staged[base + r : base + 16 : 4, :].bitcast(I32)
                 )
+            load_table(a_next)
 
         nc.scalar.copy(
             out=gain_perm[0:R_PASSES, :].rearrange("b (t m e) -> b t m e", t=4, e=4),
@@ -134,10 +138,15 @@ def tile_list_pair_bond_logits_kernel(
         gain_wide = []
         for s in range(8):
             b, t = divmod(s, 4)
-            g = turn.tile([P, PAIRS], F32, name=f"gain_wide{s}", offset=s * 4 * PAIRS)
+            g = turn.tile([P, PAIRS], F32, name=f"gain_wide{s}", offset=(60 + 2 * s) * 1024)
             nc.scalar.activation(out=g[:], in_=gain_cols[:, t, b : b + 1].to_broadcast([P, PAIRS]), func=ACT.Copy)
             gain_wide.append(g)
         gather_words(1, 0, S)
+        load_w1(1, nc.sync)
+        w2_src = w2.rearrange("(b m t e) n -> e b m t n", b=R_PASSES, t=4, e=4)
+        for b in range(R_PASSES):
+            for e in range(4):
+                nc.sync.dma_start(out=w2_raw[e:P:4, b, :, :], in_=w2_src[e, b])
         gather_words(2, 0, BANK)
         gather_words(2, BANK, BANK)
         order_w1_words(1)
@@ -182,9 +191,12 @@ def tile_list_pair_bond_logits_kernel(
 
         first = [held.tile([P, PAIRS], F32, name=f"first{s}") for s in range(8)]
         z0 = held.tile([P, 4, PAIRS], F32, name="z0")
-        z1 = [held.tile([P, 4, n], F32, name=f"z1_{lo}") for lo, n in PIECES]
+        z1 = [turn.tile([P, 4, n], F32, name=f"z1_{lo}", offset=76 * 1024 + 16 * lo) for lo, n in PIECES]
         z0_bf = held.tile([P, PAIRS, 4], BF16, name="z0_bf", align_bytes=64)
-        z1_bf = [held.tile([P, n, 4], BF16, name=f"z1_bf{lo}", align_bytes=64) for lo, n in PIECES]
+        z1_bf = [
+            turn.tile([P, n, 4], BF16, name=f"z1_bf{lo}", offset=o * 1024, align_bytes=64)
+            for (lo, n), o in zip(PIECES, (84, 86, 86))
+        ]
         z0_w = held.tile([P, PAIRS], U32, name="z0_w", align_bytes=64)
         z0_s = held.tile([P, PAIRS], U8, name="z0_s", align_bytes=64)
         z1_w = [held.tile([P, n], U32, name=f"z1_w{lo}", align_bytes=64) for lo, n in PIECES]
@@ -225,7 +237,10 @@ def tile_list_pair_bond_logits_kernel(
                 logit_pass(i, c, 1)
                 o = logit_banks[i, c]
                 bias = gain_cols[:, 0, 2 + c : 3 + c]
-                res = held.tile([P, n], F32, name=f"res{i}_{c}")
+                if i == 0:
+                    res = turn.tile([P, n], F32, name=f"res{i}_{c}", offset=(80 + c) * 1024)
+                else:
+                    res = held.tile([P, n], F32, name=f"res{i}_{c}")
                 if evac_engines[c] == "scalar":
                     nc.scalar.activation(out=res[:], in_=o[:, 0:n], func=ACT.Identity, bias=bias)
                 else:

@@ -47,25 +47,27 @@ def tile_list_pair_bond_logits_kernel(
         staged = held.tile([P, S + H], U8, name="staged", align_bytes=64)
         w1_w = [
             turn.tile([P, K_PASSES * 1024], U8, name=f"w1_w{b}", offset=o * 1024, align_bytes=64)
-            for b, o in enumerate((57, 40))
+            for b, o in enumerate((54, 40))
         ]
         v_w = [
-            turn.tile([P, S], I32, name=f"v_w{a}", offset=o * 1024, align_bytes=64) for a, o in enumerate((53, 0, 20))
+            turn.tile([P, S], I32, name=f"v_w{a}", offset=o * 1024, align_bytes=64) for a, o in enumerate((90, 0, 20))
         ]
-        planes = held.tile([P, K_PASSES, S + H], U8, name="planes", align_bytes=64)
+        planes = [
+            turn.tile([P, S + H], U8, name=f"planes{a}", offset=o * 1024, align_bytes=64)
+            for a, o in enumerate((94, 57, 59))
+        ]
         gain_rows = held.tile([R_PASSES, 512], F32, name="gain_rows")
         gain_perm = held.tile([P, 512], F32, name="gain_perm")
         gain_cols = held.tile([P, 4, 4], F32, name="gain_cols")
         ident = held.tile([P, P], F32, name="ident")
-        warm = held.tile([P, 1], F32, name="warm")
         w2_raw = turn.tile([P, R_PASSES, 4, N], F32, name="w2_raw", offset=27 * 1024)
-        w2_bf = turn.tile([P, R_PASSES, N, 4], BF16, name="w2_bf", offset=64 * 1024, align_bytes=64)
+        w2_bf = turn.tile([P, R_PASSES, N, 4], BF16, name="w2_bf", offset=65 * 1024, align_bytes=64)
         w2_w = held.tile([P, R_PASSES * N], U32, name="w2_w", align_bytes=64)
         w2_s = held.tile([P, R_PASSES * N], U8, name="w2_s", align_bytes=64)
 
         nc.vector.memset(tab_s[32:64, :].bitcast(I32), 0)
         nc.vector.memset(tab_s[96:128, :].bitcast(I32), 0)
-        nc.vector.memset(planes[:].rearrange("p a c -> p (a c)").bitcast(I32), 0)
+        nc.vector.memset(planes[0][:].bitcast(I32), 0)
 
         w1_src = w1_words.bitcast(I32).rearrange("a p (b c) -> b p a c", b=R_PASSES)
 
@@ -88,12 +90,11 @@ def tile_list_pair_bond_logits_kernel(
         nc.sync.dma_start(pos1_t[:], pos1)
         nc.sync.dma_start(pos2_t[:], pos2)
         load_table(0)
+        nc.gpsimd.memset(gain_perm[:], 0.0)
+        make_identity(nc, ident[:])
         load_w1(0, nc.gpsimd)
         nc.gpsimd.dma_start(out=gain_rows[:], in_=gain.rearrange("(b c) -> b c", b=R_PASSES))
-        nc.gpsimd.memset(gain_perm[:], 0.0)
         nc.gpsimd.dma_start(out=gain_perm[2:4, 0:P], in_=b2.rearrange("(c p) -> c p", p=P))
-        make_identity(nc, ident[:])
-        nc.scalar.activation(out=warm[:], in_=gain_perm[:, 511:512], func=ACT.Tanh)
 
         for lo, hi in ((0, 32), (64, 96)):
             nc.vector.tensor_copy(
@@ -102,11 +103,13 @@ def tile_list_pair_bond_logits_kernel(
             )
         nc.vector.tensor_copy(out=picked_s[:], in_=tab_s[:].indirect(offs_t[:]))
         nc.vector.tensor_copy(out=staged[:, 0:S].bitcast(I32), in_=picked_s[:].bitcast(I32))
+        for a in range(1, K_PASSES):
+            nc.vector.memset(planes[a][:].bitcast(I32), 0)
         moves = [(a, base, r) for a, base in enumerate((0, 16, 80)) for r in range(4)]
         for a_next, run in ((1, moves[:6]), (2, moves[6:])):
             for a, base, r in run:
                 nc.sync.dma_start(
-                    out=planes[r:P:32, a, :].bitcast(I32), in_=staged[base + r : base + 16 : 4, :].bitcast(I32)
+                    out=planes[a][r:P:32, :].bitcast(I32), in_=staged[base + r : base + 16 : 4, :].bitcast(I32)
                 )
             load_table(a_next)
 
@@ -138,7 +141,7 @@ def tile_list_pair_bond_logits_kernel(
         gain_wide = []
         for s in range(8):
             b, t = divmod(s, 4)
-            g = turn.tile([P, PAIRS], F32, name=f"gain_wide{s}", offset=(60 + 2 * s) * 1024)
+            g = turn.tile([P, PAIRS], F32, name=f"gain_wide{s}", offset=(61 + 2 * s) * 1024)
             nc.scalar.activation(out=g[:], in_=gain_cols[:, t, b : b + 1].to_broadcast([P, PAIRS]), func=ACT.Copy)
             gain_wide.append(g)
         gather_words(1, 0, S)
@@ -162,9 +165,9 @@ def tile_list_pair_bond_logits_kernel(
             nc.tensor.matmul_mx(
                 out=acc[s, half][:],
                 lhsT=w1_w[b][:, a * 1024 + t * 256 : a * 1024 + (t + 1) * 256].bitcast(FP4X4),
-                lhsT_scale=planes[:, a, S + s * P : S + (s + 1) * P],
+                lhsT_scale=planes[a][:, S + s * P : S + (s + 1) * P],
                 rhs=v_w[a][:, cols].bitcast(FP8X4),
-                rhs_scale=planes[:, a, cols],
+                rhs_scale=planes[a][:, cols],
                 start=(a == 0),
                 stop=(a == K_PASSES - 1),
             )
@@ -191,11 +194,11 @@ def tile_list_pair_bond_logits_kernel(
 
         first = [held.tile([P, PAIRS], F32, name=f"first{s}") for s in range(8)]
         z0 = held.tile([P, 4, PAIRS], F32, name="z0")
-        z1 = [turn.tile([P, 4, n], F32, name=f"z1_{lo}", offset=76 * 1024 + 16 * lo) for lo, n in PIECES]
+        z1 = [turn.tile([P, 4, n], F32, name=f"z1_{lo}", offset=77 * 1024 + 16 * lo) for lo, n in PIECES]
         z0_bf = held.tile([P, PAIRS, 4], BF16, name="z0_bf", align_bytes=64)
         z1_bf = [
             turn.tile([P, n, 4], BF16, name=f"z1_bf{lo}", offset=o * 1024, align_bytes=64)
-            for (lo, n), o in zip(PIECES, (84, 86, 86))
+            for (lo, n), o in zip(PIECES, (85, 87, 87))
         ]
         z0_w = held.tile([P, PAIRS], U32, name="z0_w", align_bytes=64)
         z0_s = held.tile([P, PAIRS], U8, name="z0_s", align_bytes=64)
@@ -238,7 +241,7 @@ def tile_list_pair_bond_logits_kernel(
                 o = logit_banks[i, c]
                 bias = gain_cols[:, 0, 2 + c : 3 + c]
                 if i == 0:
-                    res = turn.tile([P, n], F32, name=f"res{i}_{c}", offset=(80 + c) * 1024)
+                    res = turn.tile([P, n], F32, name=f"res{i}_{c}", offset=(81 + c) * 1024)
                 else:
                     res = held.tile([P, n], F32, name=f"res{i}_{c}")
                 if evac_engines[c] == "scalar":

@@ -79,14 +79,14 @@ def tile_list_pair_bond_logits_kernel(
                 out=w1_raw[b][:].bitcast(I32).rearrange("p (a c) -> p a c", a=K_PASSES), in_=w1_src[b]
             )
 
-        def load_scale_rows(dst, src):
+        def load_scale_rows(dst, src, queue):
             rows = src.bitcast(I32).rearrange("a q c -> (a q) c")
-            nc.sync.dma_start(out=dst[0:32, :].bitcast(I32), in_=rows[0:32])
-            nc.sync.dma_start(out=dst[64:96, :].bitcast(I32), in_=rows[16:48])
+            queue.dma_start(out=dst[0:32, :].bitcast(I32), in_=rows[0:32])
+            queue.dma_start(out=dst[64:96, :].bitcast(I32), in_=rows[16:48])
 
         nc.sync.dma_start(offs_t[:], offs)
-        load_scale_rows(tab_s, tab_scales)
-        load_scale_rows(w1s_raw, w1_scales)
+        load_scale_rows(tab_s, tab_scales, nc.sync)
+        load_scale_rows(w1s_raw, w1_scales, nc.sync)
         nc.sync.dma_start(pos1_t[:], pos1)
         nc.sync.dma_start(pos2_t[:], pos2)
         load_table(0)
@@ -106,12 +106,13 @@ def tile_list_pair_bond_logits_kernel(
         for a in range(1, K_PASSES):
             nc.vector.memset(planes[a][:].bitcast(I32), 0)
         moves = [(a, base, r) for a, base in enumerate((0, 16, 80)) for r in range(4)]
-        for a_next, run in ((1, moves[:6]), (2, moves[6:])):
-            for a, base, r in run:
-                nc.sync.dma_start(
-                    out=planes[a][r:P:32, :].bitcast(I32), in_=staged[base + r : base + 16 : 4, :].bitcast(I32)
-                )
-            load_table(a_next)
+        table_before_move = {6: 1, 8: 2}
+        for i, (a, base, r) in enumerate(moves):
+            if i in table_before_move:
+                load_table(table_before_move[i])
+            nc.sync.dma_start(
+                out=planes[a][r:P:32, :].bitcast(I32), in_=staged[base + r : base + 16 : 4, :].bitcast(I32)
+            )
 
         nc.scalar.copy(
             out=gain_perm[0:R_PASSES, :].rearrange("b (t m e) -> b t m e", t=4, e=4),

@@ -58,16 +58,18 @@ def tile_list_pair_bond_logits_kernel(
         ]
         gain_rows = held.tile([R_PASSES, 512], F32, name="gain_rows")
         gain_perm = held.tile([P, 512], F32, name="gain_perm")
-        gain_cols = held.tile([P, 4, 4], F32, name="gain_cols")
+        gain_cols = held.tile([P, 4, R_PASSES], F32, name="gain_cols")
+        bias_cols = turn.tile([P, N // P], F32, name="bias_cols", offset=35 * 1024)
         ident = held.tile([P, P], F32, name="ident")
         w2_raw = turn.tile([P, R_PASSES, 4, N], F32, name="w2_raw", offset=27 * 1024)
         w2_bf = turn.tile([P, R_PASSES, N, 4], BF16, name="w2_bf", offset=65 * 1024, align_bytes=64)
         w2_w = held.tile([P, R_PASSES * N], U32, name="w2_w", align_bytes=64)
         w2_s = held.tile([P, R_PASSES * N], U8, name="w2_s", align_bytes=64)
 
-        nc.vector.memset(tab_s[32:64, :].bitcast(I32), 0)
-        nc.vector.memset(tab_s[96:128, :].bitcast(I32), 0)
-        nc.vector.memset(planes[0][:].bitcast(I32), 0)
+        nc.vector.memset(tab_s[0:32, :].bitcast(I32), 0)
+        nc.vector.memset(tab_s[64:112, :].bitcast(I32), 0)
+        nc.gpsimd.memset(w1s_raw[96:112, :].bitcast(I32), 0)
+        nc.gpsimd.memset(planes[0][:].bitcast(I32), 0)
 
         w1_src = w1_words.bitcast(I32).rearrange("a p (b c) -> b p a c", b=R_PASSES)
 
@@ -81,38 +83,36 @@ def tile_list_pair_bond_logits_kernel(
 
         def load_scale_rows(dst, src, queue):
             rows = src.bitcast(I32).rearrange("a q c -> (a q) c")
-            queue.dma_start(out=dst[0:32, :].bitcast(I32), in_=rows[0:32])
-            queue.dma_start(out=dst[64:96, :].bitcast(I32), in_=rows[16:48])
+            queue.dma_start(out=dst[32:64, :].bitcast(I32), in_=rows[0:32])
+            queue.dma_start(out=dst[112:128, :].bitcast(I32), in_=rows[32:48])
 
         nc.sync.dma_start(offs_t[:], offs)
         load_scale_rows(tab_s, tab_scales, nc.sync)
         load_scale_rows(w1s_raw, w1_scales, nc.sync)
+        load_table(0)
         nc.sync.dma_start(pos1_t[:], pos1)
         nc.sync.dma_start(pos2_t[:], pos2)
-        load_table(0)
         nc.gpsimd.memset(gain_perm[:], 0.0)
-        make_identity(nc, ident[:])
-        load_w1(0, nc.gpsimd)
         nc.gpsimd.dma_start(out=gain_rows[:], in_=gain.rearrange("(b c) -> b c", b=R_PASSES))
-        nc.gpsimd.dma_start(out=gain_perm[2:4, 0:P], in_=b2.rearrange("(c p) -> c p", p=P))
+        load_w1(0, nc.gpsimd)
+        make_identity(nc, ident[:])
 
-        for lo, hi in ((0, 32), (64, 96)):
+        nc.vector.tensor_copy(out=picked_s[:], in_=tab_s[:].indirect(offs_t[:]))
+        for lo, hi in ((32, 64), (96, 128)):
             nc.vector.tensor_copy(
                 out=staged[lo:hi, S:].bitcast(I32).rearrange("p (b t m) -> p b t m", b=R_PASSES, t=4),
                 in_=w1s_raw[lo:hi, :].bitcast(I32).rearrange("p (b m t) -> p b t m", b=R_PASSES, t=4),
             )
-        nc.vector.tensor_copy(out=picked_s[:], in_=tab_s[:].indirect(offs_t[:]))
         nc.vector.tensor_copy(out=staged[:, 0:S].bitcast(I32), in_=picked_s[:].bitcast(I32))
         for a in range(1, K_PASSES):
             nc.vector.memset(planes[a][:].bitcast(I32), 0)
-        moves = [(a, base, r) for a, base in enumerate((0, 16, 80)) for r in range(4)]
-        table_before_move = {6: 1, 8: 2}
-        for i, (a, base, r) in enumerate(moves):
-            if i in table_before_move:
-                load_table(table_before_move[i])
-            nc.sync.dma_start(
-                out=planes[a][r:P:32, :].bitcast(I32), in_=staged[base + r : base + 16 : 4, :].bitcast(I32)
-            )
+        for a, base in enumerate((32, 48, 112)):
+            if a > 0:
+                load_table(a)
+            for r in range(4):
+                nc.sync.dma_start(
+                    out=planes[a][r:P:32, :].bitcast(I32), in_=staged[base + r : base + 16 : 4, :].bitcast(I32)
+                )
 
         nc.scalar.copy(
             out=gain_perm[0:R_PASSES, :].rearrange("b (t m e) -> b t m e", t=4, e=4),
@@ -121,7 +121,7 @@ def tile_list_pair_bond_logits_kernel(
         gain_ps = bank("gain_ps")
         for t in range(4):
             nc.tensor.transpose(gain_ps[:, t * P : (t + 1) * P], gain_perm[:, t * P : (t + 1) * P], ident[:])
-        nc.scalar.copy(out=gain_cols[:], in_=gain_ps[:].rearrange("p (t c) -> p t c", t=4)[:, :, 0:4])
+        nc.scalar.copy(out=gain_cols[:], in_=gain_ps[:].rearrange("p (t c) -> p t c", t=4)[:, :, 0:R_PASSES])
 
         def order_w1_words(b):
             for a in range(K_PASSES):
@@ -151,6 +151,8 @@ def tile_list_pair_bond_logits_kernel(
         for b in range(R_PASSES):
             for e in range(4):
                 nc.sync.dma_start(out=w2_raw[e:P:4, b, :, :], in_=w2_src[e, b])
+        with nc.allow_non_contiguous_dma(reason="one bias to a partition"):
+            nc.sync.dma_start(out=bias_cols[:], in_=b2.rearrange("(c p) -> p c", p=P))
         gather_words(2, 0, BANK)
         gather_words(2, BANK, BANK)
         order_w1_words(1)
@@ -240,7 +242,7 @@ def tile_list_pair_bond_logits_kernel(
             for c in range(N // P):
                 logit_pass(i, c, 1)
                 o = logit_banks[i, c]
-                bias = gain_cols[:, 0, 2 + c : 3 + c]
+                bias = bias_cols[:, c : c + 1]
                 if i == 0:
                     res = turn.tile([P, n], F32, name=f"res{i}_{c}", offset=(81 + c) * 1024)
                 else:

@@ -1,7 +1,6 @@
 from contextlib import ExitStack
 
 import concourse.mybir as mybir
-from concourse.masks import make_identity
 
 T, S, PAIRS, K, H, N = 4096, 1024, 512, 1536, 1024, 256
 FLOPS = 2 * K * H * S + 2 * H * N * PAIRS
@@ -19,6 +18,7 @@ ALU = mybir.AluOpType
 
 P = 128
 BANK = 512
+KIB = 1024
 K_PASSES = K // 512
 R_PASSES = H // 512
 PIECES = ((0, 256), (256, 128), (384, 128))
@@ -36,100 +36,107 @@ def tile_list_pair_bond_logits_kernel(
         def bank(name):
             return psum.tile([P, BANK], F32, name=name, tag="bank")
 
+        def placed(name, shape, dtype, kib):
+            return turn.tile(shape, dtype, name=name, offset=int(kib * KIB), align_bytes=64)
+
+        def kept(name, shape, dtype):
+            return held.tile(shape, dtype, name=name, align_bytes=64)
+
         offs_t = held.tile([P, S // 16], U16, name="offs_t")
         pos1_t = held.tile([P, PAIRS // 16], U16, name="pos1_t")
         pos2_t = held.tile([P, PAIRS // 16], U16, name="pos2_t")
-        tab_w = [turn.tile([P, T], I32, name=f"tab_w{a}", offset=o * 1024) for a, o in enumerate((3, 20, 36))]
-        tab_s = turn.tile([P, T], U8, name="tab_s", offset=56 * 1024)
-        picked_s = turn.tile([P, S], U8, name="picked_s", offset=36 * 1024 - 512)
-        w1_raw = [turn.tile([P, K_PASSES * 1024], U8, name=f"w1_raw{b}", offset=o * 1024) for b, o in enumerate((0, 24))]
-        w1s_raw = held.tile([P, H], U8, name="w1s_raw", align_bytes=64)
-        staged = held.tile([P, S + H], U8, name="staged", align_bytes=64)
-        w1_w = [
-            turn.tile([P, K_PASSES * 1024], U8, name=f"w1_w{b}", offset=o * 1024, align_bytes=64)
-            for b, o in enumerate((54, 40))
-        ]
-        v_w = [
-            turn.tile([P, S], I32, name=f"v_w{a}", offset=o * 1024, align_bytes=64) for a, o in enumerate((90, 0, 20))
-        ]
-        planes = [
-            turn.tile([P, S + H], U8, name=f"planes{a}", offset=o * 1024, align_bytes=64)
-            for a, o in enumerate((94, 57, 59))
-        ]
-        gain_rows = held.tile([R_PASSES, 512], F32, name="gain_rows")
-        gain_perm = held.tile([P, 512], F32, name="gain_perm")
-        gain_cols = held.tile([P, 4, R_PASSES], F32, name="gain_cols")
-        bias_cols = turn.tile([P, N // P], F32, name="bias_cols", offset=35 * 1024)
-        ident = held.tile([P, P], F32, name="ident")
-        w2_raw = turn.tile([P, R_PASSES, 4, N], F32, name="w2_raw", offset=27 * 1024)
-        w2_bf = turn.tile([P, R_PASSES, N, 4], BF16, name="w2_bf", offset=65 * 1024, align_bytes=64)
-        w2_w = held.tile([P, R_PASSES * N], U32, name="w2_w", align_bytes=64)
-        w2_s = held.tile([P, R_PASSES * N], U8, name="w2_s", align_bytes=64)
+        tab_w = [placed(f"tab_w{a}", [P, T], I32, 16 * a) for a in range(K_PASSES)]
+        picked_s = placed("picked_s", [P, S], U8, 32)
+        tab_s = kept("tab_s", [P, T], U8)
+        w1s_raw = kept("w1s_raw", [P, H], U8)
+        staged = kept("staged", [P, S + H], U8)
+        planes = [kept(f"planes{a}", [P, S + H], U8) for a in range(K_PASSES)]
+        w1_raw = [kept("w1_raw0", [P, K_PASSES * KIB], U8), placed("w1_raw1", [P, K_PASSES * KIB], U8, 16)]
+        w1_first = kept("w1_first", [P, KIB], U8)
+        w1_lead = kept("w1_lead", [P, KIB], U8)
+        w1_next = placed("w1_next", [P, KIB], U8, 33)
+        w1_late = placed("w1_late", [P, K_PASSES * KIB], U8, 34)
+        v_w = [kept(f"v_w{a}", [P, S], I32) for a in range(K_PASSES)]
+        gain_rows = kept("gain_rows", [P, P], F32)
+        gain_dealt = kept("gain_dealt", [P, P], F32)
+        gain_cols = kept("gain_cols", [P, P], F32)
+        bias_cols = placed("bias_cols", [P, N // P], F32, 27)
+        w2_raw = placed("w2_raw", [P, R_PASSES, 4, N], F32, 19)
+        w2_bf = placed("w2_bf", [P, R_PASSES, N, 4], BF16, 52)
+        w2_w = kept("w2_w", [P, R_PASSES * N], U32)
+        w2_s = placed("w2_s", [P, R_PASSES * N], U8, 62)
 
+        nc.vector.memset(gain_rows[:], 0.0)
         nc.vector.memset(tab_s[0:32, :].bitcast(I32), 0)
         nc.vector.memset(tab_s[64:112, :].bitcast(I32), 0)
-        nc.gpsimd.memset(w1s_raw[96:112, :].bitcast(I32), 0)
-        nc.gpsimd.memset(planes[0][:].bitcast(I32), 0)
+        nc.vector.memset(w1s_raw[96:112, :].bitcast(I32), 0)
+        for a in range(K_PASSES):
+            nc.vector.memset(planes[a][:].bitcast(I32), 0)
 
         w1_src = w1_words.bitcast(I32).rearrange("a p (b c) -> b p a c", b=R_PASSES)
 
         def load_table(a):
             nc.sync.dma_start(out=tab_w[a][:], in_=tab_words[a].rearrange("p t i -> p (t i)").bitcast(I32))
 
-        def load_w1(b, queue):
-            queue.dma_start(
-                out=w1_raw[b][:].bitcast(I32).rearrange("p (a c) -> p a c", a=K_PASSES), in_=w1_src[b]
-            )
+        def load_w1(b):
+            nc.sync.dma_start(out=w1_raw[b][:].bitcast(I32).rearrange("p (a c) -> p a c", a=K_PASSES), in_=w1_src[b])
 
-        def load_scale_rows(dst, src, queue):
+        def load_scale_rows(dst, src):
             rows = src.bitcast(I32).rearrange("a q c -> (a q) c")
-            queue.dma_start(out=dst[32:64, :].bitcast(I32), in_=rows[0:32])
-            queue.dma_start(out=dst[112:128, :].bitcast(I32), in_=rows[32:48])
+            nc.sync.dma_start(out=dst[32:64, :].bitcast(I32), in_=rows[0:32])
+            nc.sync.dma_start(out=dst[112:128, :].bitcast(I32), in_=rows[32:48])
 
         nc.sync.dma_start(offs_t[:], offs)
-        load_scale_rows(tab_s, tab_scales, nc.sync)
-        load_scale_rows(w1s_raw, w1_scales, nc.sync)
+        load_scale_rows(tab_s, tab_scales)
         load_table(0)
+        load_scale_rows(w1s_raw, w1_scales)
+        nc.sync.dma_start(out=gain_rows[0:P:16, :], in_=gain.rearrange("(b g c) -> g b c", b=R_PASSES, g=4))
         nc.sync.dma_start(pos1_t[:], pos1)
         nc.sync.dma_start(pos2_t[:], pos2)
-        nc.gpsimd.memset(gain_perm[:], 0.0)
-        nc.gpsimd.dma_start(out=gain_rows[:], in_=gain.rearrange("(b c) -> b c", b=R_PASSES))
-        load_w1(0, nc.gpsimd)
-        make_identity(nc, ident[:])
+        load_w1(0)
+        load_table(1)
 
         nc.vector.tensor_copy(out=picked_s[:], in_=tab_s[:].indirect(offs_t[:]))
         for lo, hi in ((32, 64), (96, 128)):
             nc.vector.tensor_copy(
-                out=staged[lo:hi, S:].bitcast(I32).rearrange("p (b t m) -> p b t m", b=R_PASSES, t=4),
-                in_=w1s_raw[lo:hi, :].bitcast(I32).rearrange("p (b m t) -> p b t m", b=R_PASSES, t=4),
+                out=staged[lo:hi, S:].bitcast(I32).rearrange("p (b t q w) -> p b t q w", b=R_PASSES, t=4, w=2),
+                in_=w1s_raw[lo:hi, :].bitcast(I32).rearrange("p (b q t w) -> p b t q w", b=R_PASSES, t=4, w=2),
             )
         nc.vector.tensor_copy(out=staged[:, 0:S].bitcast(I32), in_=picked_s[:].bitcast(I32))
-        for a in range(1, K_PASSES):
-            nc.vector.memset(planes[a][:].bitcast(I32), 0)
-        for a, base in enumerate((32, 48, 112)):
-            if a > 0:
-                load_table(a)
-            for r in range(4):
-                nc.sync.dma_start(
-                    out=planes[a][r:P:32, :].bitcast(I32), in_=staged[base + r : base + 16 : 4, :].bitcast(I32)
-                )
 
-        nc.scalar.copy(
-            out=gain_perm[0:R_PASSES, :].rearrange("b (t m e) -> b t m e", t=4, e=4),
-            in_=gain_rows[:].rearrange("b (m t e) -> b t m e", t=4, e=4),
+        def move_rows(a, r):
+            base = (32, 48, 112)[a]
+            nc.sync.dma_start(out=planes[a][r:P:32, :].bitcast(I32), in_=staged[base + r : base + 16 : 4, :].bitcast(I32))
+
+        moves = [(a, r) for a in range(K_PASSES) for r in range(4)]
+        for a, r in moves[:6]:
+            move_rows(a, r)
+        load_table(2)
+        for a, r in moves[6:]:
+            move_rows(a, r)
+
+        nc.vector.tensor_copy(
+            out=gain_dealt[:].rearrange("p (t q u) -> p t q u", t=4, u=8),
+            in_=gain_rows[:].rearrange("p (q t u) -> p t q u", t=4, u=8),
         )
-        gain_ps = bank("gain_ps")
-        for t in range(4):
-            nc.tensor.transpose(gain_ps[:, t * P : (t + 1) * P], gain_perm[:, t * P : (t + 1) * P], ident[:])
-        nc.scalar.copy(out=gain_cols[:], in_=gain_ps[:].rearrange("p (t c) -> p t c", t=4)[:, :, 0:R_PASSES])
+        nc.vector.transpose(out=gain_cols[:], in_=gain_dealt[:])
 
-        def order_w1_words(b):
-            for a in range(K_PASSES):
-                cols = slice(a * 1024, (a + 1) * 1024)
-                nc.vector.tensor_copy(
-                    out=w1_w[b][:, cols].bitcast(I32).rearrange("p (t m w) -> p t m w", t=4, w=2),
-                    in_=w1_raw[b][:, cols].bitcast(I32).rearrange("p (m t w) -> p t m w", t=4, w=2),
-                )
+        def order_w1(dst, b, passes, slots):
+            src = w1_raw[b][:].bitcast(I32).rearrange("p (a q t w) -> p t a q w", a=K_PASSES, t=4, w=4)
+            nc.vector.tensor_copy(
+                out=dst[:].bitcast(I32).rearrange("p (a t q w) -> p t a q w", q=16, w=4, t=slots.stop - slots.start),
+                in_=src[:, slots, passes],
+            )
+
+        def w1_tile(s, a):
+            b, t = divmod(s, 4)
+            if b == 1:
+                tile, place = w1_late, 4 * a + t
+            elif a == 0:
+                tile, place = w1_first, t
+            else:
+                tile, place = (w1_lead, w1_next)[t // 2], 2 * (a - 1) + t % 2
+            return tile[:, 256 * place : 256 * (place + 1)].bitcast(FP4X4)
 
         def gather_words(a, lo, n):
             nc.vector.tensor_copy(
@@ -138,53 +145,63 @@ def tile_list_pair_bond_logits_kernel(
             )
 
         gather_words(0, 0, S)
-        order_w1_words(0)
+        order_w1(w1_first, 0, slice(0, 1), slice(0, 4))
+        order_w1(w1_lead, 0, slice(1, 3), slice(0, 2))
         gain_wide = []
         for s in range(8):
             b, t = divmod(s, 4)
-            g = turn.tile([P, PAIRS], F32, name=f"gain_wide{s}", offset=(61 + 2 * s) * 1024)
-            nc.scalar.activation(out=g[:], in_=gain_cols[:, t, b : b + 1].to_broadcast([P, PAIRS]), func=ACT.Copy)
+            g = placed(f"gain_wide{s}", [P, PAIRS], F32, 48 + 2 * s)
+            col = 32 * t + 16 * b
+            nc.scalar.activation(out=g[:], in_=gain_cols[:, col : col + 1].to_broadcast([P, PAIRS]), func=ACT.Copy)
             gain_wide.append(g)
         gather_words(1, 0, S)
-        load_w1(1, nc.sync)
-        w2_src = w2.rearrange("(b m t e) n -> e b m t n", b=R_PASSES, t=4, e=4)
+        load_w1(1)
+        w2_src = w2.rearrange("(b q t u) n -> b t q u n", b=R_PASSES, t=4, u=8)
         for b in range(R_PASSES):
-            for e in range(4):
-                nc.sync.dma_start(out=w2_raw[e:P:4, b, :, :], in_=w2_src[e, b])
+            for t in range(4):
+                nc.sync.dma_start(out=w2_raw[:, b, t, :], in_=w2_src[b, t])
         with nc.allow_non_contiguous_dma(reason="one bias to a partition"):
             nc.sync.dma_start(out=bias_cols[:], in_=b2.rearrange("(c p) -> p c", p=P))
         gather_words(2, 0, BANK)
         gather_words(2, BANK, BANK)
-        order_w1_words(1)
+        order_w1(w1_next, 0, slice(1, 3), slice(2, 4))
+        order_w1(w1_late, 1, slice(0, 3), slice(0, 4))
 
-        h = [held.tile([P, S], F32, name=f"h{s}") for s in range(8)]
+        h = [kept(f"h{s}", [P, S], F32) for s in range(8)]
         acc = {}
 
-        def h_pass(s, half, a):
-            b, t = divmod(s, 4)
+        def h_pass(s, half, a, last=K_PASSES - 1):
             if a == 0:
                 acc[s, half] = bank(f"acc{s}_{half}")
             cols = slice(half * BANK, (half + 1) * BANK)
             nc.tensor.matmul_mx(
                 out=acc[s, half][:],
-                lhsT=w1_w[b][:, a * 1024 + t * 256 : a * 1024 + (t + 1) * 256].bitcast(FP4X4),
+                lhsT=w1_tile(s, a),
                 lhsT_scale=planes[a][:, S + s * P : S + (s + 1) * P],
                 rhs=v_w[a][:, cols].bitcast(FP8X4),
                 rhs_scale=planes[a][:, cols],
                 start=(a == 0),
-                stop=(a == K_PASSES - 1),
+                stop=(a == last),
             )
 
         def h_tanh(s, half):
             nc.scalar.activation(out=h[s][:, half * BANK : (half + 1) * BANK], in_=acc[s, half][:], func=ACT.Tanh)
 
-        for a in range(K_PASSES - 1):
-            for s in range(4):
-                for half in range(2):
-                    h_pass(s, half, a)
-        for s, half in ((0, 0), (1, 0), (0, 1), (1, 1), (2, 0), (2, 1), (3, 0), (3, 1)):
-            h_pass(s, half, K_PASSES - 1)
-            h_tanh(s, half)
+        for s in range(4):
+            for half in range(2):
+                h_pass(s, half, 0)
+        for s in range(2):
+            for half in range(2):
+                h_pass(s, half, 1)
+        for half in range(2):
+            for s in range(2):
+                h_pass(s, half, 2)
+                h_tanh(s, half)
+        for s in range(2, 4):
+            for half in range(2):
+                h_pass(s, half, 2, last=1)
+                h_pass(s, half, 1, last=1)
+                h_tanh(s, half)
 
         def h_whole(s):
             for half in range(2):
@@ -195,18 +212,17 @@ def tile_list_pair_bond_logits_kernel(
         def interleave_w2(b):
             nc.scalar.activation(out=w2_bf[:, b], in_=w2_raw[:, b].rearrange("p t n -> p n t"), func=ACT.Copy)
 
-        first = [held.tile([P, PAIRS], F32, name=f"first{s}") for s in range(8)]
-        z0 = held.tile([P, 4, PAIRS], F32, name="z0")
-        z1 = [turn.tile([P, 4, n], F32, name=f"z1_{lo}", offset=77 * 1024 + 16 * lo) for lo, n in PIECES]
-        z0_bf = held.tile([P, PAIRS, 4], BF16, name="z0_bf", align_bytes=64)
-        z1_bf = [
-            turn.tile([P, n, 4], BF16, name=f"z1_bf{lo}", offset=o * 1024, align_bytes=64)
-            for (lo, n), o in zip(PIECES, (85, 87, 87))
-        ]
-        z0_w = held.tile([P, PAIRS], U32, name="z0_w", align_bytes=64)
-        z0_s = held.tile([P, PAIRS], U8, name="z0_s", align_bytes=64)
-        z1_w = [held.tile([P, n], U32, name=f"z1_w{lo}", align_bytes=64) for lo, n in PIECES]
-        z1_s = [held.tile([P, n], U8, name=f"z1_s{lo}", align_bytes=64) for lo, n in PIECES]
+        wide = PIECES[2][0]
+        first = [kept(f"first{s}", [P, PAIRS], F32) for s in range(8)]
+        z0 = kept("z0", [P, 4, PAIRS], F32)
+        z0_bf = placed("z0_bf", [P, PAIRS, 4], BF16, 64)
+        z1_wide = kept("z1_wide", [P, 4, wide], F32)
+        z1_end = placed("z1_end", [P, 4, PAIRS - wide], F32, 64)
+        z1_bf = [placed(f"z1_bf{lo}", [P, n, 4], BF16, o) for (lo, n), o in zip(PIECES, (68, 70, 68))]
+        z0_w = kept("z0_w", [P, PAIRS], U32)
+        z0_s = placed("z0_s", [P, PAIRS], U8, 63)
+        z1_w = [kept(f"z1_w{lo}", [P, n], U32) for lo, n in PIECES]
+        z1_s = [kept(f"z1_s{lo}", [P, n], U8) for lo, n in PIECES]
 
         def gather_first(s):
             nc.vector.tensor_tensor(first[s][:], h[s][:].indirect(pos1_t[:]), gain_wide[s][:], ALU.mult)
@@ -239,29 +255,22 @@ def tile_list_pair_bond_logits_kernel(
 
         def logits(i, evac_engines):
             lo, n = PIECES[i]
+            res = kept(f"res{i}", [P, N // P, n], F32)
             for c in range(N // P):
                 logit_pass(i, c, 1)
                 o = logit_banks[i, c]
                 bias = bias_cols[:, c : c + 1]
-                if i == 0:
-                    res = turn.tile([P, n], F32, name=f"res{i}_{c}", offset=(81 + c) * 1024)
-                else:
-                    res = held.tile([P, n], F32, name=f"res{i}_{c}")
                 if evac_engines[c] == "scalar":
-                    nc.scalar.activation(out=res[:], in_=o[:, 0:n], func=ACT.Identity, bias=bias)
+                    nc.scalar.activation(out=res[:, c, :], in_=o[:, 0:n], func=ACT.Identity, bias=bias)
                 else:
-                    nc.vector.tensor_scalar(res[:], o[:, 0:n], bias, None, ALU.add)
-                nc.sync.dma_start(out=out[c * P : (c + 1) * P, lo : lo + n], in_=res[:])
-
-        def gather_piece(i, t):
-            lo, n = PIECES[i]
-            gather_second(4 + t, z1[i][:, t, :], lo, n)
+                    nc.vector.tensor_scalar(res[:, c, :], o[:, 0:n], bias, None, ALU.add)
+            nc.sync.dma_start(out=out.rearrange("(c p) j -> p c j", p=P)[:, :, lo : lo + n], in_=res[:])
 
         def quantize_piece(i):
             quantize(z1_w[i], z1_s[i], z1_bf[i][:].rearrange("p j t -> p (j t)"))
 
         def interleave_on_scalar(dst, src):
-            nc.scalar.activation(out=dst[:], in_=src[:].rearrange("p t j -> p j t"), func=ACT.Copy)
+            nc.scalar.activation(out=dst, in_=src.rearrange("p t j -> p j t"), func=ACT.Copy)
 
         gather_first(0)
         for s in range(1, 8):
@@ -273,28 +282,23 @@ def tile_list_pair_bond_logits_kernel(
             if s - 1 < 4:
                 gather_second(s - 1, z0[:, s - 1, :], 0, PAIRS)
             else:
-                gather_piece(0, s - 5)
-        interleave_on_scalar(z0_bf, z0)
+                gather_second(s - 1, z1_wide[:, s - 5, :], 0, wide)
+        interleave_on_scalar(z0_bf[:], z0[:])
         quantize(w2_w, w2_s, w2_bf[:].rearrange("p b n t -> p (b n t)"))
-        gather_piece(0, 3)
-        interleave_on_scalar(z1_bf[0], z1[0])
-        gather_piece(1, 0)
-        gather_piece(1, 1)
+        gather_second(7, z1_wide[:, 3, :], 0, wide)
+        for i in range(2):
+            lo, n = PIECES[i]
+            interleave_on_scalar(z1_bf[i][:], z1_wide[:, :, lo : lo + n])
         quantize(z0_w, z0_s, z0_bf[:].rearrange("p j t -> p (j t)"))
         for i in range(len(PIECES)):
             for c in range(N // P):
                 logit_pass(i, c, 0)
-        gather_piece(1, 2)
-        gather_piece(1, 3)
-        interleave_on_scalar(z1_bf[1], z1[1])
-        gather_piece(2, 0)
-        gather_piece(2, 1)
+        for t in range(4):
+            gather_second(4 + t, z1_end[:, t, :], wide, PAIRS - wide)
         quantize_piece(0)
-        logits(0, ("scalar", "scalar"))
-        gather_piece(2, 2)
-        gather_piece(2, 3)
+        nc.vector.tensor_copy(out=z1_bf[2][:], in_=z1_end[:].rearrange("p t j -> p j t"))
         quantize_piece(1)
-        logits(1, ("scalar", "scalar"))
-        nc.vector.tensor_copy(out=z1_bf[2][:], in_=z1[2][:].rearrange("p t j -> p j t"))
         quantize_piece(2)
+        logits(0, ("scalar", "scalar"))
+        logits(1, ("scalar", "vector"))
         logits(2, ("scalar", "vector"))

@@ -197,35 +197,41 @@ def tile_list_pair_bond_logits_kernel(
             for s in range(2):
                 h_pass(s, half, 2)
                 h_tanh(s, half)
-        for s in range(2, 4):
-            for half in range(2):
+        for half in range(2):
+            for s in range(2, 4):
                 h_pass(s, half, 2, last=1)
+            for s in range(2, 4):
                 h_pass(s, half, 1, last=1)
                 h_tanh(s, half)
 
-        def h_whole(s):
+        def h_pair(s0):
             for half in range(2):
-                for a in range(K_PASSES):
-                    h_pass(s, half, a)
-                h_tanh(s, half)
+                for s in (s0, s0 + 1):
+                    for a in range(K_PASSES - 1):
+                        h_pass(s, half, a)
+                for s in (s0, s0 + 1):
+                    h_pass(s, half, K_PASSES - 1)
+                    h_tanh(s, half)
 
         def interleave_w2(b):
             nc.scalar.activation(out=w2_bf[:, b], in_=w2_raw[:, b].rearrange("p t n -> p n t"), func=ACT.Copy)
 
         wide = PIECES[2][0]
-        first = [kept(f"first{s}", [P, PAIRS], F32) for s in range(8)]
+        shared = kept("shared", [P, 7 * PAIRS], F32)
+        slots = shared[:].rearrange("p (s j) -> p s j", j=PAIRS)
+        first = [kept(f"first{s}", [P, PAIRS], F32)[:] for s in range(6)] + [slots[:, 0, :], slots[:, 1, :]]
         z0 = kept("z0", [P, 4, PAIRS], F32)
         z0_bf = placed("z0_bf", [P, PAIRS, 4], BF16, 64)
-        z1_wide = kept("z1_wide", [P, 4, wide], F32)
-        z1_end = placed("z1_end", [P, 4, PAIRS - wide], F32, 64)
-        z1_bf = [placed(f"z1_bf{lo}", [P, n, 4], BF16, o) for (lo, n), o in zip(PIECES, (68, 70, 68))]
+        z1_wide = slots[:, 3:7, 0:wide]
+        z1_end = slots[:, 0:4, 0 : PAIRS - wide]
+        z1_bf = [kept(f"z1_bf{lo}", [P, n, 4], BF16) for lo, n in PIECES]
         z0_w = kept("z0_w", [P, PAIRS], U32)
         z0_s = placed("z0_s", [P, PAIRS], U8, 63)
         z1_w = [kept(f"z1_w{lo}", [P, n], U32) for lo, n in PIECES]
         z1_s = [kept(f"z1_s{lo}", [P, n], U8) for lo, n in PIECES]
 
         def gather_first(s):
-            nc.vector.tensor_tensor(first[s][:], h[s][:].indirect(pos1_t[:]), gain_wide[s][:], ALU.mult)
+            nc.vector.tensor_tensor(first[s], h[s][:].indirect(pos1_t[:]), gain_wide[s][:], ALU.mult)
 
         def gather_second(s, dst, lo, n):
             nc.vector.tensor_tensor(
@@ -264,7 +270,7 @@ def tile_list_pair_bond_logits_kernel(
                     nc.scalar.activation(out=res[:, c, :], in_=o[:, 0:n], func=ACT.Identity, bias=bias)
                 else:
                     nc.vector.tensor_scalar(res[:, c, :], o[:, 0:n], bias, None, ALU.add)
-            nc.sync.dma_start(out=out.rearrange("(c p) j -> p c j", p=P)[:, :, lo : lo + n], in_=res[:])
+                nc.sync.dma_start(out=out[c * P : (c + 1) * P, lo : lo + n], in_=res[:, c, :])
 
         def quantize_piece(i):
             quantize(z1_w[i], z1_s[i], z1_bf[i][:].rearrange("p j t -> p (j t)"))
@@ -272,20 +278,23 @@ def tile_list_pair_bond_logits_kernel(
         def interleave_on_scalar(dst, src):
             nc.scalar.activation(out=dst, in_=src.rearrange("p t j -> p j t"), func=ACT.Copy)
 
-        gather_first(0)
-        for s in range(1, 8):
-            if s >= 4:
-                h_whole(s)
-            if s in (5, 6):
-                interleave_w2(s - 5)
-            gather_first(s)
-            if s - 1 < 4:
-                gather_second(s - 1, z0[:, s - 1, :], 0, PAIRS)
-            else:
-                gather_second(s - 1, z1_wide[:, s - 5, :], 0, wide)
-        interleave_on_scalar(z0_bf[:], z0[:])
-        quantize(w2_w, w2_s, w2_bf[:].rearrange("p b n t -> p (b n t)"))
-        gather_second(7, z1_wide[:, 3, :], 0, wide)
+        for s0 in range(0, 8, 2):
+            if s0 >= 4:
+                h_pair(s0)
+            if s0 == 4:
+                for b in range(R_PASSES):
+                    interleave_w2(b)
+            if s0 == 6:
+                interleave_on_scalar(z0_bf[:], z0[:])
+            for s in (s0, s0 + 1):
+                gather_first(s)
+            if s0 == 6:
+                quantize(w2_w, w2_s, w2_bf[:].rearrange("p b n t -> p (b n t)"))
+            for s in (s0, s0 + 1):
+                if s < 4:
+                    gather_second(s, z0[:, s, :], 0, PAIRS)
+                else:
+                    gather_second(s, z1_wide[:, s - 4, :], 0, wide)
         for i in range(2):
             lo, n = PIECES[i]
             interleave_on_scalar(z1_bf[i][:], z1_wide[:, :, lo : lo + n])
@@ -293,12 +302,21 @@ def tile_list_pair_bond_logits_kernel(
         for i in range(len(PIECES)):
             for c in range(N // P):
                 logit_pass(i, c, 0)
-        for t in range(4):
+        for t in range(3):
             gather_second(4 + t, z1_end[:, t, :], wide, PAIRS - wide)
         quantize_piece(0)
-        nc.vector.tensor_copy(out=z1_bf[2][:], in_=z1_end[:].rearrange("p t j -> p j t"))
+        gather_second(7, z1_end[:, 3, :], wide, PAIRS - wide)
         quantize_piece(1)
-        quantize_piece(2)
+        for half in range(2):
+            cols = slice(64 * half, 64 * (half + 1))
+            nc.vector.tensor_copy(out=z1_bf[2][:, cols, :], in_=z1_end[:, :, cols].rearrange("p t j -> p j t"))
+        for half in range(2):
+            cols = slice(64 * half, 64 * (half + 1))
+            nc.vector.quantize_mx(
+                out=z1_w[2][:, cols].bitcast(FP8X4),
+                scales=z1_s[2][:, cols],
+                in_=z1_bf[2][:, cols, :].rearrange("p j t -> p (j t)"),
+            )
         logits(0, ("scalar", "scalar"))
-        logits(1, ("scalar", "vector"))
+        logits(1, ("scalar", "scalar"))
         logits(2, ("scalar", "vector"))

@@ -67,9 +67,9 @@ def tile_list_pair_bond_logits_kernel(
         w2_s = placed("w2_s", [P, R_PASSES * N], U8, 62)
 
         nc.vector.memset(gain_rows[:], 0.0)
-        nc.vector.memset(tab_s[0:32, :].bitcast(I32), 0)
-        nc.vector.memset(tab_s[64:112, :].bitcast(I32), 0)
-        nc.vector.memset(w1s_raw[96:112, :].bitcast(I32), 0)
+        nc.vector.memset(tab_s[0:48, :].bitcast(I32), 0)
+        nc.vector.memset(tab_s[64:96, :].bitcast(I32), 0)
+        nc.vector.memset(w1s_raw[32:48, :].bitcast(I32), 0)
         for a in range(K_PASSES):
             nc.vector.memset(planes[a][:].bitcast(I32), 0)
 
@@ -83,16 +83,14 @@ def tile_list_pair_bond_logits_kernel(
 
         def load_scale_rows(dst, src):
             rows = src.bitcast(I32).rearrange("a q c -> (a q) c")
-            nc.sync.dma_start(out=dst[32:64, :].bitcast(I32), in_=rows[0:32])
-            nc.sync.dma_start(out=dst[112:128, :].bitcast(I32), in_=rows[32:48])
+            nc.sync.dma_start(out=dst[96:128, :].bitcast(I32), in_=rows[0:32])
+            nc.sync.dma_start(out=dst[48:64, :].bitcast(I32), in_=rows[32:48])
 
         nc.sync.dma_start(offs_t[:], offs)
         load_scale_rows(tab_s, tab_scales)
-        load_table(0)
         load_scale_rows(w1s_raw, w1_scales)
+        load_table(0)
         nc.sync.dma_start(out=gain_rows[0:P:16, :], in_=gain.rearrange("(b g c) -> g b c", b=R_PASSES, g=4))
-        nc.sync.dma_start(pos1_t[:], pos1)
-        nc.sync.dma_start(pos2_t[:], pos2)
         load_w1(0)
         load_table(1)
 
@@ -105,14 +103,14 @@ def tile_list_pair_bond_logits_kernel(
         nc.vector.tensor_copy(out=staged[:, 0:S].bitcast(I32), in_=picked_s[:].bitcast(I32))
 
         def move_rows(a, r):
-            base = (32, 48, 112)[a]
+            base = (96, 112, 48)[a]
             nc.sync.dma_start(out=planes[a][r:P:32, :].bitcast(I32), in_=staged[base + r : base + 16 : 4, :].bitcast(I32))
 
         moves = [(a, r) for a in range(K_PASSES) for r in range(4)]
-        for a, r in moves[:6]:
+        for a, r in moves[:5]:
             move_rows(a, r)
         load_table(2)
-        for a, r in moves[6:]:
+        for a, r in moves[5:]:
             move_rows(a, r)
 
         nc.vector.tensor_copy(
@@ -156,6 +154,8 @@ def tile_list_pair_bond_logits_kernel(
             gain_wide.append(g)
         gather_words(1, 0, S)
         load_w1(1)
+        nc.sync.dma_start(pos1_t[:], pos1)
+        nc.sync.dma_start(pos2_t[:], pos2)
         w2_src = w2.rearrange("(b q t u) n -> b t q u n", b=R_PASSES, t=4, u=8)
         for b in range(R_PASSES):
             for t in range(4):
@@ -224,7 +224,7 @@ def tile_list_pair_bond_logits_kernel(
         z0_bf = placed("z0_bf", [P, PAIRS, 4], BF16, 64)
         z1_wide = slots[:, 3:7, 0:wide]
         z1_end = slots[:, 0:4, 0 : PAIRS - wide]
-        z1_bf = [kept(f"z1_bf{lo}", [P, n, 4], BF16) for lo, n in PIECES]
+        z1_bf = [placed(f"z1_bf{lo}", [P, n, 4], BF16, o) for (lo, n), o in zip(PIECES, (68, 70, 71))]
         z0_w = kept("z0_w", [P, PAIRS], U32)
         z0_s = placed("z0_s", [P, PAIRS], U8, 63)
         z1_w = [kept(f"z1_w{lo}", [P, n], U32) for lo, n in PIECES]
@@ -261,16 +261,17 @@ def tile_list_pair_bond_logits_kernel(
 
         def logits(i, evac_engines):
             lo, n = PIECES[i]
-            res = kept(f"res{i}", [P, N // P, n], F32)
             for c in range(N // P):
+                res = placed(f"res{i}_{c}", [P, n], F32, 71 if (i, c) == (1, 1) else 72 + 2 * i + c)
                 logit_pass(i, c, 1)
                 o = logit_banks[i, c]
                 bias = bias_cols[:, c : c + 1]
                 if evac_engines[c] == "scalar":
-                    nc.scalar.activation(out=res[:, c, :], in_=o[:, 0:n], func=ACT.Identity, bias=bias)
+                    nc.scalar.activation(out=res[:], in_=o[:, 0:n], func=ACT.Identity, bias=bias)
                 else:
-                    nc.vector.tensor_scalar(res[:, c, :], o[:, 0:n], bias, None, ALU.add)
-                nc.sync.dma_start(out=out[c * P : (c + 1) * P, lo : lo + n], in_=res[:, c, :])
+                    nc.vector.tensor_scalar(res[:], o[:, 0:n], bias, None, ALU.add)
+                queue = nc.scalar if (i, c) == (2, 0) else nc.sync
+                queue.dma_start(out=out[c * P : (c + 1) * P, lo : lo + n], in_=res[:])
 
         def quantize_piece(i):
             quantize(z1_w[i], z1_s[i], z1_bf[i][:].rearrange("p j t -> p (j t)"))
@@ -288,8 +289,6 @@ def tile_list_pair_bond_logits_kernel(
                 interleave_on_scalar(z0_bf[:], z0[:])
             for s in (s0, s0 + 1):
                 gather_first(s)
-            if s0 == 6:
-                quantize(w2_w, w2_s, w2_bf[:].rearrange("p b n t -> p (b n t)"))
             for s in (s0, s0 + 1):
                 if s < 4:
                     gather_second(s, z0[:, s, :], 0, PAIRS)
@@ -298,6 +297,7 @@ def tile_list_pair_bond_logits_kernel(
         for i in range(2):
             lo, n = PIECES[i]
             interleave_on_scalar(z1_bf[i][:], z1_wide[:, :, lo : lo + n])
+        quantize(w2_w, w2_s, w2_bf[:].rearrange("p b n t -> p (b n t)"))
         quantize(z0_w, z0_s, z0_bf[:].rearrange("p j t -> p (j t)"))
         for i in range(len(PIECES)):
             for c in range(N // P):
@@ -318,5 +318,5 @@ def tile_list_pair_bond_logits_kernel(
                 in_=z1_bf[2][:, cols, :].rearrange("p j t -> p (j t)"),
             )
         logits(0, ("scalar", "scalar"))
-        logits(1, ("scalar", "scalar"))
+        logits(1, ("scalar", "vector"))
         logits(2, ("scalar", "vector"))

@@ -48,13 +48,16 @@ def tile_list_pair_bond_logits_kernel(
         tab_w = [placed(f"tab_w{a}", [P, T], I32, 16 * a) for a in range(K_PASSES)]
         picked_s = placed("picked_s", [P, S], U8, 32)
         tab_s = kept("tab_s", [P, T], U8)
-        w1s_raw = kept("w1s_raw", [P, H], U8)
-        staged = kept("staged", [P, S + H], U8)
-        planes = [kept(f"planes{a}", [P, S + H], U8) for a in range(K_PASSES)]
+        w1s_raw = kept("w1s_raw", [P, H // 2], U8)
+        staged = kept("staged", [P, S + H // 2], U8)
+        planes = [kept(f"planes{a}", [P, S + H // 2], U8) for a in range(K_PASSES)]
+        late_raw = kept("late_raw", [P, K_PASSES * H // 2], U8)
+        late_staged = kept("late_staged", [P, K_PASSES * H // 2], U8)
+        late_planes = placed("late_planes", [P, K_PASSES * H // 2], U8, 28)
         w1_raw = [kept("w1_raw0", [P, K_PASSES * KIB], U8), placed("w1_raw1", [P, K_PASSES * KIB], U8, 16)]
         w1_first = kept("w1_first", [P, KIB], U8)
         w1_lead = kept("w1_lead", [P, KIB], U8)
-        w1_next = placed("w1_next", [P, KIB], U8, 33)
+        w1_next = placed("w1_next", [P, KIB], U8, 40)
         w1_late = placed("w1_late", [P, K_PASSES * KIB], U8, 34)
         v_w = [kept(f"v_w{a}", [P, S], I32) for a in range(K_PASSES)]
         gain_rows = kept("gain_rows", [P, P], F32)
@@ -62,7 +65,7 @@ def tile_list_pair_bond_logits_kernel(
         gain_cols = kept("gain_cols", [P, P], F32)
         bias_cols = placed("bias_cols", [P, N // P], F32, 27)
         w2_raw = placed("w2_raw", [P, R_PASSES, 4, N], F32, 19)
-        w2_bf = placed("w2_bf", [P, R_PASSES, N, 4], BF16, 52)
+        w2_bf = placed("w2_bf", [P, R_PASSES, N, 4], BF16, 31)
         w2_w = kept("w2_w", [P, R_PASSES * N], U32)
         w2_s = placed("w2_s", [P, R_PASSES * N], U8, 62)
 
@@ -70,6 +73,7 @@ def tile_list_pair_bond_logits_kernel(
         nc.vector.memset(tab_s[0:48, :].bitcast(I32), 0)
         nc.vector.memset(tab_s[64:96, :].bitcast(I32), 0)
         nc.vector.memset(w1s_raw[32:48, :].bitcast(I32), 0)
+        nc.vector.memset(late_raw[0:16, :].bitcast(I32), 0)
         for a in range(K_PASSES):
             nc.vector.memset(planes[a][:].bitcast(I32), 0)
 
@@ -82,23 +86,27 @@ def tile_list_pair_bond_logits_kernel(
             nc.sync.dma_start(out=w1_raw[b][:].bitcast(I32).rearrange("p (a c) -> p a c", a=K_PASSES), in_=w1_src[b])
 
         def load_scale_rows(dst, src):
-            rows = src.bitcast(I32).rearrange("a q c -> (a q) c")
+            rows = src.rearrange("a q c -> (a q) c")
             nc.sync.dma_start(out=dst[96:128, :].bitcast(I32), in_=rows[0:32])
             nc.sync.dma_start(out=dst[48:64, :].bitcast(I32), in_=rows[32:48])
 
         nc.sync.dma_start(offs_t[:], offs)
-        load_scale_rows(tab_s, tab_scales)
-        load_scale_rows(w1s_raw, w1_scales)
+        load_scale_rows(tab_s, tab_scales.bitcast(I32))
+        load_scale_rows(w1s_raw, w1_scales.bitcast(I32)[:, :, 0 : H // 8])
         load_table(0)
         nc.sync.dma_start(out=gain_rows[0:P:16, :], in_=gain.rearrange("(b g c) -> g b c", b=R_PASSES, g=4))
+        nc.sync.dma_start(
+            out=late_raw[16:32, :].bitcast(I32).rearrange("p (a c) -> p a c", a=K_PASSES),
+            in_=w1_scales.bitcast(I32)[:, :, H // 8 : H // 4].rearrange("a q c -> q a c"),
+        )
         load_w1(0)
         load_table(1)
 
         nc.vector.tensor_copy(out=picked_s[:], in_=tab_s[:].indirect(offs_t[:]))
         for lo, hi in ((32, 64), (96, 128)):
             nc.vector.tensor_copy(
-                out=staged[lo:hi, S:].bitcast(I32).rearrange("p (b t q w) -> p b t q w", b=R_PASSES, t=4, w=2),
-                in_=w1s_raw[lo:hi, :].bitcast(I32).rearrange("p (b q t w) -> p b t q w", b=R_PASSES, t=4, w=2),
+                out=staged[lo:hi, S:].bitcast(I32).rearrange("p (t q w) -> p t q w", t=4, w=2),
+                in_=w1s_raw[lo:hi, :].bitcast(I32).rearrange("p (q t w) -> p t q w", t=4, w=2),
             )
         nc.vector.tensor_copy(out=staged[:, 0:S].bitcast(I32), in_=picked_s[:].bitcast(I32))
 
@@ -118,6 +126,11 @@ def tile_list_pair_bond_logits_kernel(
             in_=gain_rows[:].rearrange("p (q t u) -> p t q u", t=4, u=8),
         )
         nc.vector.transpose(out=gain_cols[:], in_=gain_dealt[:])
+
+        nc.vector.tensor_copy(
+            out=late_staged[0:32, :].bitcast(I32).rearrange("p (a t q w) -> p t a q w", a=K_PASSES, t=4, w=2),
+            in_=late_raw[0:32, :].bitcast(I32).rearrange("p (a q t w) -> p t a q w", a=K_PASSES, t=4, w=2),
+        )
 
         def order_w1(dst, b, passes, slots):
             src = w1_raw[b][:].bitcast(I32).rearrange("p (a q t w) -> p t a q w", a=K_PASSES, t=4, w=4)
@@ -153,9 +166,11 @@ def tile_list_pair_bond_logits_kernel(
             nc.scalar.activation(out=g[:], in_=gain_cols[:, col : col + 1].to_broadcast([P, PAIRS]), func=ACT.Copy)
             gain_wide.append(g)
         gather_words(1, 0, S)
-        load_w1(1)
         nc.sync.dma_start(pos1_t[:], pos1)
+        load_w1(1)
         nc.sync.dma_start(pos2_t[:], pos2)
+        for r in range(4):
+            nc.sync.dma_start(out=late_planes[r:P:32, :].bitcast(I32), in_=late_staged[16 + r : 32 : 4, :].bitcast(I32))
         w2_src = w2.rearrange("(b q t u) n -> b t q u n", b=R_PASSES, t=4, u=8)
         for b in range(R_PASSES):
             for t in range(4):
@@ -177,7 +192,9 @@ def tile_list_pair_bond_logits_kernel(
             nc.tensor.matmul_mx(
                 out=acc[s, half][:],
                 lhsT=w1_tile(s, a),
-                lhsT_scale=planes[a][:, S + s * P : S + (s + 1) * P],
+                lhsT_scale=planes[a][:, S + s * P : S + (s + 1) * P]
+                if s < 4
+                else late_planes[:, (4 * a + s - 4) * P : (4 * a + s - 3) * P],
                 rhs=v_w[a][:, cols].bitcast(FP8X4),
                 rhs_scale=planes[a][:, cols],
                 start=(a == 0),
@@ -193,8 +210,8 @@ def tile_list_pair_bond_logits_kernel(
         for s in range(2):
             for half in range(2):
                 h_pass(s, half, 1)
-        for half in range(2):
-            for s in range(2):
+        for s in range(2):
+            for half in range(2):
                 h_pass(s, half, 2)
                 h_tanh(s, half)
         for half in range(2):
@@ -217,13 +234,11 @@ def tile_list_pair_bond_logits_kernel(
             nc.scalar.activation(out=w2_bf[:, b], in_=w2_raw[:, b].rearrange("p t n -> p n t"), func=ACT.Copy)
 
         wide = PIECES[2][0]
-        shared = kept("shared", [P, 7 * PAIRS], F32)
-        slots = shared[:].rearrange("p (s j) -> p s j", j=PAIRS)
-        first = [kept(f"first{s}", [P, PAIRS], F32)[:] for s in range(6)] + [slots[:, 0, :], slots[:, 1, :]]
-        z0 = kept("z0", [P, 4, PAIRS], F32)
-        z0_bf = placed("z0_bf", [P, PAIRS, 4], BF16, 64)
-        z1_wide = slots[:, 3:7, 0:wide]
-        z1_end = slots[:, 0:4, 0 : PAIRS - wide]
+        first = [kept(f"first{s}", [P, PAIRS], F32) for s in range(8)]
+        z0 = placed("z0", [P, 4, PAIRS], F32, 40)
+        z0_bf = placed("z0_bf", [P, PAIRS, 4], BF16, 36)
+        z1_wide = kept("z1_wide", [P, 4, wide], F32)
+        z1_end = placed("z1_end", [P, 4, PAIRS - wide], F32, 36)
         z1_bf = [placed(f"z1_bf{lo}", [P, n, 4], BF16, o) for (lo, n), o in zip(PIECES, (68, 70, 71))]
         z0_w = kept("z0_w", [P, PAIRS], U32)
         z0_s = placed("z0_s", [P, PAIRS], U8, 63)
@@ -231,7 +246,7 @@ def tile_list_pair_bond_logits_kernel(
         z1_s = [kept(f"z1_s{lo}", [P, n], U8) for lo, n in PIECES]
 
         def gather_first(s):
-            nc.vector.tensor_tensor(first[s], h[s][:].indirect(pos1_t[:]), gain_wide[s][:], ALU.mult)
+            nc.vector.tensor_tensor(first[s][:], h[s][:].indirect(pos1_t[:]), gain_wide[s][:], ALU.mult)
 
         def gather_second(s, dst, lo, n):
             nc.vector.tensor_tensor(
@@ -239,7 +254,11 @@ def tile_list_pair_bond_logits_kernel(
             )
 
         def quantize(codes, scales, src):
-            nc.vector.quantize_mx(out=codes[:].bitcast(FP8X4), scales=scales[:], in_=src)
+            nc.vector.quantize_mx(out=codes.bitcast(FP8X4), scales=scales, in_=src)
+
+        def quantize_w2(b):
+            cols = slice(b * N, (b + 1) * N)
+            quantize(w2_w[:, cols], w2_s[:, cols], w2_bf[:, b].rearrange("p n t -> p (n t)"))
 
         logit_banks = {}
 
@@ -274,7 +293,7 @@ def tile_list_pair_bond_logits_kernel(
                 queue.dma_start(out=out[c * P : (c + 1) * P, lo : lo + n], in_=res[:])
 
         def quantize_piece(i):
-            quantize(z1_w[i], z1_s[i], z1_bf[i][:].rearrange("p j t -> p (j t)"))
+            quantize(z1_w[i][:], z1_s[i][:], z1_bf[i][:].rearrange("p j t -> p (j t)"))
 
         def interleave_on_scalar(dst, src):
             nc.scalar.activation(out=dst, in_=src.rearrange("p t j -> p j t"), func=ACT.Copy)
@@ -282,13 +301,14 @@ def tile_list_pair_bond_logits_kernel(
         for s0 in range(0, 8, 2):
             if s0 >= 4:
                 h_pair(s0)
-            if s0 == 4:
+            if s0 == 6:
                 for b in range(R_PASSES):
                     interleave_w2(b)
-            if s0 == 6:
                 interleave_on_scalar(z0_bf[:], z0[:])
             for s in (s0, s0 + 1):
                 gather_first(s)
+            if s0 == 6:
+                quantize_w2(0)
             for s in (s0, s0 + 1):
                 if s < 4:
                     gather_second(s, z0[:, s, :], 0, PAIRS)
@@ -297,8 +317,8 @@ def tile_list_pair_bond_logits_kernel(
         for i in range(2):
             lo, n = PIECES[i]
             interleave_on_scalar(z1_bf[i][:], z1_wide[:, :, lo : lo + n])
-        quantize(w2_w, w2_s, w2_bf[:].rearrange("p b n t -> p (b n t)"))
-        quantize(z0_w, z0_s, z0_bf[:].rearrange("p j t -> p (j t)"))
+        quantize(z0_w[:], z0_s[:], z0_bf[:].rearrange("p j t -> p (j t)"))
+        quantize_w2(1)
         for i in range(len(PIECES)):
             for c in range(N // P):
                 logit_pass(i, c, 0)

@@ -55,7 +55,7 @@ def tile_list_pair_bond_logits_kernel(
         late_staged = kept("late_staged", [P, K_PASSES * H // 2], U8)
         late_planes = placed("late_planes", [P, K_PASSES * H // 2], U8, 28)
         w1_raw = [kept("w1_raw0", [P, K_PASSES * KIB], U8), placed("w1_raw1", [P, K_PASSES * KIB], U8, 16)]
-        w1_first = kept("w1_first", [P, KIB], U8)
+        w1_first = placed("w1_first", [P, KIB], U8, 30)
         w1_lead = kept("w1_lead", [P, KIB], U8)
         w1_next = placed("w1_next", [P, KIB], U8, 40)
         w1_late = placed("w1_late", [P, K_PASSES * KIB], U8, 34)
@@ -156,7 +156,6 @@ def tile_list_pair_bond_logits_kernel(
             )
 
         gather_words(0, 0, S)
-        order_w1(w1_first, 0, slice(0, 1), slice(0, 4))
         order_w1(w1_lead, 0, slice(1, 3), slice(0, 2))
         gain_wide = []
         for s in range(8):
@@ -166,6 +165,7 @@ def tile_list_pair_bond_logits_kernel(
             nc.scalar.activation(out=g[:], in_=gain_cols[:, col : col + 1].to_broadcast([P, PAIRS]), func=ACT.Copy)
             gain_wide.append(g)
         gather_words(1, 0, S)
+        order_w1(w1_first, 0, slice(0, 1), slice(0, 4))
         nc.sync.dma_start(pos1_t[:], pos1)
         load_w1(1)
         nc.sync.dma_start(pos2_t[:], pos2)
@@ -207,13 +207,15 @@ def tile_list_pair_bond_logits_kernel(
         for s in range(4):
             for half in range(2):
                 h_pass(s, half, 0)
-        for s in range(2):
-            for half in range(2):
-                h_pass(s, half, 1)
-        for s in range(2):
-            for half in range(2):
-                h_pass(s, half, 2)
-                h_tanh(s, half)
+        for half in range(2):
+            h_pass(0, half, 1)
+        for half in range(2):
+            h_pass(0, half, 2)
+            h_tanh(0, half)
+        for half in range(2):
+            h_pass(1, half, 2, last=1)
+            h_pass(1, half, 1, last=1)
+            h_tanh(1, half)
         for half in range(2):
             for s in range(2, 4):
                 h_pass(s, half, 2, last=1)

@@ -48,24 +48,22 @@ def tile_list_pair_bond_logits_kernel(
         tab_w = [placed(f"tab_w{a}", [P, T], I32, 16 * a) for a in range(K_PASSES)]
         picked_s = placed("picked_s", [P, S], U8, 32)
         tab_s = kept("tab_s", [P, T], U8)
-        w1s_raw = kept("w1s_raw", [P, H // 2], U8)
-        staged = kept("staged", [P, S + H // 2], U8)
+        w1s_raw = kept("w1s_raw", [P, H], U8)
+        staged = kept("staged", [P, S + H], U8)
         planes = [kept(f"planes{a}", [P, S + H // 2], U8) for a in range(K_PASSES)]
-        late_raw = kept("late_raw", [P, K_PASSES * H // 2], U8)
-        late_staged = kept("late_staged", [P, K_PASSES * H // 2], U8)
-        late_planes = placed("late_planes", [P, K_PASSES * H // 2], U8, 28)
+        late_planes = [placed(f"late_planes{a}", [P, H // 2], U8, 28 + a / 2) for a in range(K_PASSES)]
         w1_raw = [kept("w1_raw0", [P, K_PASSES * KIB], U8), placed("w1_raw1", [P, K_PASSES * KIB], U8, 16)]
-        w1_first = placed("w1_first", [P, KIB], U8, 30)
+        w1_first = kept("w1_first", [P, KIB], U8)
         w1_lead = kept("w1_lead", [P, KIB], U8)
-        w1_next = placed("w1_next", [P, KIB], U8, 40)
+        w1_next = [placed(f"w1_next{a}", [P, KIB // 2], U8, o) for a, o in ((1, 33), (2, 40))]
         w1_late = placed("w1_late", [P, K_PASSES * KIB], U8, 34)
         v_w = [kept(f"v_w{a}", [P, S], I32) for a in range(K_PASSES)]
         gain_rows = kept("gain_rows", [P, P], F32)
         gain_dealt = kept("gain_dealt", [P, P], F32)
         gain_cols = kept("gain_cols", [P, P], F32)
         bias_cols = placed("bias_cols", [P, N // P], F32, 27)
-        w2_raw = placed("w2_raw", [P, R_PASSES, 4, N], F32, 19)
-        w2_bf = placed("w2_bf", [P, R_PASSES, N, 4], BF16, 31)
+        w2_raw = [placed(f"w2_raw{b}", [P, 4, N], F32, 19 + 4 * b) for b in range(R_PASSES)]
+        w2_bf = [kept("w2_bf0", [P, N, 4], BF16), placed("w2_bf1", [P, N, 4], BF16, 33.5)]
         w2_w = kept("w2_w", [P, R_PASSES * N], U32)
         w2_s = placed("w2_s", [P, R_PASSES * N], U8, 62)
 
@@ -73,7 +71,6 @@ def tile_list_pair_bond_logits_kernel(
         nc.vector.memset(tab_s[0:48, :].bitcast(I32), 0)
         nc.vector.memset(tab_s[64:96, :].bitcast(I32), 0)
         nc.vector.memset(w1s_raw[32:48, :].bitcast(I32), 0)
-        nc.vector.memset(late_raw[0:16, :].bitcast(I32), 0)
         for a in range(K_PASSES):
             nc.vector.memset(planes[a][:].bitcast(I32), 0)
 
@@ -92,45 +89,38 @@ def tile_list_pair_bond_logits_kernel(
 
         nc.sync.dma_start(offs_t[:], offs)
         load_scale_rows(tab_s, tab_scales.bitcast(I32))
-        load_scale_rows(w1s_raw, w1_scales.bitcast(I32)[:, :, 0 : H // 8])
+        load_scale_rows(w1s_raw, w1_scales.bitcast(I32))
         load_table(0)
         nc.sync.dma_start(out=gain_rows[0:P:16, :], in_=gain.rearrange("(b g c) -> g b c", b=R_PASSES, g=4))
-        nc.sync.dma_start(
-            out=late_raw[16:32, :].bitcast(I32).rearrange("p (a c) -> p a c", a=K_PASSES),
-            in_=w1_scales.bitcast(I32)[:, :, H // 8 : H // 4].rearrange("a q c -> q a c"),
-        )
         load_w1(0)
         load_table(1)
 
         nc.vector.tensor_copy(out=picked_s[:], in_=tab_s[:].indirect(offs_t[:]))
         for lo, hi in ((32, 64), (96, 128)):
             nc.vector.tensor_copy(
-                out=staged[lo:hi, S:].bitcast(I32).rearrange("p (t q w) -> p t q w", t=4, w=2),
-                in_=w1s_raw[lo:hi, :].bitcast(I32).rearrange("p (q t w) -> p t q w", t=4, w=2),
+                out=staged[lo:hi, S:].bitcast(I32).rearrange("p (b t q w) -> p b t q w", b=R_PASSES, t=4, w=2),
+                in_=w1s_raw[lo:hi, :].bitcast(I32).rearrange("p (b q t w) -> p b t q w", b=R_PASSES, t=4, w=2),
             )
         nc.vector.tensor_copy(out=staged[:, 0:S].bitcast(I32), in_=picked_s[:].bitcast(I32))
 
-        def move_rows(a, r):
+        def move_rows(dst, a, r, cols):
             base = (96, 112, 48)[a]
-            nc.sync.dma_start(out=planes[a][r:P:32, :].bitcast(I32), in_=staged[base + r : base + 16 : 4, :].bitcast(I32))
+            nc.sync.dma_start(
+                out=dst[a][r:P:32, :].bitcast(I32), in_=staged[base + r : base + 16 : 4, cols].bitcast(I32)
+            )
 
         moves = [(a, r) for a in range(K_PASSES) for r in range(4)]
         for a, r in moves[:5]:
-            move_rows(a, r)
+            move_rows(planes, a, r, slice(0, S + H // 2))
         load_table(2)
         for a, r in moves[5:]:
-            move_rows(a, r)
+            move_rows(planes, a, r, slice(0, S + H // 2))
 
         nc.vector.tensor_copy(
             out=gain_dealt[:].rearrange("p (t q u) -> p t q u", t=4, u=8),
             in_=gain_rows[:].rearrange("p (q t u) -> p t q u", t=4, u=8),
         )
         nc.vector.transpose(out=gain_cols[:], in_=gain_dealt[:])
-
-        nc.vector.tensor_copy(
-            out=late_staged[0:32, :].bitcast(I32).rearrange("p (a t q w) -> p t a q w", a=K_PASSES, t=4, w=2),
-            in_=late_raw[0:32, :].bitcast(I32).rearrange("p (a q t w) -> p t a q w", a=K_PASSES, t=4, w=2),
-        )
 
         def order_w1(dst, b, passes, slots):
             src = w1_raw[b][:].bitcast(I32).rearrange("p (a q t w) -> p t a q w", a=K_PASSES, t=4, w=4)
@@ -146,7 +136,7 @@ def tile_list_pair_bond_logits_kernel(
             elif a == 0:
                 tile, place = w1_first, t
             else:
-                tile, place = (w1_lead, w1_next)[t // 2], 2 * (a - 1) + t % 2
+                tile, place = (w1_lead, 2 * (a - 1) + t) if t < 2 else (w1_next[a - 1], t - 2)
             return tile[:, 256 * place : 256 * (place + 1)].bitcast(FP4X4)
 
         def gather_words(a, lo, n):
@@ -156,6 +146,7 @@ def tile_list_pair_bond_logits_kernel(
             )
 
         gather_words(0, 0, S)
+        order_w1(w1_first, 0, slice(0, 1), slice(0, 4))
         order_w1(w1_lead, 0, slice(1, 3), slice(0, 2))
         gain_wide = []
         for s in range(8):
@@ -165,24 +156,24 @@ def tile_list_pair_bond_logits_kernel(
             nc.scalar.activation(out=g[:], in_=gain_cols[:, col : col + 1].to_broadcast([P, PAIRS]), func=ACT.Copy)
             gain_wide.append(g)
         gather_words(1, 0, S)
-        order_w1(w1_first, 0, slice(0, 1), slice(0, 4))
-        nc.sync.dma_start(pos1_t[:], pos1)
         load_w1(1)
+        nc.sync.dma_start(pos1_t[:], pos1)
         nc.sync.dma_start(pos2_t[:], pos2)
-        for r in range(4):
-            nc.sync.dma_start(out=late_planes[r:P:32, :].bitcast(I32), in_=late_staged[16 + r : 32 : 4, :].bitcast(I32))
+        for a, r in moves:
+            move_rows(late_planes, a, r, slice(S + H // 2, S + H))
         w2_src = w2.rearrange("(b q t u) n -> b t q u n", b=R_PASSES, t=4, u=8)
         for b in range(R_PASSES):
             for t in range(4):
-                nc.sync.dma_start(out=w2_raw[:, b, t, :], in_=w2_src[b, t])
+                nc.sync.dma_start(out=w2_raw[b][:, t, :], in_=w2_src[b, t])
         with nc.allow_non_contiguous_dma(reason="one bias to a partition"):
             nc.sync.dma_start(out=bias_cols[:], in_=b2.rearrange("(c p) -> p c", p=P))
         gather_words(2, 0, BANK)
         gather_words(2, BANK, BANK)
-        order_w1(w1_next, 0, slice(1, 3), slice(2, 4))
+        for a in (2, 1):
+            order_w1(w1_next[a - 1], 0, slice(a, a + 1), slice(2, 4))
         order_w1(w1_late, 1, slice(0, 3), slice(0, 4))
 
-        h = [kept(f"h{s}", [P, S], F32) for s in range(8)]
+        h = [placed("h6", [P, S], F32, 19) if s == 6 else kept(f"h{s}", [P, S], F32) for s in range(8)]
         acc = {}
 
         def h_pass(s, half, a, last=K_PASSES - 1):
@@ -194,7 +185,7 @@ def tile_list_pair_bond_logits_kernel(
                 lhsT=w1_tile(s, a),
                 lhsT_scale=planes[a][:, S + s * P : S + (s + 1) * P]
                 if s < 4
-                else late_planes[:, (4 * a + s - 4) * P : (4 * a + s - 3) * P],
+                else late_planes[a][:, (s - 4) * P : (s - 3) * P],
                 rhs=v_w[a][:, cols].bitcast(FP8X4),
                 rhs_scale=planes[a][:, cols],
                 start=(a == 0),
@@ -219,6 +210,7 @@ def tile_list_pair_bond_logits_kernel(
         for half in range(2):
             for s in range(2, 4):
                 h_pass(s, half, 2, last=1)
+        for half in range(2):
             for s in range(2, 4):
                 h_pass(s, half, 1, last=1)
                 h_tanh(s, half)
@@ -233,7 +225,7 @@ def tile_list_pair_bond_logits_kernel(
                     h_tanh(s, half)
 
         def interleave_w2(b):
-            nc.scalar.activation(out=w2_bf[:, b], in_=w2_raw[:, b].rearrange("p t n -> p n t"), func=ACT.Copy)
+            nc.scalar.activation(out=w2_bf[b][:], in_=w2_raw[b][:].rearrange("p t n -> p n t"), func=ACT.Copy)
 
         wide = PIECES[2][0]
         first = [kept(f"first{s}", [P, PAIRS], F32) for s in range(8)]
@@ -260,7 +252,7 @@ def tile_list_pair_bond_logits_kernel(
 
         def quantize_w2(b):
             cols = slice(b * N, (b + 1) * N)
-            quantize(w2_w[:, cols], w2_s[:, cols], w2_bf[:, b].rearrange("p n t -> p (n t)"))
+            quantize(w2_w[:, cols], w2_s[:, cols], w2_bf[b][:].rearrange("p n t -> p (n t)"))
 
         logit_banks = {}
 
@@ -301,11 +293,12 @@ def tile_list_pair_bond_logits_kernel(
             nc.scalar.activation(out=dst, in_=src.rearrange("p t j -> p j t"), func=ACT.Copy)
 
         for s0 in range(0, 8, 2):
+            if s0 == 6:
+                interleave_w2(0)
             if s0 >= 4:
                 h_pair(s0)
             if s0 == 6:
-                for b in range(R_PASSES):
-                    interleave_w2(b)
+                interleave_w2(1)
                 interleave_on_scalar(z0_bf[:], z0[:])
             for s in (s0, s0 + 1):
                 gather_first(s)

@@ -110,10 +110,10 @@ def tile_list_pair_bond_logits_kernel(
             )
 
         moves = [(a, r) for a in range(K_PASSES) for r in range(4)]
-        for a, r in moves[:5]:
+        for a, r in moves[:4]:
             move_rows(planes, a, r, slice(0, S + H // 2))
         load_table(2)
-        for a, r in moves[5:]:
+        for a, r in moves[4:]:
             move_rows(planes, a, r, slice(0, S + H // 2))
 
         nc.vector.tensor_copy(

@@ -21,6 +21,7 @@ BANK = 512
 KIB = 1024
 K_PASSES = K // 512
 R_PASSES = H // 512
+ROW = S + H // 2
 PIECES = ((0, 256), (256, 128), (384, 128))
 
 
@@ -31,7 +32,7 @@ def tile_list_pair_bond_logits_kernel(
     with ExitStack() as ctx:
         held = ctx.enter_context(tc.tile_pool(name="held", bufs=1))
         turn = ctx.enter_context(tc.tile_pool(name="turn", bufs=1))
-        psum = ctx.enter_context(tc.psum_pool(name="psum", bufs=8))
+        psum = ctx.enter_context(tc.psum_pool(name="psum", bufs=7))
 
         def bank(name):
             return psum.tile([P, BANK], F32, name=name, tag="bank")
@@ -50,12 +51,14 @@ def tile_list_pair_bond_logits_kernel(
         tab_s = kept("tab_s", [P, T], U8)
         w1s_raw = kept("w1s_raw", [P, H], U8)
         staged = kept("staged", [P, S + H], U8)
-        planes = [kept(f"planes{a}", [P, S + H // 2], U8) for a in range(K_PASSES)]
-        late_planes = [placed(f"late_planes{a}", [P, H // 2], U8, 28 + a / 2) for a in range(K_PASSES)]
+        planes01 = kept("planes01", [P, 2 * ROW], U8)
+        plane2 = kept("plane2", [P, ROW], U8)
+        late01 = placed("late01", [P, H], U8, 28)
+        late2 = placed("late2", [P, H // 2], U8, 29)
         w1_raw = [kept("w1_raw0", [P, K_PASSES * KIB], U8), placed("w1_raw1", [P, K_PASSES * KIB], U8, 16)]
-        w1_first = kept("w1_first", [P, KIB], U8)
-        w1_lead = kept("w1_lead", [P, KIB], U8)
-        w1_next = [placed(f"w1_next{a}", [P, KIB // 2], U8, o) for a, o in ((1, 33), (2, 40))]
+        w1_ahead = kept("w1_ahead", [P, 2 * KIB], U8)
+        w1_lead = kept("w1_lead", [P, KIB // 2], U8)
+        w1_next = placed("w1_next", [P, KIB // 2], U8, 80)
         w1_late = placed("w1_late", [P, K_PASSES * KIB], U8, 34)
         v_w = [kept(f"v_w{a}", [P, S], I32) for a in range(K_PASSES)]
         gain_rows = kept("gain_rows", [P, P], F32)
@@ -71,8 +74,8 @@ def tile_list_pair_bond_logits_kernel(
         nc.vector.memset(tab_s[0:48, :].bitcast(I32), 0)
         nc.vector.memset(tab_s[64:96, :].bitcast(I32), 0)
         nc.vector.memset(w1s_raw[32:48, :].bitcast(I32), 0)
-        for a in range(K_PASSES):
-            nc.vector.memset(planes[a][:].bitcast(I32), 0)
+        nc.vector.memset(planes01[:].bitcast(I32), 0)
+        nc.vector.memset(plane2[:].bitcast(I32), 0)
 
         w1_src = w1_words.bitcast(I32).rearrange("a p (b c) -> b p a c", b=R_PASSES)
 
@@ -83,9 +86,8 @@ def tile_list_pair_bond_logits_kernel(
             nc.sync.dma_start(out=w1_raw[b][:].bitcast(I32).rearrange("p (a c) -> p a c", a=K_PASSES), in_=w1_src[b])
 
         def load_scale_rows(dst, src):
-            rows = src.rearrange("a q c -> (a q) c")
-            nc.sync.dma_start(out=dst[96:128, :].bitcast(I32), in_=rows[0:32])
-            nc.sync.dma_start(out=dst[48:64, :].bitcast(I32), in_=rows[32:48])
+            nc.sync.dma_start(out=dst[96:128, :].bitcast(I32), in_=src[0:2].rearrange("a q c -> q a c"))
+            nc.sync.dma_start(out=dst[48:64, :].bitcast(I32), in_=src[2])
 
         nc.sync.dma_start(offs_t[:], offs)
         load_scale_rows(tab_s, tab_scales.bitcast(I32))
@@ -103,18 +105,29 @@ def tile_list_pair_bond_logits_kernel(
             )
         nc.vector.tensor_copy(out=staged[:, 0:S].bitcast(I32), in_=picked_s[:].bitcast(I32))
 
-        def move_rows(dst, a, r, cols):
-            base = (96, 112, 48)[a]
-            nc.sync.dma_start(
-                out=dst[a][r:P:32, :].bitcast(I32), in_=staged[base + r : base + 16 : 4, cols].bitcast(I32)
-            )
+        def move_rows01(dst, cols):
+            for q in (0, 2, 1, 3):
+                nc.sync.dma_start(
+                    out=dst[32 * q : 32 * q + 4, :].bitcast(I32).rearrange("p (a c) -> p a c", a=2),
+                    in_=staged[96 + 8 * q : 104 + 8 * q, cols].bitcast(I32),
+                )
 
-        moves = [(a, r) for a in range(K_PASSES) for r in range(4)]
-        for a, r in moves[:4]:
-            move_rows(planes, a, r, slice(0, S + H // 2))
+        def move_rows2(dst, cols):
+            for r in range(4):
+                nc.sync.dma_start(out=dst[r:P:32, :].bitcast(I32), in_=staged[48 + r : 64 : 4, cols].bitcast(I32))
+
+        move_rows01(planes01, slice(0, ROW))
         load_table(2)
-        for a, r in moves[4:]:
-            move_rows(planes, a, r, slice(0, S + H // 2))
+        move_rows2(plane2, slice(0, ROW))
+
+        def plane(a, lo, n):
+            return planes01[:, a * ROW + lo : a * ROW + lo + n] if a < 2 else plane2[:, lo : lo + n]
+
+        def w1_plane(s, a):
+            if s < 4:
+                return plane(a, S + s * P, P)
+            lo = (s - 4) * P
+            return late01[:, a * (H // 2) + lo : a * (H // 2) + lo + P] if a < 2 else late2[:, lo : lo + P]
 
         nc.vector.tensor_copy(
             out=gain_dealt[:].rearrange("p (t q u) -> p t q u", t=4, u=8),
@@ -133,10 +146,10 @@ def tile_list_pair_bond_logits_kernel(
             b, t = divmod(s, 4)
             if b == 1:
                 tile, place = w1_late, 4 * a + t
-            elif a == 0:
-                tile, place = w1_first, t
+            elif a < 2:
+                tile, place = w1_ahead, 4 * a + t
             else:
-                tile, place = (w1_lead, 2 * (a - 1) + t) if t < 2 else (w1_next[a - 1], t - 2)
+                tile, place = (w1_lead, t) if t < 2 else (w1_next, t - 2)
             return tile[:, 256 * place : 256 * (place + 1)].bitcast(FP4X4)
 
         def gather_words(a, lo, n):
@@ -146,8 +159,9 @@ def tile_list_pair_bond_logits_kernel(
             )
 
         gather_words(0, 0, S)
-        order_w1(w1_first, 0, slice(0, 1), slice(0, 4))
-        order_w1(w1_lead, 0, slice(1, 3), slice(0, 2))
+        order_w1(w1_ahead, 0, slice(0, 2), slice(0, 4))
+        order_w1(w1_lead, 0, slice(2, 3), slice(0, 2))
+        order_w1(w1_next, 0, slice(2, 3), slice(2, 4))
         gain_wide = []
         for s in range(8):
             b, t = divmod(s, 4)
@@ -159,8 +173,8 @@ def tile_list_pair_bond_logits_kernel(
         load_w1(1)
         nc.sync.dma_start(pos1_t[:], pos1)
         nc.sync.dma_start(pos2_t[:], pos2)
-        for a, r in moves:
-            move_rows(late_planes, a, r, slice(S + H // 2, S + H))
+        move_rows01(late01, slice(ROW, S + H))
+        move_rows2(late2, slice(ROW, S + H))
         w2_src = w2.rearrange("(b q t u) n -> b t q u n", b=R_PASSES, t=4, u=8)
         for b in range(R_PASSES):
             for t in range(4):
@@ -168,55 +182,50 @@ def tile_list_pair_bond_logits_kernel(
         with nc.allow_non_contiguous_dma(reason="one bias to a partition"):
             nc.sync.dma_start(out=bias_cols[:], in_=b2.rearrange("(c p) -> p c", p=P))
         gather_words(2, 0, BANK)
-        gather_words(2, BANK, BANK)
-        for a in (2, 1):
-            order_w1(w1_next[a - 1], 0, slice(a, a + 1), slice(2, 4))
+        gather_words(2, BANK, BANK // 2)
+        gather_words(2, BANK + BANK // 2, BANK // 2)
         order_w1(w1_late, 1, slice(0, 3), slice(0, 4))
 
         h = [placed("h6", [P, S], F32, 19) if s == 6 else kept(f"h{s}", [P, S], F32) for s in range(8)]
         acc = {}
 
-        def h_pass(s, half, a, last=K_PASSES - 1):
-            if a == 0:
-                acc[s, half] = bank(f"acc{s}_{half}")
-            cols = slice(half * BANK, (half + 1) * BANK)
+        def h_pass(s, span, a, first=0, last=K_PASSES - 1):
+            lo, n = span
+            if a == first:
+                acc[s, lo] = bank(f"acc{s}_{lo}")
             nc.tensor.matmul_mx(
-                out=acc[s, half][:],
+                out=acc[s, lo][:, 0:n],
                 lhsT=w1_tile(s, a),
-                lhsT_scale=planes[a][:, S + s * P : S + (s + 1) * P]
-                if s < 4
-                else late_planes[a][:, (s - 4) * P : (s - 3) * P],
-                rhs=v_w[a][:, cols].bitcast(FP8X4),
-                rhs_scale=planes[a][:, cols],
-                start=(a == 0),
+                lhsT_scale=w1_plane(s, a),
+                rhs=v_w[a][:, lo : lo + n].bitcast(FP8X4),
+                rhs_scale=plane(a, lo, n),
+                start=(a == first),
                 stop=(a == last),
             )
 
-        def h_tanh(s, half):
-            nc.scalar.activation(out=h[s][:, half * BANK : (half + 1) * BANK], in_=acc[s, half][:], func=ACT.Tanh)
+        def h_tanh(s, span):
+            lo, n = span
+            nc.scalar.activation(out=h[s][:, lo : lo + n], in_=acc[s, lo][:, 0:n], func=ACT.Tanh)
 
-        for s in range(4):
-            for half in range(2):
-                h_pass(s, half, 0)
-        for half in range(2):
-            h_pass(0, half, 1)
-        for half in range(2):
-            h_pass(0, half, 2)
-            h_tanh(0, half)
-        for half in range(2):
-            h_pass(1, half, 2, last=1)
-            h_pass(1, half, 1, last=1)
-            h_tanh(1, half)
-        for half in range(2):
-            for s in range(2, 4):
-                h_pass(s, half, 2, last=1)
-        for half in range(2):
-            for s in range(2, 4):
-                h_pass(s, half, 1, last=1)
-                h_tanh(s, half)
+        halves = ((0, BANK), (BANK, BANK))
+        thirds = ((0, BANK), (BANK, BANK // 2), (BANK + BANK // 2, BANK // 2))
+        ahead = [(0, span) for span in thirds] + [(1, span) for span in halves] + [(s, halves[0]) for s in (2, 3)]
+        for group in (ahead[:5], ahead[5:]):
+            for a in range(2):
+                for s, span in group:
+                    h_pass(s, span, a)
+        for s, span in ahead:
+            h_pass(s, span, 2)
+            h_tanh(s, span)
+        for a in (0, 2):
+            for s in (2, 3):
+                h_pass(s, halves[1], a, last=1)
+        for s in (2, 3):
+            h_pass(s, halves[1], 1, last=1)
+            h_tanh(s, halves[1])
 
         def h_pair(s0):
-            for half in range(2):
+            for half in halves:
                 for s in (s0, s0 + 1):
                     for a in range(K_PASSES - 1):
                         h_pass(s, half, a)
@@ -229,7 +238,7 @@ def tile_list_pair_bond_logits_kernel(
 
         wide = PIECES[2][0]
         first = [kept(f"first{s}", [P, PAIRS], F32) for s in range(8)]
-        z0 = placed("z0", [P, 4, PAIRS], F32, 40)
+        z0 = placed("z0", [P, 4, PAIRS], F32, 80)
         z0_bf = placed("z0_bf", [P, PAIRS, 4], BF16, 36)
         z1_wide = kept("z1_wide", [P, 4, wide], F32)
         z1_end = placed("z1_end", [P, 4, PAIRS - wide], F32, 36)

@@ -32,7 +32,7 @@ def tile_list_pair_bond_logits_kernel(
     with ExitStack() as ctx:
         held = ctx.enter_context(tc.tile_pool(name="held", bufs=1))
         turn = ctx.enter_context(tc.tile_pool(name="turn", bufs=1))
-        psum = ctx.enter_context(tc.psum_pool(name="psum", bufs=7))
+        psum = ctx.enter_context(tc.psum_pool(name="psum", bufs=8))
 
         def bank(name):
             return psum.tile([P, BANK], F32, name=name, tag="bank")
@@ -55,7 +55,9 @@ def tile_list_pair_bond_logits_kernel(
         plane2 = kept("plane2", [P, ROW], U8)
         late01 = placed("late01", [P, H], U8, 28)
         late2 = placed("late2", [P, H // 2], U8, 29)
-        w1_raw = [kept("w1_raw0", [P, K_PASSES * KIB], U8), placed("w1_raw1", [P, K_PASSES * KIB], U8, 16)]
+        w1_raw01 = kept("w1_raw01", [P, 2 * KIB], U8)
+        w1_raw2 = kept("w1_raw2", [P, KIB], U8)
+        w1_raw_late = placed("w1_raw_late", [P, K_PASSES * KIB], U8, 16)
         w1_ahead = kept("w1_ahead", [P, 2 * KIB], U8)
         w1_lead = kept("w1_lead", [P, KIB // 2], U8)
         w1_next = placed("w1_next", [P, KIB // 2], U8, 80)
@@ -70,55 +72,58 @@ def tile_list_pair_bond_logits_kernel(
         w2_w = kept("w2_w", [P, R_PASSES * N], U32)
         w2_s = placed("w2_s", [P, R_PASSES * N], U8, 62)
 
+        nc.vector.memset(tab_s[:].bitcast(I32), 0)
+        nc.vector.memset(w1s_raw[:].bitcast(I32), 0)
         nc.vector.memset(gain_rows[:], 0.0)
-        nc.vector.memset(tab_s[0:48, :].bitcast(I32), 0)
-        nc.vector.memset(tab_s[64:96, :].bitcast(I32), 0)
-        nc.vector.memset(w1s_raw[32:48, :].bitcast(I32), 0)
         nc.vector.memset(planes01[:].bitcast(I32), 0)
         nc.vector.memset(plane2[:].bitcast(I32), 0)
 
         w1_src = w1_words.bitcast(I32).rearrange("a p (b c) -> b p a c", b=R_PASSES)
 
-        def load_table(a):
-            nc.sync.dma_start(out=tab_w[a][:], in_=tab_words[a].rearrange("p t i -> p (t i)").bitcast(I32))
+        def load_table(a, cols=slice(0, T)):
+            words = tab_words[a].rearrange("p t i -> p (t i)").bitcast(I32)
+            nc.sync.dma_start(out=tab_w[a][:, cols], in_=words[:, cols])
 
-        def load_w1(b):
-            nc.sync.dma_start(out=w1_raw[b][:].bitcast(I32).rearrange("p (a c) -> p a c", a=K_PASSES), in_=w1_src[b])
+        def load_w1(dst, b, passes):
+            nc.sync.dma_start(
+                out=dst[:].bitcast(I32).rearrange("p (a c) -> p a c", c=KIB // 4), in_=w1_src[b][:, passes, :]
+            )
 
         def load_scale_rows(dst, src):
-            nc.sync.dma_start(out=dst[96:128, :].bitcast(I32), in_=src[0:2].rearrange("a q c -> q a c"))
-            nc.sync.dma_start(out=dst[48:64, :].bitcast(I32), in_=src[2])
+            nc.sync.dma_start(out=dst[0:P:4, :].bitcast(I32), in_=src[0:2].rearrange("a q c -> q a c"))
+            nc.sync.dma_start(out=dst[5:P:8, :].bitcast(I32), in_=src[2])
 
         nc.sync.dma_start(offs_t[:], offs)
+        load_table(0, slice(0, T // 2))
         load_scale_rows(tab_s, tab_scales.bitcast(I32))
         load_scale_rows(w1s_raw, w1_scales.bitcast(I32))
-        load_table(0)
+        load_table(0, slice(T // 2, T))
         nc.sync.dma_start(out=gain_rows[0:P:16, :], in_=gain.rearrange("(b g c) -> g b c", b=R_PASSES, g=4))
-        load_w1(0)
+        load_w1(w1_raw01, 0, slice(0, 2))
         load_table(1)
 
         nc.vector.tensor_copy(out=picked_s[:], in_=tab_s[:].indirect(offs_t[:]))
-        for lo, hi in ((32, 64), (96, 128)):
-            nc.vector.tensor_copy(
-                out=staged[lo:hi, S:].bitcast(I32).rearrange("p (b t q w) -> p b t q w", b=R_PASSES, t=4, w=2),
-                in_=w1s_raw[lo:hi, :].bitcast(I32).rearrange("p (b q t w) -> p b t q w", b=R_PASSES, t=4, w=2),
-            )
+        nc.vector.tensor_copy(
+            out=staged[:, S:].bitcast(I32).rearrange("p (b t q w) -> p b t q w", b=R_PASSES, t=4, w=2),
+            in_=w1s_raw[:].bitcast(I32).rearrange("p (b q t w) -> p b t q w", b=R_PASSES, t=4, w=2),
+        )
         nc.vector.tensor_copy(out=staged[:, 0:S].bitcast(I32), in_=picked_s[:].bitcast(I32))
 
         def move_rows01(dst, cols):
             for q in (0, 2, 1, 3):
                 nc.sync.dma_start(
                     out=dst[32 * q : 32 * q + 4, :].bitcast(I32).rearrange("p (a c) -> p a c", a=2),
-                    in_=staged[96 + 8 * q : 104 + 8 * q, cols].bitcast(I32),
+                    in_=staged[32 * q : 32 * q + 32 : 4, cols].bitcast(I32),
                 )
 
         def move_rows2(dst, cols):
             for r in range(4):
-                nc.sync.dma_start(out=dst[r:P:32, :].bitcast(I32), in_=staged[48 + r : 64 : 4, cols].bitcast(I32))
+                nc.sync.dma_start(out=dst[r:P:32, :].bitcast(I32), in_=staged[8 * r + 5 : P : 32, cols].bitcast(I32))
 
         move_rows01(planes01, slice(0, ROW))
         load_table(2)
         move_rows2(plane2, slice(0, ROW))
+        load_w1(w1_raw2, 0, slice(2, 3))
 
         def plane(a, lo, n):
             return planes01[:, a * ROW + lo : a * ROW + lo + n] if a < 2 else plane2[:, lo : lo + n]
@@ -135,11 +140,11 @@ def tile_list_pair_bond_logits_kernel(
         )
         nc.vector.transpose(out=gain_cols[:], in_=gain_dealt[:])
 
-        def order_w1(dst, b, passes, slots):
-            src = w1_raw[b][:].bitcast(I32).rearrange("p (a q t w) -> p t a q w", a=K_PASSES, t=4, w=4)
-            nc.vector.tensor_copy(
-                out=dst[:].bitcast(I32).rearrange("p (a t q w) -> p t a q w", q=16, w=4, t=slots.stop - slots.start),
-                in_=src[:, slots, passes],
+        def order_w1(copy, dst, raw, slots, word):
+            src = raw[:].bitcast(word).rearrange("p (a q t w) -> p t a q w", q=16, t=4, w=4)
+            copy(
+                out=dst[:].bitcast(word).rearrange("p (a t q w) -> p t a q w", q=16, w=4, t=slots.stop - slots.start),
+                in_=src[:, slots],
             )
 
         def w1_tile(s, a):
@@ -159,9 +164,7 @@ def tile_list_pair_bond_logits_kernel(
             )
 
         gather_words(0, 0, S)
-        order_w1(w1_ahead, 0, slice(0, 2), slice(0, 4))
-        order_w1(w1_lead, 0, slice(2, 3), slice(0, 2))
-        order_w1(w1_next, 0, slice(2, 3), slice(2, 4))
+        order_w1(nc.vector.tensor_copy, w1_ahead, w1_raw01, slice(0, 4), I32)
         gain_wide = []
         for s in range(8):
             b, t = divmod(s, 4)
@@ -170,7 +173,7 @@ def tile_list_pair_bond_logits_kernel(
             nc.scalar.activation(out=g[:], in_=gain_cols[:, col : col + 1].to_broadcast([P, PAIRS]), func=ACT.Copy)
             gain_wide.append(g)
         gather_words(1, 0, S)
-        load_w1(1)
+        load_w1(w1_raw_late, 1, slice(0, 3))
         nc.sync.dma_start(pos1_t[:], pos1)
         nc.sync.dma_start(pos2_t[:], pos2)
         move_rows01(late01, slice(ROW, S + H))
@@ -184,7 +187,9 @@ def tile_list_pair_bond_logits_kernel(
         gather_words(2, 0, BANK)
         gather_words(2, BANK, BANK // 2)
         gather_words(2, BANK + BANK // 2, BANK // 2)
-        order_w1(w1_late, 1, slice(0, 3), slice(0, 4))
+        order_w1(nc.scalar.copy, w1_lead, w1_raw2, slice(0, 2), U32)
+        order_w1(nc.scalar.copy, w1_next, w1_raw2, slice(2, 4), U32)
+        order_w1(nc.vector.tensor_copy, w1_late, w1_raw_late, slice(0, 4), I32)
 
         h = [placed("h6", [P, S], F32, 19) if s == 6 else kept(f"h{s}", [P, S], F32) for s in range(8)]
         acc = {}
@@ -210,6 +215,7 @@ def tile_list_pair_bond_logits_kernel(
         halves = ((0, BANK), (BANK, BANK))
         thirds = ((0, BANK), (BANK, BANK // 2), (BANK + BANK // 2, BANK // 2))
         ahead = [(0, span) for span in thirds] + [(1, span) for span in halves] + [(s, halves[0]) for s in (2, 3)]
+        ahead.append((2, halves[1]))
         for group in (ahead[:5], ahead[5:]):
             for a in range(2):
                 for s, span in group:
@@ -217,12 +223,9 @@ def tile_list_pair_bond_logits_kernel(
         for s, span in ahead:
             h_pass(s, span, 2)
             h_tanh(s, span)
-        for a in (0, 2):
-            for s in (2, 3):
-                h_pass(s, halves[1], a, last=1)
-        for s in (2, 3):
-            h_pass(s, halves[1], 1, last=1)
-            h_tanh(s, halves[1])
+        for a in range(K_PASSES):
+            h_pass(3, halves[1], a)
+        h_tanh(3, halves[1])
 
         def h_pair(s0):
             for half in halves:

@@ -56,10 +56,10 @@ def tile_list_pair_bond_logits_kernel(
         late01 = placed("late01", [P, H], U8, 28)
         late2 = placed("late2", [P, H // 2], U8, 29)
         w1_raw01 = kept("w1_raw01", [P, 2 * KIB], U8)
-        w1_raw2 = kept("w1_raw2", [P, KIB], U8)
-        w1_raw_late = placed("w1_raw_late", [P, K_PASSES * KIB], U8, 16)
+        w1_raw2 = placed("w1_raw2", [P, KIB], U8, 81)
+        w1_raw_late = kept("w1_raw_late", [P, K_PASSES * KIB], U8)
         w1_ahead = kept("w1_ahead", [P, 2 * KIB], U8)
-        w1_lead = kept("w1_lead", [P, KIB // 2], U8)
+        w1_lead = [kept("w1_lead0", [P, KIB // 4], U8), placed("w1_lead1", [P, KIB // 4], U8, 80)]
         w1_next = placed("w1_next", [P, KIB // 2], U8, 80)
         w1_late = placed("w1_late", [P, K_PASSES * KIB], U8, 34)
         v_w = [kept(f"v_w{a}", [P, S], I32) for a in range(K_PASSES)]
@@ -154,7 +154,7 @@ def tile_list_pair_bond_logits_kernel(
             elif a < 2:
                 tile, place = w1_ahead, 4 * a + t
             else:
-                tile, place = (w1_lead, t) if t < 2 else (w1_next, t - 2)
+                tile, place = (w1_lead[t], 0) if t < 2 else (w1_next, t - 2)
             return tile[:, 256 * place : 256 * (place + 1)].bitcast(FP4X4)
 
         def gather_words(a, lo, n):
@@ -187,8 +187,8 @@ def tile_list_pair_bond_logits_kernel(
         gather_words(2, 0, BANK)
         gather_words(2, BANK, BANK // 2)
         gather_words(2, BANK + BANK // 2, BANK // 2)
-        order_w1(nc.scalar.copy, w1_lead, w1_raw2, slice(0, 2), U32)
-        order_w1(nc.scalar.copy, w1_next, w1_raw2, slice(2, 4), U32)
+        for t in range(2):
+            order_w1(nc.scalar.copy, w1_lead[t], w1_raw2, slice(t, t + 1), U32)
         order_w1(nc.vector.tensor_copy, w1_late, w1_raw_late, slice(0, 4), I32)
 
         h = [placed("h6", [P, S], F32, 19) if s == 6 else kept(f"h{s}", [P, S], F32) for s in range(8)]
@@ -220,7 +220,11 @@ def tile_list_pair_bond_logits_kernel(
             for a in range(2):
                 for s, span in group:
                     h_pass(s, span, a)
-        for s, span in ahead:
+        for s, span in ahead[:5]:
+            h_pass(s, span, 2)
+            h_tanh(s, span)
+        order_w1(nc.scalar.copy, w1_next, w1_raw2, slice(2, 4), U32)
+        for s, span in ahead[5:]:
             h_pass(s, span, 2)
             h_tanh(s, span)
         for a in range(K_PASSES):
@@ -241,7 +245,7 @@ def tile_list_pair_bond_logits_kernel(
 
         wide = PIECES[2][0]
         first = [kept(f"first{s}", [P, PAIRS], F32) for s in range(8)]
-        z0 = placed("z0", [P, 4, PAIRS], F32, 80)
+        z0 = placed("z0", [P, 4, PAIRS], F32, 81)
         z0_bf = placed("z0_bf", [P, PAIRS, 4], BF16, 36)
         z1_wide = kept("z1_wide", [P, 4, wide], F32)
         z1_end = placed("z1_end", [P, 4, PAIRS - wide], F32, 36)

@@ -47,14 +47,12 @@ def tile_list_pair_bond_logits_kernel(
         pos1_t = held.tile([P, PAIRS // 16], U16, name="pos1_t")
         pos2_t = held.tile([P, PAIRS // 16], U16, name="pos2_t")
         tab_w = [placed(f"tab_w{a}", [P, T], I32, 16 * a) for a in range(K_PASSES)]
-        picked_s = placed("picked_s", [P, S], U8, 32)
+        picked_s = kept("picked_s", [P, S], U8)
         tab_s = kept("tab_s", [P, T], U8)
         w1s_raw = kept("w1s_raw", [P, H], U8)
         staged = kept("staged", [P, S + H], U8)
-        planes01 = kept("planes01", [P, 2 * ROW], U8)
-        plane2 = kept("plane2", [P, ROW], U8)
-        late01 = placed("late01", [P, H], U8, 28)
-        late2 = placed("late2", [P, H // 2], U8, 29)
+        planes = [kept(f"planes{a}", [P, ROW], U8) for a in range(K_PASSES)]
+        late_planes = [placed(f"late_planes{a}", [P, H // 2], U8, 28 + a / 2) for a in range(K_PASSES)]
         w1_raw01 = kept("w1_raw01", [P, 2 * KIB], U8)
         w1_raw2 = placed("w1_raw2", [P, KIB], U8, 81)
         w1_raw_late = kept("w1_raw_late", [P, K_PASSES * KIB], U8)
@@ -72,11 +70,12 @@ def tile_list_pair_bond_logits_kernel(
         w2_w = kept("w2_w", [P, R_PASSES * N], U32)
         w2_s = placed("w2_s", [P, R_PASSES * N], U8, 62)
 
-        nc.vector.memset(tab_s[:].bitcast(I32), 0)
-        nc.vector.memset(w1s_raw[:].bitcast(I32), 0)
         nc.vector.memset(gain_rows[:], 0.0)
-        nc.vector.memset(planes01[:].bitcast(I32), 0)
-        nc.vector.memset(plane2[:].bitcast(I32), 0)
+        nc.vector.memset(tab_s[0:48, :].bitcast(I32), 0)
+        nc.vector.memset(tab_s[64:96, :].bitcast(I32), 0)
+        nc.vector.memset(w1s_raw[32:48, :].bitcast(I32), 0)
+        for a in range(K_PASSES):
+            nc.vector.memset(planes[a][:].bitcast(I32), 0)
 
         w1_src = w1_words.bitcast(I32).rearrange("a p (b c) -> b p a c", b=R_PASSES)
 
@@ -90,49 +89,45 @@ def tile_list_pair_bond_logits_kernel(
             )
 
         def load_scale_rows(dst, src):
-            nc.sync.dma_start(out=dst[0:P:4, :].bitcast(I32), in_=src[0:2].rearrange("a q c -> q a c"))
-            nc.sync.dma_start(out=dst[5:P:8, :].bitcast(I32), in_=src[2])
+            rows = src.rearrange("a q c -> (a q) c")
+            nc.sync.dma_start(out=dst[96:128, :].bitcast(I32), in_=rows[0:32])
+            nc.sync.dma_start(out=dst[48:64, :].bitcast(I32), in_=rows[32:48])
 
         nc.sync.dma_start(offs_t[:], offs)
-        load_table(0, slice(0, T // 2))
         load_scale_rows(tab_s, tab_scales.bitcast(I32))
         load_scale_rows(w1s_raw, w1_scales.bitcast(I32))
-        load_table(0, slice(T // 2, T))
+        load_table(0)
         nc.sync.dma_start(out=gain_rows[0:P:16, :], in_=gain.rearrange("(b g c) -> g b c", b=R_PASSES, g=4))
         load_w1(w1_raw01, 0, slice(0, 2))
         load_table(1)
 
         nc.vector.tensor_copy(out=picked_s[:], in_=tab_s[:].indirect(offs_t[:]))
-        nc.vector.tensor_copy(
-            out=staged[:, S:].bitcast(I32).rearrange("p (b t q w) -> p b t q w", b=R_PASSES, t=4, w=2),
-            in_=w1s_raw[:].bitcast(I32).rearrange("p (b q t w) -> p b t q w", b=R_PASSES, t=4, w=2),
-        )
+        for lo, hi in ((32, 64), (96, 128)):
+            nc.vector.tensor_copy(
+                out=staged[lo:hi, S:].bitcast(I32).rearrange("p (b t q w) -> p b t q w", b=R_PASSES, t=4, w=2),
+                in_=w1s_raw[lo:hi, :].bitcast(I32).rearrange("p (b q t w) -> p b t q w", b=R_PASSES, t=4, w=2),
+            )
         nc.vector.tensor_copy(out=staged[:, 0:S].bitcast(I32), in_=picked_s[:].bitcast(I32))
 
-        def move_rows01(dst, cols):
-            for q in (0, 2, 1, 3):
+        def move_rows(dst, a, cols):
+            base = (96, 112, 48)[a]
+            for r in range(4):
                 nc.sync.dma_start(
-                    out=dst[32 * q : 32 * q + 4, :].bitcast(I32).rearrange("p (a c) -> p a c", a=2),
-                    in_=staged[32 * q : 32 * q + 32 : 4, cols].bitcast(I32),
+                    out=dst[a][r:P:32, :].bitcast(I32), in_=staged[base + r : base + 16 : 4, cols].bitcast(I32)
                 )
 
-        def move_rows2(dst, cols):
-            for r in range(4):
-                nc.sync.dma_start(out=dst[r:P:32, :].bitcast(I32), in_=staged[8 * r + 5 : P : 32, cols].bitcast(I32))
-
-        move_rows01(planes01, slice(0, ROW))
-        load_table(2)
-        move_rows2(plane2, slice(0, ROW))
+        move_rows(planes, 0, slice(0, ROW))
+        load_table(2, slice(0, T // 2))
+        move_rows(planes, 1, slice(0, ROW))
+        load_table(2, slice(T // 2, T))
         load_w1(w1_raw2, 0, slice(2, 3))
+        move_rows(planes, 2, slice(0, ROW))
 
         def plane(a, lo, n):
-            return planes01[:, a * ROW + lo : a * ROW + lo + n] if a < 2 else plane2[:, lo : lo + n]
+            return planes[a][:, lo : lo + n]
 
         def w1_plane(s, a):
-            if s < 4:
-                return plane(a, S + s * P, P)
-            lo = (s - 4) * P
-            return late01[:, a * (H // 2) + lo : a * (H // 2) + lo + P] if a < 2 else late2[:, lo : lo + P]
+            return plane(a, S + s * P, P) if s < 4 else late_planes[a][:, (s - 4) * P : (s - 3) * P]
 
         nc.vector.tensor_copy(
             out=gain_dealt[:].rearrange("p (t q u) -> p t q u", t=4, u=8),
@@ -176,8 +171,8 @@ def tile_list_pair_bond_logits_kernel(
         load_w1(w1_raw_late, 1, slice(0, 3))
         nc.sync.dma_start(pos1_t[:], pos1)
         nc.sync.dma_start(pos2_t[:], pos2)
-        move_rows01(late01, slice(ROW, S + H))
-        move_rows2(late2, slice(ROW, S + H))
+        for a in range(K_PASSES):
+            move_rows(late_planes, a, slice(ROW, S + H))
         w2_src = w2.rearrange("(b q t u) n -> b t q u n", b=R_PASSES, t=4, u=8)
         for b in range(R_PASSES):
             for t in range(4):
@@ -216,10 +211,9 @@ def tile_list_pair_bond_logits_kernel(
         thirds = ((0, BANK), (BANK, BANK // 2), (BANK + BANK // 2, BANK // 2))
         ahead = [(0, span) for span in thirds] + [(1, span) for span in halves] + [(s, halves[0]) for s in (2, 3)]
         ahead.append((2, halves[1]))
-        for group in (ahead[:5], ahead[5:]):
-            for a in range(2):
-                for s, span in group:
-                    h_pass(s, span, a)
+        for a in range(2):
+            for s, span in ahead:
+                h_pass(s, span, a)
         for s, span in ahead[:5]:
             h_pass(s, span, 2)
             h_tanh(s, span)

@@ -22,6 +22,7 @@ KIB = 1024
 K_PASSES = K // 512
 R_PASSES = H // 512
 ROW = S + H // 2
+LEAD = S + 2 * P
 PIECES = ((0, 256), (256, 128), (384, 128))
 
 
@@ -51,8 +52,10 @@ def tile_list_pair_bond_logits_kernel(
         tab_s = kept("tab_s", [P, T], U8)
         w1s_raw = kept("w1s_raw", [P, H], U8)
         staged = kept("staged", [P, S + H], U8)
-        planes = [kept(f"planes{a}", [P, ROW], U8) for a in range(K_PASSES)]
-        late_planes = [placed(f"late_planes{a}", [P, H // 2], U8, 28 + a / 2) for a in range(K_PASSES)]
+        plane0 = kept("plane0", [P, ROW], U8)
+        planes12 = kept("planes12", [P, 2 * LEAD], U8)
+        late0 = placed("late0", [P, H // 2], U8, 28)
+        late12 = placed("late12", [P, 2 * (S + H - LEAD)], U8, 28.5)
         w1_raw01 = kept("w1_raw01", [P, 2 * KIB], U8)
         w1_raw2 = placed("w1_raw2", [P, KIB], U8, 81)
         w1_raw_late = kept("w1_raw_late", [P, K_PASSES * KIB], U8)
@@ -74,8 +77,8 @@ def tile_list_pair_bond_logits_kernel(
         nc.vector.memset(tab_s[0:48, :].bitcast(I32), 0)
         nc.vector.memset(tab_s[64:96, :].bitcast(I32), 0)
         nc.vector.memset(w1s_raw[32:48, :].bitcast(I32), 0)
-        for a in range(K_PASSES):
-            nc.vector.memset(planes[a][:].bitcast(I32), 0)
+        nc.vector.memset(plane0[:].bitcast(I32), 0)
+        nc.vector.memset(planes12[:].bitcast(I32), 0)
 
         w1_src = w1_words.bitcast(I32).rearrange("a p (b c) -> b p a c", b=R_PASSES)
 
@@ -89,9 +92,8 @@ def tile_list_pair_bond_logits_kernel(
             )
 
         def load_scale_rows(dst, src):
-            rows = src.rearrange("a q c -> (a q) c")
-            nc.sync.dma_start(out=dst[96:128, :].bitcast(I32), in_=rows[0:32])
-            nc.sync.dma_start(out=dst[48:64, :].bitcast(I32), in_=rows[32:48])
+            nc.sync.dma_start(out=dst[96:128, :].bitcast(I32), in_=src[1:3].rearrange("a q c -> q a c"))
+            nc.sync.dma_start(out=dst[48:64, :].bitcast(I32), in_=src[0])
 
         nc.sync.dma_start(offs_t[:], offs)
         load_scale_rows(tab_s, tab_scales.bitcast(I32))
@@ -100,6 +102,7 @@ def tile_list_pair_bond_logits_kernel(
         nc.sync.dma_start(out=gain_rows[0:P:16, :], in_=gain.rearrange("(b g c) -> g b c", b=R_PASSES, g=4))
         load_w1(w1_raw01, 0, slice(0, 2))
         load_table(1)
+        load_table(2, slice(0, T // 2))
 
         nc.vector.tensor_copy(out=picked_s[:], in_=tab_s[:].indirect(offs_t[:]))
         for lo, hi in ((32, 64), (96, 128)):
@@ -109,25 +112,32 @@ def tile_list_pair_bond_logits_kernel(
             )
         nc.vector.tensor_copy(out=staged[:, 0:S].bitcast(I32), in_=picked_s[:].bitcast(I32))
 
-        def move_rows(dst, a, cols):
-            base = (96, 112, 48)[a]
+        def move_rows0(dst, cols):
             for r in range(4):
+                nc.sync.dma_start(out=dst[r:P:32, :].bitcast(I32), in_=staged[48 + r : 64 : 4, cols].bitcast(I32))
+
+        def move_rows12(dst, cols):
+            for q in (0, 2, 1, 3):
                 nc.sync.dma_start(
-                    out=dst[a][r:P:32, :].bitcast(I32), in_=staged[base + r : base + 16 : 4, cols].bitcast(I32)
+                    out=dst[32 * q : 32 * q + 4, :].bitcast(I32).rearrange("p (a c) -> p a c", a=2),
+                    in_=staged[96 + 8 * q : 104 + 8 * q, cols].bitcast(I32),
                 )
 
-        move_rows(planes, 0, slice(0, ROW))
-        load_table(2, slice(0, T // 2))
-        move_rows(planes, 1, slice(0, ROW))
+        move_rows0(plane0, slice(0, ROW))
         load_table(2, slice(T // 2, T))
         load_w1(w1_raw2, 0, slice(2, 3))
-        move_rows(planes, 2, slice(0, ROW))
+        move_rows12(planes12, slice(0, LEAD))
 
         def plane(a, lo, n):
-            return planes[a][:, lo : lo + n]
+            return plane0[:, lo : lo + n] if a == 0 else planes12[:, (a - 1) * LEAD + lo : (a - 1) * LEAD + lo + n]
 
         def w1_plane(s, a):
-            return plane(a, S + s * P, P) if s < 4 else late_planes[a][:, (s - 4) * P : (s - 3) * P]
+            if s < (4 if a == 0 else 2):
+                return plane(a, S + s * P, P)
+            if a == 0:
+                return late0[:, (s - 4) * P : (s - 3) * P]
+            lo = (a - 1) * (S + H - LEAD) + (s - 2) * P
+            return late12[:, lo : lo + P]
 
         nc.vector.tensor_copy(
             out=gain_dealt[:].rearrange("p (t q u) -> p t q u", t=4, u=8),
@@ -171,8 +181,8 @@ def tile_list_pair_bond_logits_kernel(
         load_w1(w1_raw_late, 1, slice(0, 3))
         nc.sync.dma_start(pos1_t[:], pos1)
         nc.sync.dma_start(pos2_t[:], pos2)
-        for a in range(K_PASSES):
-            move_rows(late_planes, a, slice(ROW, S + H))
+        move_rows12(late12, slice(LEAD, S + H))
+        move_rows0(late0, slice(ROW, S + H))
         w2_src = w2.rearrange("(b q t u) n -> b t q u n", b=R_PASSES, t=4, u=8)
         for b in range(R_PASSES):
             for t in range(4):
@@ -208,22 +218,23 @@ def tile_list_pair_bond_logits_kernel(
             nc.scalar.activation(out=h[s][:, lo : lo + n], in_=acc[s, lo][:, 0:n], func=ACT.Tanh)
 
         halves = ((0, BANK), (BANK, BANK))
-        thirds = ((0, BANK), (BANK, BANK // 2), (BANK + BANK // 2, BANK // 2))
-        ahead = [(0, span) for span in thirds] + [(1, span) for span in halves] + [(s, halves[0]) for s in (2, 3)]
-        ahead.append((2, halves[1]))
-        for a in range(2):
-            for s, span in ahead:
+        quarters = [(lo, BANK // 2) for lo in range(0, S, BANK // 2)]
+        lead = [(0, span) for span in quarters] + [(1, span) for span in halves]
+        for s, span in lead + [(2, halves[0]), (3, halves[0])]:
+            h_pass(s, span, 0)
+        for s, span in lead:
+            for a in (1, 2):
                 h_pass(s, span, a)
-        for s, span in ahead[:5]:
-            h_pass(s, span, 2)
             h_tanh(s, span)
         order_w1(nc.scalar.copy, w1_next, w1_raw2, slice(2, 4), U32)
-        for s, span in ahead[5:]:
-            h_pass(s, span, 2)
-            h_tanh(s, span)
-        for a in range(K_PASSES):
-            h_pass(3, halves[1], a)
-        h_tanh(3, halves[1])
+        for s in (2, 3):
+            h_pass(s, halves[1], 0)
+        for half in halves:
+            for s in (2, 3):
+                h_pass(s, half, 1)
+            for s in (2, 3):
+                h_pass(s, half, 2)
+                h_tanh(s, half)
 
         def h_pair(s0):
             for half in halves:

@@ -21,8 +21,9 @@ BANK = 512
 KIB = 1024
 K_PASSES = K // 512
 R_PASSES = H // 512
+LEAD = 2 * P
+OWN = LEAD + S
 ROW = S + H // 2
-LEAD = S + 2 * P
 PIECES = ((0, 256), (256, 128), (384, 128))
 
 
@@ -51,11 +52,12 @@ def tile_list_pair_bond_logits_kernel(
         picked_s = kept("picked_s", [P, S], U8)
         tab_s = kept("tab_s", [P, T], U8)
         w1s_raw = kept("w1s_raw", [P, H], U8)
-        staged = kept("staged", [P, S + H], U8)
+        w1s_ord = kept("w1s_ord", [P, H], U8)
+        staged = kept("staged", [P, 2 * (S + H)], U8)
         plane0 = kept("plane0", [P, ROW], U8)
-        planes12 = kept("planes12", [P, 2 * LEAD], U8)
+        planes12 = kept("planes12", [P, 2 * OWN], U8)
         late0 = placed("late0", [P, H // 2], U8, 28)
-        late12 = placed("late12", [P, 2 * (S + H - LEAD)], U8, 28.5)
+        late12 = placed("late12", [P, 2 * (H - LEAD)], U8, 28.5)
         w1_raw01 = kept("w1_raw01", [P, 2 * KIB], U8)
         w1_raw2 = placed("w1_raw2", [P, KIB], U8, 81)
         w1_raw_late = kept("w1_raw_late", [P, K_PASSES * KIB], U8)
@@ -73,10 +75,9 @@ def tile_list_pair_bond_logits_kernel(
         w2_w = kept("w2_w", [P, R_PASSES * N], U32)
         w2_s = placed("w2_s", [P, R_PASSES * N], U8, 62)
 
+        nc.vector.memset(tab_s[:].bitcast(I32), 0)
+        nc.vector.memset(w1s_raw[:].bitcast(I32), 0)
         nc.vector.memset(gain_rows[:], 0.0)
-        nc.vector.memset(tab_s[0:48, :].bitcast(I32), 0)
-        nc.vector.memset(tab_s[64:96, :].bitcast(I32), 0)
-        nc.vector.memset(w1s_raw[32:48, :].bitcast(I32), 0)
         nc.vector.memset(plane0[:].bitcast(I32), 0)
         nc.vector.memset(planes12[:].bitcast(I32), 0)
 
@@ -92,51 +93,62 @@ def tile_list_pair_bond_logits_kernel(
             )
 
         def load_scale_rows(dst, src):
-            nc.sync.dma_start(out=dst[96:128, :].bitcast(I32), in_=src[1:3].rearrange("a q c -> q a c"))
-            nc.sync.dma_start(out=dst[48:64, :].bitcast(I32), in_=src[0])
+            nc.sync.dma_start(out=dst[32:96:2, :].bitcast(I32), in_=src[1:3].rearrange("a q c -> (a q) c"))
+            nc.sync.dma_start(out=dst[33:96:4, :].bitcast(I32), in_=src[0])
 
+        load_table(0, slice(0, T // 2))
         nc.sync.dma_start(offs_t[:], offs)
         load_scale_rows(tab_s, tab_scales.bitcast(I32))
         load_scale_rows(w1s_raw, w1_scales.bitcast(I32))
-        load_table(0)
+        load_table(0, slice(T // 2, T))
         nc.sync.dma_start(out=gain_rows[0:P:16, :], in_=gain.rearrange("(b g c) -> g b c", b=R_PASSES, g=4))
         load_w1(w1_raw01, 0, slice(0, 2))
         load_table(1)
         load_table(2, slice(0, T // 2))
 
         nc.vector.tensor_copy(out=picked_s[:], in_=tab_s[:].indirect(offs_t[:]))
-        for lo, hi in ((32, 64), (96, 128)):
-            nc.vector.tensor_copy(
-                out=staged[lo:hi, S:].bitcast(I32).rearrange("p (b t q w) -> p b t q w", b=R_PASSES, t=4, w=2),
-                in_=w1s_raw[lo:hi, :].bitcast(I32).rearrange("p (b q t w) -> p b t q w", b=R_PASSES, t=4, w=2),
-            )
-        nc.vector.tensor_copy(out=staged[:, 0:S].bitcast(I32), in_=picked_s[:].bitcast(I32))
+        nc.vector.tensor_copy(
+            out=w1s_ord[:].bitcast(I32).rearrange("p (b t q w) -> p b t q w", b=R_PASSES, t=4, w=2),
+            in_=w1s_raw[:].bitcast(I32).rearrange("p (b q t w) -> p b t q w", b=R_PASSES, t=4, w=2),
+        )
 
-        def move_rows0(dst, cols):
+        def stage(rows, lo, src):
+            nc.vector.tensor_copy(out=staged[rows, lo : lo + src.shape[1]].bitcast(I32), in_=src.bitcast(I32))
+
+        stage(slice(0, P), OWN, picked_s[:])
+        stage(slice(0, P), OWN + S, w1s_ord[:])
+        stage(slice(32, 64), LEAD, picked_s[64:96, :])
+        stage(slice(32, 64), 0, w1s_ord[64:96, 0:LEAD])
+        stage(slice(32, 64), OWN + S + H, w1s_ord[64:96, LEAD:H])
+
+        def move_rows0(dst, lo):
             for r in range(4):
-                nc.sync.dma_start(out=dst[r:P:32, :].bitcast(I32), in_=staged[48 + r : 64 : 4, cols].bitcast(I32))
+                src = staged[33 + 4 * r : 96 : 16, lo : lo + dst.shape[1]]
+                nc.sync.dma_start(out=dst[r:P:32, :].bitcast(I32), in_=src.bitcast(I32))
 
-        def move_rows12(dst, cols):
-            for q in (0, 2, 1, 3):
-                nc.sync.dma_start(
-                    out=dst[32 * q : 32 * q + 4, :].bitcast(I32).rearrange("p (a c) -> p a c", a=2),
-                    in_=staged[96 + 8 * q : 104 + 8 * q, cols].bitcast(I32),
-                )
+        def move_rows12(dst, lo):
+            for r in range(4):
+                src = staged[32 + 2 * r : 64 : 8, lo : lo + dst.shape[1]]
+                nc.sync.dma_start(out=dst[r:P:32, :].bitcast(I32), in_=src.bitcast(I32))
 
-        move_rows0(plane0, slice(0, ROW))
+        move_rows0(plane0, OWN)
         load_table(2, slice(T // 2, T))
         load_w1(w1_raw2, 0, slice(2, 3))
-        move_rows12(planes12, slice(0, LEAD))
+        move_rows12(planes12, 0)
 
         def plane(a, lo, n):
-            return plane0[:, lo : lo + n] if a == 0 else planes12[:, (a - 1) * LEAD + lo : (a - 1) * LEAD + lo + n]
+            if a == 0:
+                return plane0[:, lo : lo + n]
+            lo = lo + (OWN if a == 1 else LEAD)
+            return planes12[:, lo : lo + n]
 
         def w1_plane(s, a):
-            if s < (4 if a == 0 else 2):
-                return plane(a, S + s * P, P)
             if a == 0:
-                return late0[:, (s - 4) * P : (s - 3) * P]
-            lo = (a - 1) * (S + H - LEAD) + (s - 2) * P
+                return plane0[:, S + s * P : S + (s + 1) * P] if s < 4 else late0[:, (s - 4) * P : (s - 3) * P]
+            if s < 2:
+                lo = (OWN + S if a == 1 else 0) + s * P
+                return planes12[:, lo : lo + P]
+            lo = (a - 1) * (H - LEAD) + (s - 2) * P
             return late12[:, lo : lo + P]
 
         nc.vector.tensor_copy(
@@ -181,8 +193,8 @@ def tile_list_pair_bond_logits_kernel(
         load_w1(w1_raw_late, 1, slice(0, 3))
         nc.sync.dma_start(pos1_t[:], pos1)
         nc.sync.dma_start(pos2_t[:], pos2)
-        move_rows12(late12, slice(LEAD, S + H))
-        move_rows0(late0, slice(ROW, S + H))
+        move_rows12(late12, OWN + S + LEAD)
+        move_rows0(late0, OWN + ROW)
         w2_src = w2.rearrange("(b q t u) n -> b t q u n", b=R_PASSES, t=4, u=8)
         for b in range(R_PASSES):
             for t in range(4):

@@ -49,23 +49,23 @@ def tile_list_pair_bond_logits_kernel(
         pos1_t = held.tile([P, PAIRS // 16], U16, name="pos1_t")
         pos2_t = held.tile([P, PAIRS // 16], U16, name="pos2_t")
         tab_w = [placed(f"tab_w{a}", [P, T], I32, 16 * a) for a in range(K_PASSES)]
-        picked_s = kept("picked_s", [P, S], U8)
+        picked_s = placed("picked_s", [P, S], U8, 64)
         tab_s = kept("tab_s", [P, T], U8)
         w1s_raw = kept("w1s_raw", [P, H], U8)
         w1s_ord = kept("w1s_ord", [P, H], U8)
-        staged = kept("staged", [P, 2 * (S + H)], U8)
+        staged = kept("staged", [P, 2 * (S + H) + H // 2], U8)
         plane0 = kept("plane0", [P, ROW], U8)
         planes12 = kept("planes12", [P, 2 * OWN], U8)
-        late0 = placed("late0", [P, H // 2], U8, 28)
-        late12 = placed("late12", [P, 2 * (H - LEAD)], U8, 28.5)
-        w1_raw01 = kept("w1_raw01", [P, 2 * KIB], U8)
-        w1_raw2 = placed("w1_raw2", [P, KIB], U8, 81)
+        late = placed("late", [P, 2 * H], U8, 28)
+        w1_raw0 = kept("w1_raw0", [P, KIB], U8)
+        w1_raw12 = placed("w1_raw12", [P, 2 * KIB], U8, 81)
         w1_raw_late = kept("w1_raw_late", [P, K_PASSES * KIB], U8)
-        w1_ahead = kept("w1_ahead", [P, 2 * KIB], U8)
-        w1_lead = [kept("w1_lead0", [P, KIB // 4], U8), placed("w1_lead1", [P, KIB // 4], U8, 80)]
+        w1_ahead = kept("w1_ahead", [P, KIB], U8)
+        w1_mid = kept("w1_mid", [P, KIB // 2], U8)
+        w1_lead = [kept("w1_lead0", [P, KIB // 2], U8), placed("w1_lead1", [P, KIB // 2], U8, 80)]
         w1_next = placed("w1_next", [P, KIB // 2], U8, 80)
         w1_late = placed("w1_late", [P, K_PASSES * KIB], U8, 34)
-        v_w = [kept(f"v_w{a}", [P, S], I32) for a in range(K_PASSES)]
+        v_w = [placed("v_w0", [P, S], I32, 64)] + [kept(f"v_w{a}", [P, S], I32) for a in (1, 2)]
         gain_rows = kept("gain_rows", [P, P], F32)
         gain_dealt = kept("gain_dealt", [P, P], F32)
         gain_cols = kept("gain_cols", [P, P], F32)
@@ -93,16 +93,14 @@ def tile_list_pair_bond_logits_kernel(
             )
 
         def load_scale_rows(dst, src):
-            nc.sync.dma_start(out=dst[32:96:2, :].bitcast(I32), in_=src[1:3].rearrange("a q c -> (a q) c"))
-            nc.sync.dma_start(out=dst[33:96:4, :].bitcast(I32), in_=src[0])
+            nc.sync.dma_start(out=dst[32:P:2, :].bitcast(I32), in_=src.rearrange("a q c -> (a q) c"))
 
-        load_table(0, slice(0, T // 2))
+        load_table(0)
         nc.sync.dma_start(offs_t[:], offs)
         load_scale_rows(tab_s, tab_scales.bitcast(I32))
         load_scale_rows(w1s_raw, w1_scales.bitcast(I32))
-        load_table(0, slice(T // 2, T))
         nc.sync.dma_start(out=gain_rows[0:P:16, :], in_=gain.rearrange("(b g c) -> g b c", b=R_PASSES, g=4))
-        load_w1(w1_raw01, 0, slice(0, 2))
+        load_w1(w1_raw0, 0, slice(0, 1))
         load_table(1)
         load_table(2, slice(0, T // 2))
 
@@ -117,24 +115,20 @@ def tile_list_pair_bond_logits_kernel(
 
         stage(slice(0, P), OWN, picked_s[:])
         stage(slice(0, P), OWN + S, w1s_ord[:])
-        stage(slice(32, 64), LEAD, picked_s[64:96, :])
-        stage(slice(32, 64), 0, w1s_ord[64:96, 0:LEAD])
-        stage(slice(32, 64), OWN + S + H, w1s_ord[64:96, LEAD:H])
+        stage(slice(64, 96), LEAD, picked_s[96:P, :])
+        stage(slice(64, 96), 0, w1s_ord[96:P, 0:LEAD])
+        stage(slice(64, 96), OWN + S + H, w1s_ord[96:P, LEAD:H])
+        stage(slice(64, 96), 2 * (S + H), w1s_ord[32:64, H // 2 : H])
 
-        def move_rows0(dst, lo):
+        def move_rows(dst, first, lo):
             for r in range(4):
-                src = staged[33 + 4 * r : 96 : 16, lo : lo + dst.shape[1]]
+                src = staged[first + 2 * r : first + 32 : 8, lo : lo + dst.shape[1]]
                 nc.sync.dma_start(out=dst[r:P:32, :].bitcast(I32), in_=src.bitcast(I32))
 
-        def move_rows12(dst, lo):
-            for r in range(4):
-                src = staged[32 + 2 * r : 64 : 8, lo : lo + dst.shape[1]]
-                nc.sync.dma_start(out=dst[r:P:32, :].bitcast(I32), in_=src.bitcast(I32))
-
-        move_rows0(plane0, OWN)
+        move_rows(plane0, 32, OWN)
         load_table(2, slice(T // 2, T))
-        load_w1(w1_raw2, 0, slice(2, 3))
-        move_rows12(planes12, 0)
+        load_w1(w1_raw12, 0, slice(1, 3))
+        move_rows(planes12, 64, 0)
 
         def plane(a, lo, n):
             if a == 0:
@@ -144,12 +138,12 @@ def tile_list_pair_bond_logits_kernel(
 
         def w1_plane(s, a):
             if a == 0:
-                return plane0[:, S + s * P : S + (s + 1) * P] if s < 4 else late0[:, (s - 4) * P : (s - 3) * P]
+                return plane0[:, S + s * P : S + (s + 1) * P] if s < 4 else late[:, H + s * P : H + (s + 1) * P]
             if s < 2:
                 lo = (OWN + S if a == 1 else 0) + s * P
                 return planes12[:, lo : lo + P]
             lo = (a - 1) * (H - LEAD) + (s - 2) * P
-            return late12[:, lo : lo + P]
+            return late[:, lo : lo + P]
 
         nc.vector.tensor_copy(
             out=gain_dealt[:].rearrange("p (t q u) -> p t q u", t=4, u=8),
@@ -158,7 +152,7 @@ def tile_list_pair_bond_logits_kernel(
         nc.vector.transpose(out=gain_cols[:], in_=gain_dealt[:])
 
         def order_w1(copy, dst, raw, slots, word):
-            src = raw[:].bitcast(word).rearrange("p (a q t w) -> p t a q w", q=16, t=4, w=4)
+            src = raw.bitcast(word).rearrange("p (a q t w) -> p t a q w", q=16, t=4, w=4)
             copy(
                 out=dst[:].bitcast(word).rearrange("p (a t q w) -> p t a q w", q=16, w=4, t=slots.stop - slots.start),
                 in_=src[:, slots],
@@ -168,10 +162,12 @@ def tile_list_pair_bond_logits_kernel(
             b, t = divmod(s, 4)
             if b == 1:
                 tile, place = w1_late, 4 * a + t
-            elif a < 2:
-                tile, place = w1_ahead, 4 * a + t
+            elif a == 0:
+                tile, place = w1_ahead, t
+            elif t < 2:
+                tile, place = w1_lead[t], a - 1
             else:
-                tile, place = (w1_lead[t], 0) if t < 2 else (w1_next, t - 2)
+                tile, place = (w1_mid if a == 1 else w1_next), t - 2
             return tile[:, 256 * place : 256 * (place + 1)].bitcast(FP4X4)
 
         def gather_words(a, lo, n):
@@ -181,7 +177,7 @@ def tile_list_pair_bond_logits_kernel(
             )
 
         gather_words(0, 0, S)
-        order_w1(nc.vector.tensor_copy, w1_ahead, w1_raw01, slice(0, 4), I32)
+        order_w1(nc.vector.tensor_copy, w1_ahead, w1_raw0[:], slice(0, 4), I32)
         gain_wide = []
         for s in range(8):
             b, t = divmod(s, 4)
@@ -193,8 +189,7 @@ def tile_list_pair_bond_logits_kernel(
         load_w1(w1_raw_late, 1, slice(0, 3))
         nc.sync.dma_start(pos1_t[:], pos1)
         nc.sync.dma_start(pos2_t[:], pos2)
-        move_rows12(late12, OWN + S + LEAD)
-        move_rows0(late0, OWN + ROW)
+        move_rows(late, 64, OWN + S + LEAD)
         w2_src = w2.rearrange("(b q t u) n -> b t q u n", b=R_PASSES, t=4, u=8)
         for b in range(R_PASSES):
             for t in range(4):
@@ -205,8 +200,9 @@ def tile_list_pair_bond_logits_kernel(
         gather_words(2, BANK, BANK // 2)
         gather_words(2, BANK + BANK // 2, BANK // 2)
         for t in range(2):
-            order_w1(nc.scalar.copy, w1_lead[t], w1_raw2, slice(t, t + 1), U32)
-        order_w1(nc.vector.tensor_copy, w1_late, w1_raw_late, slice(0, 4), I32)
+            order_w1(nc.scalar.copy, w1_lead[t], w1_raw12[:], slice(t, t + 1), U32)
+        order_w1(nc.vector.tensor_copy, w1_mid, w1_raw12[:, 0:KIB], slice(2, 4), I32)
+        order_w1(nc.vector.tensor_copy, w1_late, w1_raw_late[:], slice(0, 4), I32)
 
         h = [placed("h6", [P, S], F32, 19) if s == 6 else kept(f"h{s}", [P, S], F32) for s in range(8)]
         acc = {}
@@ -238,7 +234,7 @@ def tile_list_pair_bond_logits_kernel(
             for a in (1, 2):
                 h_pass(s, span, a)
             h_tanh(s, span)
-        order_w1(nc.scalar.copy, w1_next, w1_raw2, slice(2, 4), U32)
+        order_w1(nc.scalar.copy, w1_next, w1_raw12[:, KIB:], slice(2, 4), U32)
         for s in (2, 3):
             h_pass(s, halves[1], 0)
         for half in halves:

@@ -24,6 +24,7 @@ R_PASSES = H // 512
 LEAD = 2 * P
 OWN = LEAD + S
 ROW = S + H // 2
+CUT = 9 * T // 16
 PIECES = ((0, 256), (256, 128), (384, 128))
 
 
@@ -97,12 +98,12 @@ def tile_list_pair_bond_logits_kernel(
 
         load_table(0)
         nc.sync.dma_start(offs_t[:], offs)
+        nc.sync.dma_start(out=gain_rows[0:P:16, :], in_=gain.rearrange("(b g c) -> g b c", b=R_PASSES, g=4))
         load_scale_rows(tab_s, tab_scales.bitcast(I32))
         load_scale_rows(w1s_raw, w1_scales.bitcast(I32))
-        nc.sync.dma_start(out=gain_rows[0:P:16, :], in_=gain.rearrange("(b g c) -> g b c", b=R_PASSES, g=4))
         load_w1(w1_raw0, 0, slice(0, 1))
         load_table(1)
-        load_table(2, slice(0, T // 2))
+        load_table(2, slice(0, CUT))
 
         nc.vector.tensor_copy(out=picked_s[:], in_=tab_s[:].indirect(offs_t[:]))
         nc.vector.tensor_copy(
@@ -126,7 +127,7 @@ def tile_list_pair_bond_logits_kernel(
                 nc.sync.dma_start(out=dst[r:P:32, :].bitcast(I32), in_=src.bitcast(I32))
 
         move_rows(plane0, 32, OWN)
-        load_table(2, slice(T // 2, T))
+        load_table(2, slice(CUT, T))
         load_w1(w1_raw12, 0, slice(1, 3))
         move_rows(planes12, 64, 0)
 

@@ -313,8 +313,7 @@ def tile_list_pair_bond_logits_kernel(
                     nc.scalar.activation(out=res[:], in_=o[:, 0:n], func=ACT.Identity, bias=bias)
                 else:
                     nc.vector.tensor_scalar(res[:], o[:, 0:n], bias, None, ALU.add)
-                queue = nc.scalar if (i, c) == (2, 0) else nc.sync
-                queue.dma_start(out=out[c * P : (c + 1) * P, lo : lo + n], in_=res[:])
+                nc.sync.dma_start(out=out[c * P : (c + 1) * P, lo : lo + n], in_=res[:])
 
         def quantize_piece(i):
             quantize(z1_w[i][:], z1_s[i][:], z1_bf[i][:].rearrange("p j t -> p (j t)"))

from contextlib import ExitStack

import concourse.mybir as mybir

T, S, PAIRS, K, H, N = 4096, 1024, 512, 1536, 1024, 256
FLOPS = 2 * K * H * S + 2 * H * N * PAIRS

F32 = mybir.dt.float32
BF16 = mybir.dt.bfloat16
I32 = mybir.dt.int32
U32 = mybir.dt.uint32
U16 = mybir.dt.uint16
U8 = mybir.dt.uint8
FP8X4 = mybir.dt.float8_e4m3fn_x4
FP4X4 = mybir.dt.float4_e2m1fn_x4
ACT = mybir.ActivationFunctionType
ALU = mybir.AluOpType

P = 128
BANK = 512
KIB = 1024
K_PASSES = K // 512
R_PASSES = H // 512
LEAD = 2 * P
OWN = LEAD + S
ROW = S + H // 2
CUT = 9 * T // 16
PIECES = ((0, 256), (256, 128), (384, 128))


def tile_list_pair_bond_logits_kernel(
    tc, tab_words, tab_scales, offs, w1_words, w1_scales, pos1, pos2, gain, w2, b2, out
):
    nc = tc.nc
    with ExitStack() as ctx:
        held = ctx.enter_context(tc.tile_pool(name="held", bufs=1))
        turn = ctx.enter_context(tc.tile_pool(name="turn", bufs=1))
        psum = ctx.enter_context(tc.psum_pool(name="psum", bufs=8))

        def bank(name):
            return psum.tile([P, BANK], F32, name=name, tag="bank")

        def placed(name, shape, dtype, kib):
            return turn.tile(shape, dtype, name=name, offset=int(kib * KIB), align_bytes=64)

        def kept(name, shape, dtype):
            return held.tile(shape, dtype, name=name, align_bytes=64)

        offs_t = held.tile([P, S // 16], U16, name="offs_t")
        pos1_t = held.tile([P, PAIRS // 16], U16, name="pos1_t")
        pos2_t = held.tile([P, PAIRS // 16], U16, name="pos2_t")
        tab_w = [placed(f"tab_w{a}", [P, T], I32, 16 * a) for a in range(K_PASSES)]
        picked_s = placed("picked_s", [P, S], U8, 64)
        tab_s = kept("tab_s", [P, T], U8)
        w1s_raw = kept("w1s_raw", [P, H], U8)
        w1s_ord = kept("w1s_ord", [P, H], U8)
        staged = kept("staged", [P, 2 * (S + H) + H // 2], U8)
        plane0 = kept("plane0", [P, ROW], U8)
        planes12 = kept("planes12", [P, 2 * OWN], U8)
        late = placed("late", [P, 2 * H], U8, 28)
        w1_raw0 = kept("w1_raw0", [P, KIB], U8)
        w1_raw12 = placed("w1_raw12", [P, 2 * KIB], U8, 81)
        w1_raw_late = kept("w1_raw_late", [P, K_PASSES * KIB], U8)
        w1_ahead = kept("w1_ahead", [P, KIB], U8)
        w1_mid = kept("w1_mid", [P, KIB // 2], U8)
        w1_lead = [kept("w1_lead0", [P, KIB // 2], U8), placed("w1_lead1", [P, KIB // 2], U8, 80)]
        w1_next = placed("w1_next", [P, KIB // 2], U8, 80)
        w1_late = placed("w1_late", [P, K_PASSES * KIB], U8, 34)
        v_w = [placed("v_w0", [P, S], I32, 64)] + [kept(f"v_w{a}", [P, S], I32) for a in (1, 2)]
        gain_rows = kept("gain_rows", [P, P], F32)
        gain_dealt = kept("gain_dealt", [P, P], F32)
        gain_cols = kept("gain_cols", [P, P], F32)
        bias_cols = placed("bias_cols", [P, N // P], F32, 27)
        w2_raw = [placed(f"w2_raw{b}", [P, 4, N], F32, 19 + 4 * b) for b in range(R_PASSES)]
        w2_bf = [kept("w2_bf0", [P, N, 4], BF16), placed("w2_bf1", [P, N, 4], BF16, 33.5)]
        w2_w = kept("w2_w", [P, R_PASSES * N], U32)
        w2_s = placed("w2_s", [P, R_PASSES * N], U8, 62)

        nc.vector.memset(tab_s[:].bitcast(I32), 0)
        nc.vector.memset(w1s_raw[:].bitcast(I32), 0)
        nc.vector.memset(gain_rows[:], 0.0)
        nc.vector.memset(plane0[:].bitcast(I32), 0)
        nc.vector.memset(planes12[:].bitcast(I32), 0)

        w1_src = w1_words.bitcast(I32).rearrange("a p (b c) -> b p a c", b=R_PASSES)

        def load_table(a, cols=slice(0, T)):
            words = tab_words[a].rearrange("p t i -> p (t i)").bitcast(I32)
            nc.sync.dma_start(out=tab_w[a][:, cols], in_=words[:, cols])

        def load_w1(dst, b, passes):
            nc.sync.dma_start(
                out=dst[:].bitcast(I32).rearrange("p (a c) -> p a c", c=KIB // 4), in_=w1_src[b][:, passes, :]
            )

        def load_scale_rows(dst, src):
            nc.sync.dma_start(out=dst[32:P:2, :].bitcast(I32), in_=src.rearrange("a q c -> (a q) c"))

        load_table(0)
        nc.sync.dma_start(offs_t[:], offs)
        nc.sync.dma_start(out=gain_rows[0:P:16, :], in_=gain.rearrange("(b g c) -> g b c", b=R_PASSES, g=4))
        load_scale_rows(tab_s, tab_scales.bitcast(I32))
        load_scale_rows(w1s_raw, w1_scales.bitcast(I32))
        load_w1(w1_raw0, 0, slice(0, 1))
        load_table(1)
        load_table(2, slice(0, CUT))

        nc.vector.tensor_copy(out=picked_s[:], in_=tab_s[:].indirect(offs_t[:]))
        nc.vector.tensor_copy(
            out=w1s_ord[:].bitcast(I32).rearrange("p (b t q w) -> p b t q w", b=R_PASSES, t=4, w=2),
            in_=w1s_raw[:].bitcast(I32).rearrange("p (b q t w) -> p b t q w", b=R_PASSES, t=4, w=2),
        )

        def stage(rows, lo, src):
            nc.vector.tensor_copy(out=staged[rows, lo : lo + src.shape[1]].bitcast(I32), in_=src.bitcast(I32))

        stage(slice(0, P), OWN, picked_s[:])
        stage(slice(0, P), OWN + S, w1s_ord[:])
        stage(slice(64, 96), LEAD, picked_s[96:P, :])
        stage(slice(64, 96), 0, w1s_ord[96:P, 0:LEAD])
        stage(slice(64, 96), OWN + S + H, w1s_ord[96:P, LEAD:H])
        stage(slice(64, 96), 2 * (S + H), w1s_ord[32:64, H // 2 : H])

        def move_rows(dst, first, lo):
            for r in range(4):
                src = staged[first + 2 * r : first + 32 : 8, lo : lo + dst.shape[1]]
                nc.sync.dma_start(out=dst[r:P:32, :].bitcast(I32), in_=src.bitcast(I32))

        move_rows(plane0, 32, OWN)
        load_table(2, slice(CUT, T))
        load_w1(w1_raw12, 0, slice(1, 3))
        move_rows(planes12, 64, 0)

        def plane(a, lo, n):
            if a == 0:
                return plane0[:, lo : lo + n]
            lo = lo + (OWN if a == 1 else LEAD)
            return planes12[:, lo : lo + n]

        def w1_plane(s, a):
            if a == 0:
                return plane0[:, S + s * P : S + (s + 1) * P] if s < 4 else late[:, H + s * P : H + (s + 1) * P]
            if s < 2:
                lo = (OWN + S if a == 1 else 0) + s * P
                return planes12[:, lo : lo + P]
            lo = (a - 1) * (H - LEAD) + (s - 2) * P
            return late[:, lo : lo + P]

        nc.vector.tensor_copy(
            out=gain_dealt[:].rearrange("p (t q u) -> p t q u", t=4, u=8),
            in_=gain_rows[:].rearrange("p (q t u) -> p t q u", t=4, u=8),
        )
        nc.vector.transpose(out=gain_cols[:], in_=gain_dealt[:])

        def order_w1(copy, dst, raw, slots, word):
            src = raw.bitcast(word).rearrange("p (a q t w) -> p t a q w", q=16, t=4, w=4)
            copy(
                out=dst[:].bitcast(word).rearrange("p (a t q w) -> p t a q w", q=16, w=4, t=slots.stop - slots.start),
                in_=src[:, slots],
            )

        def w1_tile(s, a):
            b, t = divmod(s, 4)
            if b == 1:
                tile, place = w1_late, 4 * a + t
            elif a == 0:
                tile, place = w1_ahead, t
            elif t < 2:
                tile, place = w1_lead[t], a - 1
            else:
                tile, place = (w1_mid if a == 1 else w1_next), t - 2
            return tile[:, 256 * place : 256 * (place + 1)].bitcast(FP4X4)

        def gather_words(a, lo, n):
            nc.vector.tensor_copy(
                out=v_w[a][:, lo : lo + n].bitcast(U32),
                in_=tab_w[a][:].bitcast(U32).indirect(offs_t[:, lo // 16 : (lo + n) // 16]),
            )

        gather_words(0, 0, S)
        order_w1(nc.vector.tensor_copy, w1_ahead, w1_raw0[:], slice(0, 4), I32)
        gain_wide = []
        for s in range(8):
            b, t = divmod(s, 4)
            g = placed(f"gain_wide{s}", [P, PAIRS], F32, 48 + 2 * s)
            col = 32 * t + 16 * b
            nc.scalar.activation(out=g[:], in_=gain_cols[:, col : col + 1].to_broadcast([P, PAIRS]), func=ACT.Copy)
            gain_wide.append(g)
        gather_words(1, 0, S)
        load_w1(w1_raw_late, 1, slice(0, 3))
        nc.sync.dma_start(pos1_t[:], pos1)
        nc.sync.dma_start(pos2_t[:], pos2)
        move_rows(late, 64, OWN + S + LEAD)
        w2_src = w2.rearrange("(b q t u) n -> b t q u n", b=R_PASSES, t=4, u=8)
        for b in range(R_PASSES):
            for t in range(4):
                nc.sync.dma_start(out=w2_raw[b][:, t, :], in_=w2_src[b, t])
        with nc.allow_non_contiguous_dma(reason="one bias to a partition"):
            nc.sync.dma_start(out=bias_cols[:], in_=b2.rearrange("(c p) -> p c", p=P))
        gather_words(2, 0, BANK)
        gather_words(2, BANK, BANK // 2)
        gather_words(2, BANK + BANK // 2, BANK // 2)
        for t in range(2):
            order_w1(nc.scalar.copy, w1_lead[t], w1_raw12[:], slice(t, t + 1), U32)
        order_w1(nc.vector.tensor_copy, w1_mid, w1_raw12[:, 0:KIB], slice(2, 4), I32)
        order_w1(nc.vector.tensor_copy, w1_late, w1_raw_late[:], slice(0, 4), I32)

        h = [placed("h6", [P, S], F32, 19) if s == 6 else kept(f"h{s}", [P, S], F32) for s in range(8)]
        acc = {}

        def h_pass(s, span, a, first=0, last=K_PASSES - 1):
            lo, n = span
            if a == first:
                acc[s, lo] = bank(f"acc{s}_{lo}")
            nc.tensor.matmul_mx(
                out=acc[s, lo][:, 0:n],
                lhsT=w1_tile(s, a),
                lhsT_scale=w1_plane(s, a),
                rhs=v_w[a][:, lo : lo + n].bitcast(FP8X4),
                rhs_scale=plane(a, lo, n),
                start=(a == first),
                stop=(a == last),
            )

        def h_tanh(s, span):
            lo, n = span
            nc.scalar.activation(out=h[s][:, lo : lo + n], in_=acc[s, lo][:, 0:n], func=ACT.Tanh)

        halves = ((0, BANK), (BANK, BANK))
        quarters = [(lo, BANK // 2) for lo in range(0, S, BANK // 2)]
        lead = [(0, span) for span in quarters] + [(1, span) for span in halves]
        for s, span in lead + [(2, halves[0]), (3, halves[0])]:
            h_pass(s, span, 0)
        for s, span in lead:
            for a in (1, 2):
                h_pass(s, span, a)
            h_tanh(s, span)
        order_w1(nc.scalar.copy, w1_next, w1_raw12[:, KIB:], slice(2, 4), U32)
        for s in (2, 3):
            h_pass(s, halves[1], 0)
        for half in halves:
            for s in (2, 3):
                h_pass(s, half, 1)
            for s in (2, 3):
                h_pass(s, half, 2)
                h_tanh(s, half)

        def h_pair(s0):
            for half in halves:
                for s in (s0, s0 + 1):
                    for a in range(K_PASSES - 1):
                        h_pass(s, half, a)
                for s in (s0, s0 + 1):
                    h_pass(s, half, K_PASSES - 1)
                    h_tanh(s, half)

        def interleave_w2(b):
            nc.scalar.activation(out=w2_bf[b][:], in_=w2_raw[b][:].rearrange("p t n -> p n t"), func=ACT.Copy)

        wide = PIECES[2][0]
        first = [kept(f"first{s}", [P, PAIRS], F32) for s in range(8)]
        z0 = placed("z0", [P, 4, PAIRS], F32, 81)
        z0_bf = placed("z0_bf", [P, PAIRS, 4], BF16, 36)
        z1_wide = kept("z1_wide", [P, 4, wide], F32)
        z1_end = placed("z1_end", [P, 4, PAIRS - wide], F32, 36)
        z1_bf = [placed(f"z1_bf{lo}", [P, n, 4], BF16, o) for (lo, n), o in zip(PIECES, (68, 70, 71))]
        z0_w = kept("z0_w", [P, PAIRS], U32)
        z0_s = placed("z0_s", [P, PAIRS], U8, 63)
        z1_w = [kept(f"z1_w{lo}", [P, n], U32) for lo, n in PIECES]
        z1_s = [kept(f"z1_s{lo}", [P, n], U8) for lo, n in PIECES]

        def gather_first(s):
            nc.vector.tensor_tensor(first[s][:], h[s][:].indirect(pos1_t[:]), gain_wide[s][:], ALU.mult)

        def gather_second(s, dst, lo, n):
            nc.vector.tensor_tensor(
                dst, h[s][:].indirect(pos2_t[:, lo // 16 : (lo + n) // 16]), first[s][:, lo : lo + n], ALU.mult
            )

        def quantize(codes, scales, src):
            nc.vector.quantize_mx(out=codes.bitcast(FP8X4), scales=scales, in_=src)

        def quantize_w2(b):
            cols = slice(b * N, (b + 1) * N)
            quantize(w2_w[:, cols], w2_s[:, cols], w2_bf[b][:].rearrange("p n t -> p (n t)"))

        logit_banks = {}

        def logit_pass(i, c, b):
            lo, n = PIECES[i]
            if b == 0:
                logit_banks[i, c] = bank(f"o{i}_{c}")
            zw, zs = (z0_w[:, lo : lo + n], z0_s[:, lo : lo + n]) if b == 0 else (z1_w[i][:], z1_s[i][:])
            cols = slice(b * N + c * P, b * N + (c + 1) * P)
            nc.tensor.matmul_mx(
                out=logit_banks[i, c][:, 0:n],
                lhsT=w2_w[:, cols].bitcast(FP8X4),
                lhsT_scale=w2_s[:, cols],
                rhs=zw.bitcast(FP8X4),
                rhs_scale=zs,
                start=(b == 0),
                stop=(b == R_PASSES - 1),
            )

        def logits(i, evac_engines):
            lo, n = PIECES[i]
            for c in range(N // P):
                res = placed(f"res{i}_{c}", [P, n], F32, 71 if (i, c) == (1, 1) else 72 + 2 * i + c)
                logit_pass(i, c, 1)
                o = logit_banks[i, c]
                bias = bias_cols[:, c : c + 1]
                if evac_engines[c] == "scalar":
                    nc.scalar.activation(out=res[:], in_=o[:, 0:n], func=ACT.Identity, bias=bias)
                else:
                    nc.vector.tensor_scalar(res[:], o[:, 0:n], bias, None, ALU.add)
                nc.sync.dma_start(out=out[c * P : (c + 1) * P, lo : lo + n], in_=res[:])

        def quantize_piece(i):
            quantize(z1_w[i][:], z1_s[i][:], z1_bf[i][:].rearrange("p j t -> p (j t)"))

        def interleave_on_scalar(dst, src):
            nc.scalar.activation(out=dst, in_=src.rearrange("p t j -> p j t"), func=ACT.Copy)

        for s0 in range(0, 8, 2):
            if s0 == 6:
                interleave_w2(0)
            if s0 >= 4:
                h_pair(s0)
            if s0 == 6:
                interleave_w2(1)
                interleave_on_scalar(z0_bf[:], z0[:])
            for s in (s0, s0 + 1):
                gather_first(s)
            if s0 == 6:
                quantize_w2(0)
            for s in (s0, s0 + 1):
                if s < 4:
                    gather_second(s, z0[:, s, :], 0, PAIRS)
                else:
                    gather_second(s, z1_wide[:, s - 4, :], 0, wide)
        for i in range(2):
            lo, n = PIECES[i]
            interleave_on_scalar(z1_bf[i][:], z1_wide[:, :, lo : lo + n])
        quantize(z0_w[:], z0_s[:], z0_bf[:].rearrange("p j t -> p (j t)"))
        quantize_w2(1)
        for i in range(len(PIECES)):
            for c in range(N // P):
                logit_pass(i, c, 0)
        for t in range(3):
            gather_second(4 + t, z1_end[:, t, :], wide, PAIRS - wide)
        quantize_piece(0)
        gather_second(7, z1_end[:, 3, :], wide, PAIRS - wide)
        quantize_piece(1)
        for half in range(2):
            cols = slice(64 * half, 64 * (half + 1))
            nc.vector.tensor_copy(out=z1_bf[2][:, cols, :], in_=z1_end[:, :, cols].rearrange("p t j -> p j t"))
        for half in range(2):
            cols = slice(64 * half, 64 * (half + 1))
            nc.vector.quantize_mx(
                out=z1_w[2][:, cols].bitcast(FP8X4),
                scales=z1_s[2][:, cols],
                in_=z1_bf[2][:, cols, :].rearrange("p j t -> p (j t)"),
            )
        logits(0, ("scalar", "scalar"))
        logits(1, ("scalar", "vector"))
        logits(2, ("scalar", "vector"))
